import numpy as np
import ml_dtypes


def mxq(x, axis, fmt="e4m3"):
    dtype, down = {"e4m3": (ml_dtypes.float8_e4m3fn, 7), "e5m2": (ml_dtypes.float8_e5m2, 14)}[fmt]
    v = np.moveaxis(np.asarray(x, np.float32).astype(ml_dtypes.bfloat16).astype(np.float64), axis, -1)
    blocks = v.reshape(v.shape[:-1] + (-1, 32))
    amax = np.abs(blocks).max(-1, keepdims=True)
    byte = np.maximum(np.where(amax > 0, np.frexp(amax)[1] - 1 + 127, 0) - down, 1)
    scale = np.exp2(byte - 127.0)
    codes = (blocks / scale).astype(np.float32).astype(dtype).astype(np.float64)
    return np.moveaxis((codes * scale).reshape(v.shape), -1, axis)


WIDE = False


def mx_kscale(k):
    if not WIDE:
        return np.ones(k)
    levels = np.array([10, -10, 5, -5, 0])
    if k % 512:
        return np.exp2(np.random.permutation(np.resize(levels, k // 32))).repeat(32)
    a = np.empty((k // 512, 16))
    for p in range(k // 512):
        a[p, :8] = np.random.permutation(np.resize(levels, 8))
        for g in range(8):
            far = levels[np.abs(levels - a[p, g]) >= 10]
            a[p, g + 8] = far[np.random.randint(len(far))]
    return np.exp2(a.ravel()).repeat(32)


def f64(x):
    return np.asarray(x).astype(np.float64)


def striped(idx):
    return np.tile(idx.reshape(-1, 16).T, (8, 1)).astype(np.uint16)


def unstriped(offs):
    return offs[:16].T.reshape(-1).astype(np.int64)


E2M1 = np.array([0.0, 0.5, 1.0, 1.5, 2.0, 3.0, 4.0, 6.0, -0.0, -0.5, -1.0, -1.5, -2.0, -3.0, -4.0, -6.0])


def pack_weight(w, fmt):
    k, n = w.shape
    w = f64(np.asarray(w, np.float32).astype(ml_dtypes.bfloat16)).reshape(k // 32, 32, n)
    amax = np.abs(w).max(1)
    if fmt == "e4m3":
        byte = np.frexp(amax)[1] - 1 + 127 - 7
    else:
        mant, ex = np.frexp(amax / 6.0)
        byte = np.where(mant > 0.5, ex, ex - 1) + 127
    byte = np.clip(np.where(amax > 0, byte, 1), 1, 254)
    scaled = (w * np.exp2(127.0 - byte)[:, None, :]).reshape(k, n).astype(np.float32)
    by_word = np.ascontiguousarray(scaled.reshape(k // 512, 128, 4, n).transpose(0, 1, 3, 2))
    if fmt == "e4m3":
        words = by_word.astype(ml_dtypes.float8_e4m3fn).view(np.uint8)
    else:
        c = by_word.astype(ml_dtypes.float4_e2m1fn).view(np.uint8) & 0xF
        words = (c[..., 0::2] | (c[..., 1::2] << 4)).reshape(k // 512, 128, 2 * n)
    return np.ascontiguousarray(words), np.ascontiguousarray(byte.astype(np.uint8).reshape(k // 512, 16, n))


def unpack_weight(words, scales, fmt):
    g, _, n = scales.shape
    words = np.ascontiguousarray(words).reshape(g, 128, n, -1)
    if fmt == "e4m3":
        vals = words.view(ml_dtypes.float8_e4m3fn).astype(np.float64)
    else:
        nib = np.empty((g, 128, n, 4), np.uint8)
        nib[..., 0::2] = words & 0xF
        nib[..., 1::2] = words >> 4
        vals = E2M1[nib]
    vals = vals * np.repeat(np.exp2(scales.astype(np.float64) - 127.0), 8, axis=1)[..., None]
    return vals.transpose(0, 1, 3, 2).reshape(g * 512, n)


def gelu(v):
    return 0.5 * v * (1.0 + np.tanh(np.sqrt(2.0 / np.pi) * (v + 0.044715 * v**3)))


K, T, S, H, T2, P, N = 512, 2048, 1024, 1024, 2048, 1024, 512

def setup_inputs():
    n = np.random.standard_normal
    s = mx_kscale(K)[:, None]
    u = mx_kscale(H)[:, None]
    tab_words, tab_scales = pack_weight(n((K, T)) * s, "e4m3")
    wg_words, wg_scales = pack_weight(n((K, H)) / np.sqrt(K) / s, "e2m1")
    wh_words, wh_scales = pack_weight(n((K, H)) / np.sqrt(K) / s * u.T, "e4m3")
    perm = np.random.permutation(T2)
    return {
        "tab_words": tab_words, "tab_scales": tab_scales,
        "offs": striped(np.random.permutation(T)[:S]),
        "offs2": striped(np.random.permutation(T2)[:S]),
        "offs3": striped(perm[:P]),
        "offs4": striped(perm[P // 2:P // 2 + P]),
        "wg_words": wg_words, "wg_scales": wg_scales,
        "wl": (n((K, H)) / np.sqrt(K) / s * u.T).astype(np.float32),
        "wh_words": wh_words, "wh_scales": wh_scales,
        "wgs": np.exp(0.3 * n((128, S))).astype(np.float32),
        "page0": (n((H, T2)) * u).astype(np.float32),
        "wd": (n((H, N)) / np.sqrt(H) / u).astype(np.float32),
    }

def reference(tab_words, tab_scales, offs, offs2, offs3, offs4, wg_words, wg_scales,
              wl, wh_words, wh_scales, wgs, page0, wd):
    v = unpack_weight(tab_words, tab_scales, "e4m3")[:, unstriped(offs)]
    gate = unpack_weight(wg_words, wg_scales, "e2m1").T @ v
    low = mxq(f64(wl), 0, "e4m3").T @ v
    high = unpack_weight(wh_words, wh_scales, "e4m3").T @ v
    h = low + (high - low) / (1.0 + np.exp(-gate))
    page = f64(page0).copy()
    page[:, unstriped(offs2)] = np.tile(f64(wgs), (H // 128, 1)) * h
    x1 = page[:, unstriped(offs3)]
    x2 = page[:, unstriped(offs4)]
    z = np.abs(x1 - x2)
    return mxq(f64(wd), 0, "e4m3").T @ mxq(z, 0, "e4m3")

@@ -1,0 +1,359 @@
+from contextlib import ExitStack
+
+import concourse.mybir as mybir
+from concourse.masks import make_identity
+
+K, T, S, H, T2, M_OUT, N = 512, 2048, 1024, 1024, 2048, 1024, 512
+FLOPS = 2 * (3 * K * H * S + H * N * M_OUT)
+
+F32 = mybir.dt.float32
+BF16 = mybir.dt.bfloat16
+I32 = mybir.dt.int32
+U32 = mybir.dt.uint32
+U16 = mybir.dt.uint16
+U8 = mybir.dt.uint8
+FP8X4 = mybir.dt.float8_e4m3fn_x4
+FP4X4 = mybir.dt.float4_e2m1fn_x4
+ACT = mybir.ActivationFunctionType
+ALU = mybir.AluOpType
+
+P = 128
+PACK = 4
+PASS = P * PACK
+BANK = 512
+QUADS = 4
+PASSES = H // PASS
+TILES = H // P
+HALVES = S // BANK
+CHUNK = 256
+CHUNKS = ((0, 256), (256, 256), (512, 256), (768, 128), (896, 128))
+PAGE_BUFS = 6
+WH_ROW = 4
+
+
+def tile_list_limb_cut_advice_kernel(
+    tc, tab_words, tab_scales, offs, offs2, offs3, offs4, wg_words, wg_scales,
+    wl, wh_words, wh_scales, wgs, page0, wd, out,
+):
+    nc = tc.nc
+    with ExitStack() as ctx:
+        keep = ctx.enter_context(tc.tile_pool(name="keep", bufs=1))
+        ring = ctx.enter_context(tc.tile_pool(name="ring", bufs=2))
+        psum = ctx.enter_context(tc.psum_pool(name="psum", bufs=1))
+
+        def held(shape, dtype, name):
+            return keep.tile(shape, dtype, name=name, align_bytes=64)
+
+        banks = [psum.tile([P, BANK], F32, name="bank%d" % i) for i in range(8)]
+        low_bank, high_bank, diff_bank, h_bank = banks[0:2], banks[2:4], banks[4:6], banks[6:8]
+
+        lists = {}
+        for name in ("offs", "offs2", "offs3", "offs4"):
+            lists[name] = held([P, S // 16], U16, name)
+
+        def offsets(name, start, count):
+            return lists[name][:, start // 16 : (start + count) // 16]
+
+        tab_w = held([P, T], U32, "tab_w")
+        tab_s = held([P, T], U8, "tab_s")
+        w_s = held([P, H], U8, "w_s")
+        wh_w = [held([P, PASS], U32, "wh_w%d" % b) for b in range(PASSES)]
+        wg_w = [held([P, 2 * PASS], U8, "wg_w%d" % b) for b in range(PASSES)]
+        ident = held([P, P], F32, "ident")
+        warm = held([P, 16], F32, "warm")
+
+        nc.gpsimd.memset(w_s[:].bitcast(I32), 0)
+        nc.gpsimd.memset(warm[:, 0:8], 0.0)
+        nc.scalar.activation(warm[:, 8:16], warm[:, 0:8], ACT.Sigmoid)
+
+        def load_scale_rows(plane, rows, first, queue):
+            for q in range(QUADS):
+                p0 = 32 * q + first
+                queue.dma_start(out=plane[p0 : p0 + 4, :].bitcast(I32), in_=rows[0, 4 * q : 4 * q + 4, :].bitcast(I32))
+
+        def load_f32_rows(src):
+            raw = ring.tile([P, PACK, BANK], F32, name="raw")
+            nc.sync.dma_start(out=raw[:], in_=src.rearrange("(p j) c -> p j c", j=PACK))
+            return raw
+
+        page_rows = page0.rearrange("(b p t) c -> b t p c", p=P, t=PACK)
+        pages = {}
+
+        def load_page(i):
+            pages[i] = ring.tile([P, T2], F32, name="page", bufs=PAGE_BUFS)
+            nc.sync.dma_start(out=pages[i][:], in_=page_rows[i // PACK, i % PACK])
+
+        wgs_rows = wgs.rearrange("(s t) j -> t s j", t=PACK)
+        wgs_t = [held([P, S], F32, "wgs%d" % t) for t in range(PACK)]
+
+        def load_wgs(t):
+            for q in range(QUADS):
+                nc.sync.dma_start(out=wgs_t[t][32 * q : 32 * q + 32, :], in_=wgs_rows[t])
+
+        wh_rows = wh_words[0].rearrange("p c i -> p (c i)").bitcast(I32)
+        wg_rows = wg_words[0].bitcast(I32)
+
+        def load_packed_weights(b):
+            nc.sync.dma_start(out=wh_w[b][:].bitcast(I32), in_=wh_rows[:, b * PASS : (b + 1) * PASS])
+            nc.sync.dma_start(out=wg_w[b][:].bitcast(I32), in_=wg_rows[:, b * PASS // 2 : (b + 1) * PASS // 2])
+
+        nc.sync.dma_start(lists["offs"][:], offs)
+        for q in range(QUADS):
+            rows = tab_scales[0, 4 * q : 4 * q + 4, :].bitcast(I32)
+            nc.sync.dma_start(out=tab_s[32 * q : 32 * q + 32, :].bitcast(I32), in_=rows.partition_broadcast(8))
+        nc.sync.dma_start(out=tab_w[:].bitcast(I32), in_=tab_words[0].rearrange("p t i -> p (t i)").bitcast(I32))
+        wl_raw = [load_f32_rows(wl[:, 0:PASS])]
+        load_packed_weights(0)
+        load_scale_rows(w_s, wh_scales, WH_ROW, nc.sync)
+        load_scale_rows(w_s, wg_scales, 0, nc.gpsimd)
+        make_identity(nc, ident[:])
+        load_page(0)
+        nc.sync.dma_start(lists["offs2"][:], offs2)
+        load_wgs(0)
+        nc.sync.dma_start(lists["offs4"][:], offs4)
+        nc.sync.dma_start(lists["offs3"][:], offs3)
+        load_wgs(1)
+        load_page(1)
+        wl_raw.append(load_f32_rows(wl[:, PASS : 2 * PASS]))
+        load_packed_weights(1)
+        for i in (2, 3):
+            load_wgs(i)
+            load_page(i)
+
+        v_w = [held([P, BANK], U32, "v_w%d" % a) for a in range(HALVES)]
+        v_s = [held([P, BANK], U8, "v_s%d" % a) for a in range(HALVES)]
+        for a in range(HALVES):
+            nc.vector.tensor_copy(v_s[a][:], tab_s[:].indirect(offsets("offs", a * BANK, BANK)))
+        for a in range(HALVES):
+            nc.vector.tensor_copy(v_w[a][:], tab_w[:].indirect(offsets("offs", a * BANK, BANK)))
+
+        wl_w = [held([P, PASS], U32, "wl_w%d" % b) for b in range(PASSES)]
+        wl_s = [held([P, PASS], U8, "wl_s%d" % b) for b in range(PASSES)]
+        wh_p = [held([P, PASS], U32, "wh_p%d" % b) for b in range(PASSES)]
+        wg_p = [held([P, 2 * PASS], U8, "wg_p%d" % b) for b in range(PASSES)]
+        ws_p = [held([P, PASS], U8, "ws_p%d" % b) for b in range(PASSES)]
+        wd_w = [held([P, N], U32, "wd_w%d" % b) for b in range(PASSES)]
+        wd_s = [held([P, N], U8, "wd_s%d" % b) for b in range(PASSES)]
+
+        def order_packed_weights(b):
+            for dst, src in (
+                (wh_p[b][:], wh_w[b][:]),
+                (ws_p[b][:], w_s[:, b * PASS : (b + 1) * PASS]),
+                (wg_p[b][:].bitcast(U16), wg_w[b][:].bitcast(U16)),
+            ):
+                nc.vector.tensor_copy(
+                    dst.rearrange("p (t m) -> p m t", t=PACK), src.rearrange("p (m t) -> p m t", t=PACK)
+                )
+
+        def quantise_wl(b, t0, count, copy):
+            grouped = ring.tile([P, count * PASS], BF16, name="grouped", align_bytes=64)
+            copy(
+                grouped[:].rearrange("p (t m j) -> p m j t", t=count, j=PACK),
+                wl_raw[b][:].rearrange("p j (m t) -> p m j t", t=PACK)[:, :, :, t0 : t0 + count],
+            )
+            cols = slice(t0 * P, (t0 + count) * P)
+            nc.vector.quantize_mx(out=wl_w[b][:, cols].bitcast(FP8X4), scales=wl_s[b][:, cols], in_=grouped[:])
+
+        def quantise_wd(b):
+            raw = load_f32_rows(wd[b * PASS : (b + 1) * PASS, :])
+            grouped = ring.tile([P, N * PACK], BF16, name="grouped", align_bytes=64)
+            for n0 in range(0, N, CHUNK):
+                nc.scalar.copy(
+                    grouped[:, n0 * PACK : (n0 + CHUNK) * PACK].rearrange("p (n t) -> p n t", t=PACK),
+                    raw[:, :, n0 : n0 + CHUNK].rearrange("p t n -> p n t"),
+                )
+            nc.vector.quantize_mx(out=wd_w[b][:].bitcast(FP8X4), scales=wd_s[b][:], in_=grouped[:])
+
+        high_sb = [held([P, BANK], F32, "high_sb%d" % a) for a in range(HALVES)]
+        nlow_sb = [held([P, BANK], F32, "nlow_sb%d" % a) for a in range(HALVES)]
+        step_t = [held([P, BANK], F32, "step_t%d" % a) for a in range(HALVES)]
+        low_t = [[held([P, BANK], F32, "low_t%d_%d" % (s, a)) for a in range(HALVES)] for s in range(2)]
+        shared = [[held([P, BANK], F32, "shared%d_%d" % (s, a)) for a in range(HALVES)] for s in range(2)]
+        h_sb = [held([P, S], F32, "h_sb%d" % s) for s in range(2)]
+        early = [held([P, PACK, M_OUT], F32, "early0"), held([P, 2, M_OUT], F32, "early1")]
+        tail = {m0: held([P, 2, w], F32, "tail%d" % m0) for m0, w in CHUNKS}
+        z_w = [{m0: held([P, w], U32, "z_w%d_%d" % (b, m0)) for m0, w in CHUNKS} for b in range(PASSES)]
+        z_s = [{m0: held([P, w], U8, "z_s%d_%d" % (b, m0)) for m0, w in CHUNKS} for b in range(PASSES)]
+
+        def blocks():
+            return [slice(x, x + P) for x in range(0, BANK, P)]
+
+        def add_transposed(bank, first, second):
+            for blk in blocks():
+                nc.tensor.matmul(bank[:, blk], first[:, blk], ident[:], start=True, stop=False, is_transpose=True)
+                nc.tensor.matmul(bank[:, blk], second[:, blk], ident[:], start=False, stop=True, is_transpose=True)
+
+        def high_and_low(i):
+            b, t = divmod(i, PACK)
+            cols = slice(t * P, (t + 1) * P)
+            for a in range(HALVES):
+                nc.tensor.matmul_mx(
+                    high_bank[a][:], lhsT=wh_p[b][:, cols].bitcast(FP8X4), lhsT_scale=ws_p[b][WH_ROW:P, cols],
+                    rhs=v_w[a][:].bitcast(FP8X4), rhs_scale=v_s[a][:], start=True, stop=True,
+                )
+                nc.tensor.matmul_mx(
+                    low_bank[a][:], lhsT=wl_w[b][:, cols].bitcast(FP8X4), lhsT_scale=wl_s[b][:, cols],
+                    rhs=v_w[a][:].bitcast(FP8X4), rhs_scale=v_s[a][:], start=True, stop=True,
+                )
+
+        def first_tile():
+            high_and_low(0)
+            for a in range(HALVES):
+                nc.tensor.matmul_mx(
+                    diff_bank[a][:], lhsT=wg_p[0][:, 0 : 2 * P].bitcast(FP4X4), lhsT_scale=ws_p[0][:, 0:P],
+                    rhs=v_w[a][:].bitcast(FP8X4), rhs_scale=v_s[a][:], start=True, stop=True,
+                )
+            for a in range(HALVES):
+                nc.scalar.copy(low_t[0][a][:], low_bank[a][:])
+            for a in range(HALVES):
+                nc.scalar.activation(shared[0][a][:], diff_bank[a][:], ACT.Sigmoid)
+            for a in range(HALVES):
+                nc.vector.tensor_tensor(step_t[a][:], high_bank[a][:], low_t[0][a][:], ALU.subtract)
+            for a in range(HALVES):
+                nc.vector.tensor_tensor(step_t[a][:], step_t[a][:], shared[0][a][:], ALU.mult)
+            for a in range(HALVES):
+                nc.vector.tensor_tensor(h_sb[0][:, a * BANK : (a + 1) * BANK], step_t[a][:], low_t[0][a][:], ALU.add)
+
+        def products(i):
+            b, t = divmod(i, PACK)
+            cols = slice(t * P, (t + 1) * P)
+            high_and_low(i)
+            for a in range(HALVES):
+                nc.scalar.copy(high_sb[a][:], high_bank[a][:])
+                nc.scalar.activation(nlow_sb[a][:], low_bank[a][:], ACT.Copy, scale=-1.0)
+            for a in range(HALVES):
+                for blk in blocks():
+                    nc.tensor.matmul_mx(
+                        high_bank[a][:, blk], lhsT=v_w[a][:, blk].bitcast(FP8X4), lhsT_scale=v_s[a][:, blk],
+                        rhs=wg_p[b][:, 2 * t * P : 2 * (t + 1) * P].bitcast(FP4X4), rhs_scale=ws_p[b][:, cols],
+                        start=True, stop=True,
+                    )
+            for a in range(HALVES):
+                add_transposed(diff_bank[a], high_sb[a], nlow_sb[a])
+            for a in range(HALVES):
+                for blk in blocks():
+                    nc.tensor.transpose(low_bank[a][:, blk], nlow_sb[a][:, blk], ident[:])
+            for a in range(HALVES):
+                nc.scalar.activation(shared[i % 2][a][:], high_bank[a][:], ACT.Sigmoid)
+            for a in range(HALVES):
+                nc.scalar.activation(low_t[i % 2][a][:], low_bank[a][:], ACT.Copy, scale=-1.0)
+
+        def interpolate(i):
+            for a in range(HALVES):
+                nc.vector.tensor_tensor(step_t[a][:], diff_bank[a][:], shared[i % 2][a][:], ALU.mult)
+            for a in range(HALVES):
+                add_transposed(h_bank[a], low_t[i % 2][a], step_t[a])
+                nc.scalar.copy(h_sb[i % 2][:, a * BANK : (a + 1) * BANK], h_bank[a][:])
+
+        def scatter(i, width):
+            for j0 in range(0, S, width):
+                cols = slice(j0, j0 + width)
+                nc.vector.tensor_tensor(
+                    pages[i][:].indirect(offsets("offs2", j0, width)),
+                    h_sb[i % 2][:, cols], wgs_t[i % PACK][:, cols], ALU.mult,
+                )
+
+        def fetch_bearers(i, m0, into):
+            nc.vector.tensor_copy(into, pages[i][:].indirect(offsets("offs4", m0, into.shape[1])))
+
+        def fetch_limbs(i, m0, bearers, into):
+            nc.vector.tensor_tensor(into, pages[i][:].indirect(offsets("offs3", m0, into.shape[1])), bearers, ALU.subtract)
+
+        def round_z(source, grouped, slots):
+            nc.scalar.activation(
+                grouped.rearrange("p (m t) -> p m t", t=PACK)[:, :, slots], source.rearrange("p t m -> p m t"), ACT.Abs
+            )
+
+        def quantise_z(b, m0, grouped):
+            nc.vector.quantize_mx(out=z_w[b][m0][:].bitcast(FP8X4), scales=z_s[b][m0][:], in_=grouped)
+
+        def score_pass(b, m0, width):
+            per_bank = BANK // width
+            for nb in range(N // P):
+                part, side = divmod(nb, per_bank)
+                cols = slice(nb * P, (nb + 1) * P)
+                nc.tensor.matmul_mx(
+                    banks[m0 // P + part][:, side * width : (side + 1) * width],
+                    lhsT=wd_w[b][:, cols].bitcast(FP8X4), lhsT_scale=wd_s[b][:, cols],
+                    rhs=z_w[b][m0][:].bitcast(FP8X4), rhs_scale=z_s[b][m0][:],
+                    start=(b == 0 and side == 0), stop=(b == PASSES - 1 and side == per_bank - 1),
+                )
+
+        def store(m0, width):
+            per_bank = BANK // width
+            out_rows = out.rearrange("(a s p) m -> a p s m", s=per_bank, p=P)
+            for part in range(width // P):
+                staged = ring.tile([P, BANK], F32, name="staged", bufs=4)
+                if m0 + width == M_OUT or (m0 == 512 and part == 1):
+                    nc.vector.tensor_copy(staged[:], banks[m0 // P + part][:])
+                else:
+                    nc.scalar.copy(staged[:], banks[m0 // P + part][:])
+                nc.sync.dma_start(
+                    out=out_rows[part][:, :, m0 : m0 + width],
+                    in_=staged[:].rearrange("p (s m) -> p s m", s=per_bank),
+                )
+
+        quantise_wl(0, 0, 1, nc.scalar.copy)
+        order_packed_weights(0)
+        quantise_wl(0, 1, 1, nc.vector.tensor_copy)
+        quantise_wl(0, 2, 2, nc.vector.tensor_copy)
+        first_tile()
+        last = TILES - 1
+        jobs = [(i, a * BANK) for i in range(last - 1) for a in range(HALVES)]
+        done = 0
+        for i in range(last):
+            products(i + 1)
+            scatter(i, S if i != 1 and i != 2 else BANK)
+            interpolate(i + 1)
+            now = jobs[done : done + (1 if i < 2 else 2)]
+            done = done + len(now)
+            free = shared[(i + 1) % 2][HALVES - len(now) :]
+            for (tile_i, m0), buf in zip(now, free):
+                fetch_bearers(tile_i, m0, buf[:])
+            for (tile_i, m0), buf in zip(now, free):
+                fetch_limbs(tile_i, m0, buf[:], early[tile_i // PACK][:, tile_i % PACK, m0 : m0 + BANK])
+            if i == 0:
+                load_page(4)
+                load_page(5)
+            if i == 1:
+                order_packed_weights(1)
+                quantise_wl(1, 0, PACK, nc.scalar.copy)
+            if i in (2, 3):
+                quantise_wd(i - 2)
+                load_page(i + 4)
+        spent = high_sb + nlow_sb
+        for m0, width in CHUNKS:
+            x = (m0 % CHUNK) * PACK
+            grouped = spent[m0 // CHUNK][:].bitcast(BF16)[:, x : x + width * PACK]
+            round_z(early[0][:, :, m0 : m0 + width], grouped, slice(0, PACK))
+            quantise_z(0, m0, grouped)
+        scatter(last, S)
+        late = {m0: held([P, w * PACK], BF16, "late%d" % m0) for m0, w in CHUNKS}
+        for m0, width in CHUNKS:
+            score_pass(0, m0, width)
+            round_z(early[1][:, :, m0 : m0 + width], late[m0][:], slice(0, 2))
+
+        def finish(m0, width):
+            round_z(tail[m0][:], late[m0][:], slice(2, PACK))
+            quantise_z(1, m0, late[m0][:])
+            score_pass(1, m0, width)
+
+        bearers = {}
+        for c, (m0, width) in enumerate(CHUNKS):
+            if c >= 2:
+                finish(*CHUNKS[c - 2])
+            if m0 % CHUNK == 0:
+                for s, i in enumerate((last - 1, last)):
+                    source = shared[0][s][:] if c < 2 else late[m0 - 2 * CHUNK][:].bitcast(F32)
+                    x = (m0 if c < 2 else s * CHUNK)
+                    bearers[i] = source[:, x : x + CHUNK]
+                    fetch_bearers(i, m0, bearers[i])
+            for s, i in enumerate((last - 1, last)):
+                x = m0 % CHUNK
+                fetch_limbs(i, m0, bearers[i][:, x : x + width], tail[m0][:, s, :])
+            if c >= 2:
+                store(*CHUNKS[c - 2])
+        for m0, width in CHUNKS[-2:]:
+            finish(m0, width)
+        for m0, width in CHUNKS[-2:]:
+            store(m0, width)

@@ -166,7 +166,8 @@ def tile_list_limb_cut_advice_kernel(
 
         high_sb = [held([P, BANK], F32, "high_sb%d" % a) for a in range(HALVES)]
         nlow_sb = [held([P, BANK], F32, "nlow_sb%d" % a) for a in range(HALVES)]
-        step_t = [held([P, BANK], F32, "step_t%d" % a) for a in range(HALVES)]
+        diff_sb = [held([P, BANK], F32, "diff_sb%d" % a) for a in range(HALVES)]
+        step_t = [[held([P, BANK], F32, "step_t%d_%d" % (s, a)) for a in range(HALVES)] for s in range(2)]
         low_t = [[held([P, BANK], F32, "low_t%d_%d" % (s, a)) for a in range(HALVES)] for s in range(2)]
         shared = [[held([P, BANK], F32, "shared%d_%d" % (s, a)) for a in range(HALVES)] for s in range(2)]
         h_sb = [held([P, S], F32, "h_sb%d" % s) for s in range(2)]
@@ -208,11 +209,14 @@ def tile_list_limb_cut_advice_kernel(
             for a in range(HALVES):
                 nc.scalar.activation(shared[0][a][:], diff_bank[a][:], ACT.Sigmoid)
             for a in range(HALVES):
-                nc.vector.tensor_tensor(step_t[a][:], high_bank[a][:], low_t[0][a][:], ALU.subtract)
+                nc.vector.tensor_tensor(step_t[0][a][:], high_bank[a][:], low_t[0][a][:], ALU.subtract)
             for a in range(HALVES):
-                nc.vector.tensor_tensor(step_t[a][:], step_t[a][:], shared[0][a][:], ALU.mult)
+                nc.vector.tensor_tensor(step_t[0][a][:], step_t[0][a][:], shared[0][a][:], ALU.mult)
             for a in range(HALVES):
-                nc.vector.tensor_tensor(h_sb[0][:, a * BANK : (a + 1) * BANK], step_t[a][:], low_t[0][a][:], ALU.add)
+                nc.vector.tensor_tensor(step_t[0][a][:], step_t[0][a][:], low_t[0][a][:], ALU.add)
+            for a in range(HALVES):
+                cols = slice(a * BANK, (a + 1) * BANK)
+                nc.vector.tensor_tensor(h_sb[0][:, cols], step_t[0][a][:], wgs_t[0][:, cols], ALU.mult)
 
         def products(i):
             b, t = divmod(i, PACK)
@@ -236,21 +240,23 @@ def tile_list_limb_cut_advice_kernel(
             for a in range(HALVES):
                 nc.scalar.activation(shared[i % 2][a][:], high_bank[a][:], ACT.Sigmoid)
             for a in range(HALVES):
+                nc.scalar.copy(diff_sb[a][:], diff_bank[a][:])
+            for a in range(HALVES):
                 nc.scalar.activation(low_t[i % 2][a][:], low_bank[a][:], ACT.Copy, scale=-1.0)
 
         def interpolate(i):
             for a in range(HALVES):
-                nc.vector.tensor_tensor(step_t[a][:], diff_bank[a][:], shared[i % 2][a][:], ALU.mult)
+                nc.gpsimd.tensor_tensor(step_t[i % 2][a][:], diff_sb[a][:], shared[i % 2][a][:], ALU.mult)
             for a in range(HALVES):
-                add_transposed(h_bank[a], low_t[i % 2][a], step_t[a])
-                nc.scalar.copy(h_sb[i % 2][:, a * BANK : (a + 1) * BANK], h_bank[a][:])
+                cols = slice(a * BANK, (a + 1) * BANK)
+                add_transposed(h_bank[a], low_t[i % 2][a], step_t[i % 2][a])
+                nc.scalar.copy(h_sb[i % 2][:, cols], h_bank[a][:])
+                nc.gpsimd.tensor_tensor(h_sb[i % 2][:, cols], h_sb[i % 2][:, cols], wgs_t[i % PACK][:, cols], ALU.mult)
 
         def scatter(i, width):
             for j0 in range(0, S, width):
-                cols = slice(j0, j0 + width)
-                nc.vector.tensor_tensor(
-                    pages[i][:].indirect(offsets("offs2", j0, width)),
-                    h_sb[i % 2][:, cols], wgs_t[i % PACK][:, cols], ALU.mult,
+                nc.vector.tensor_copy(
+                    pages[i][:].indirect(offsets("offs2", j0, width)), h_sb[i % 2][:, j0 : j0 + width]
                 )
 
         def fetch_bearers(i, m0, into):
@@ -299,19 +305,15 @@ def tile_list_limb_cut_advice_kernel(
         quantise_wl(0, 2, 2, nc.vector.tensor_copy)
         first_tile()
         last = TILES - 1
-        jobs = [(i, a * BANK) for i in range(last - 1) for a in range(HALVES)]
-        done = 0
         for i in range(last):
             products(i + 1)
-            scatter(i, S if i != 1 and i != 2 else BANK)
+            scatter(i, S)
             interpolate(i + 1)
-            now = jobs[done : done + (1 if i < 2 else 2)]
-            done = done + len(now)
-            free = shared[(i + 1) % 2][HALVES - len(now) :]
-            for (tile_i, m0), buf in zip(now, free):
-                fetch_bearers(tile_i, m0, buf[:])
-            for (tile_i, m0), buf in zip(now, free):
-                fetch_limbs(tile_i, m0, buf[:], early[tile_i // PACK][:, tile_i % PACK, m0 : m0 + BANK])
+            if i < last - 1:
+                for a in range(HALVES):
+                    fetch_bearers(i, a * BANK, step_t[i % 2][a][:])
+                for a in range(HALVES):
+                    fetch_limbs(i, a * BANK, step_t[i % 2][a][:], early[i // PACK][:, i % PACK, a * BANK : (a + 1) * BANK])
             if i == 0:
                 load_page(4)
                 load_page(5)
@@ -327,7 +329,7 @@ def tile_list_limb_cut_advice_kernel(
             grouped = spent[m0 // CHUNK][:].bitcast(BF16)[:, x : x + width * PACK]
             round_z(early[0][:, :, m0 : m0 + width], grouped, slice(0, PACK))
             quantise_z(0, m0, grouped)
-        scatter(last, S)
+        scatter(last, BANK)
         late = {m0: held([P, w * PACK], BF16, "late%d" % m0) for m0, w in CHUNKS}
         for m0, width in CHUNKS:
             score_pass(0, m0, width)
@@ -344,7 +346,7 @@ def tile_list_limb_cut_advice_kernel(
                 finish(*CHUNKS[c - 2])
             if m0 % CHUNK == 0:
                 for s, i in enumerate((last - 1, last)):
-                    source = shared[0][s][:] if c < 2 else late[m0 - 2 * CHUNK][:].bitcast(F32)
+                    source = step_t[0][s][:] if c < 2 else late[m0 - 2 * CHUNK][:].bitcast(F32)
                     x = (m0 if c < 2 else s * CHUNK)
                     bearers[i] = source[:, x : x + CHUNK]
                     fetch_bearers(i, m0, bearers[i])

@@ -45,7 +45,7 @@ def tile_list_limb_cut_advice_kernel(
             return keep.tile(shape, dtype, name=name, align_bytes=64)
 
         banks = [psum.tile([P, BANK], F32, name="bank%d" % i) for i in range(8)]
-        low_bank, high_bank, diff_bank, h_bank = banks[0:2], banks[2:4], banks[4:6], banks[6:8]
+        low_bank, high_bank, gate_bank = banks[0:2], banks[2:4], banks[4:6]
 
         lists = {}
         for name in ("offs", "offs2", "offs3", "offs4"):
@@ -57,8 +57,8 @@ def tile_list_limb_cut_advice_kernel(
         tab_w = held([P, T], U32, "tab_w")
         tab_s = held([P, T], U8, "tab_s")
         w_s = held([P, H], U8, "w_s")
-        wh_w = [held([P, PASS], U32, "wh_w%d" % b) for b in range(PASSES)]
-        wg_w = [held([P, 2 * PASS], U8, "wg_w%d" % b) for b in range(PASSES)]
+        wh_w = held([P, H], U32, "wh_w")
+        wg_w = held([P, 2 * H], U8, "wg_w")
         ident = held([P, P], F32, "ident")
         warm = held([P, 16], F32, "warm")
 
@@ -90,20 +90,14 @@ def tile_list_limb_cut_advice_kernel(
             for q in range(QUADS):
                 nc.sync.dma_start(out=wgs_t[t][32 * q : 32 * q + 32, :], in_=wgs_rows[t])
 
-        wh_rows = wh_words[0].rearrange("p c i -> p (c i)").bitcast(I32)
-        wg_rows = wg_words[0].bitcast(I32)
-
-        def load_packed_weights(b):
-            nc.sync.dma_start(out=wh_w[b][:].bitcast(I32), in_=wh_rows[:, b * PASS : (b + 1) * PASS])
-            nc.sync.dma_start(out=wg_w[b][:].bitcast(I32), in_=wg_rows[:, b * PASS // 2 : (b + 1) * PASS // 2])
-
         nc.sync.dma_start(lists["offs"][:], offs)
         for q in range(QUADS):
             rows = tab_scales[0, 4 * q : 4 * q + 4, :].bitcast(I32)
             nc.sync.dma_start(out=tab_s[32 * q : 32 * q + 32, :].bitcast(I32), in_=rows.partition_broadcast(8))
         nc.sync.dma_start(out=tab_w[:].bitcast(I32), in_=tab_words[0].rearrange("p t i -> p (t i)").bitcast(I32))
         wl_raw = [load_f32_rows(wl[:, 0:PASS])]
-        load_packed_weights(0)
+        nc.sync.dma_start(out=wh_w[:].bitcast(I32), in_=wh_words[0].rearrange("p c i -> p (c i)").bitcast(I32))
+        nc.sync.dma_start(out=wg_w[:].bitcast(I32), in_=wg_words[0].bitcast(I32))
         load_scale_rows(w_s, wh_scales, WH_ROW, nc.sync)
         load_scale_rows(w_s, wg_scales, 0, nc.gpsimd)
         make_identity(nc, ident[:])
@@ -115,7 +109,6 @@ def tile_list_limb_cut_advice_kernel(
         load_wgs(1)
         load_page(1)
         wl_raw.append(load_f32_rows(wl[:, PASS : 2 * PASS]))
-        load_packed_weights(1)
         for i in (2, 3):
             load_wgs(i)
             load_page(i)
@@ -137,121 +130,104 @@ def tile_list_limb_cut_advice_kernel(
 
         def order_packed_weights(b):
             for dst, src in (
-                (wh_p[b][:], wh_w[b][:]),
+                (wh_p[b][:], wh_w[:, b * PASS : (b + 1) * PASS]),
                 (ws_p[b][:], w_s[:, b * PASS : (b + 1) * PASS]),
-                (wg_p[b][:].bitcast(U16), wg_w[b][:].bitcast(U16)),
+                (wg_p[b][:].bitcast(U16), wg_w[:].bitcast(U16)[:, b * PASS : (b + 1) * PASS]),
             ):
                 nc.vector.tensor_copy(
                     dst.rearrange("p (t m) -> p m t", t=PACK), src.rearrange("p (m t) -> p m t", t=PACK)
                 )
 
-        def quantise_wl(b, t0, count, copy):
-            grouped = ring.tile([P, count * PASS], BF16, name="grouped", align_bytes=64)
+        def quantise_wl(b, t0, count, copy, grouped):
             copy(
-                grouped[:].rearrange("p (t m j) -> p m j t", t=count, j=PACK),
+                grouped.rearrange("p (t m j) -> p m j t", t=count, j=PACK),
                 wl_raw[b][:].rearrange("p j (m t) -> p m j t", t=PACK)[:, :, :, t0 : t0 + count],
             )
             cols = slice(t0 * P, (t0 + count) * P)
-            nc.vector.quantize_mx(out=wl_w[b][:, cols].bitcast(FP8X4), scales=wl_s[b][:, cols], in_=grouped[:])
+            nc.vector.quantize_mx(out=wl_w[b][:, cols].bitcast(FP8X4), scales=wl_s[b][:, cols], in_=grouped)
 
-        def quantise_wd(b):
+        def quantise_wd(b, grouped):
             raw = load_f32_rows(wd[b * PASS : (b + 1) * PASS, :])
-            grouped = ring.tile([P, N * PACK], BF16, name="grouped", align_bytes=64)
-            for n0 in range(0, N, CHUNK):
-                nc.scalar.copy(
-                    grouped[:, n0 * PACK : (n0 + CHUNK) * PACK].rearrange("p (n t) -> p n t", t=PACK),
-                    raw[:, :, n0 : n0 + CHUNK].rearrange("p t n -> p n t"),
-                )
-            nc.vector.quantize_mx(out=wd_w[b][:].bitcast(FP8X4), scales=wd_s[b][:], in_=grouped[:])
+            nc.scalar.copy(grouped.rearrange("p (n t) -> p n t", t=PACK), raw[:].rearrange("p t n -> p n t"))
+            nc.vector.quantize_mx(out=wd_w[b][:].bitcast(FP8X4), scales=wd_s[b][:], in_=grouped)
 
-        high_sb = [held([P, BANK], F32, "high_sb%d" % a) for a in range(HALVES)]
-        nlow_sb = [held([P, BANK], F32, "nlow_sb%d" % a) for a in range(HALVES)]
-        diff_sb = [held([P, BANK], F32, "diff_sb%d" % a) for a in range(HALVES)]
-        step_t = [[held([P, BANK], F32, "step_t%d_%d" % (s, a)) for a in range(HALVES)] for s in range(2)]
-        low_t = [[held([P, BANK], F32, "low_t%d_%d" % (s, a)) for a in range(HALVES)] for s in range(2)]
-        shared = [[held([P, BANK], F32, "shared%d_%d" % (s, a)) for a in range(HALVES)] for s in range(2)]
+        high_sb = held([P, S], F32, "high_sb")
+        diff_sb = held([P, S], F32, "diff_sb")
+        step_t = [held([P, S], F32, "step_t%d" % s) for s in range(2)]
+        low_t = [held([P, S], F32, "low_t%d" % s) for s in range(2)]
+        gate_t = [held([P, S], F32, "gate_t%d" % s) for s in range(2)]
         h_sb = [held([P, S], F32, "h_sb%d" % s) for s in range(2)]
         early = [held([P, PACK, M_OUT], F32, "early0"), held([P, 2, M_OUT], F32, "early1")]
-        tail = {m0: held([P, 2, w], F32, "tail%d" % m0) for m0, w in CHUNKS}
-        z_w = [{m0: held([P, w], U32, "z_w%d_%d" % (b, m0)) for m0, w in CHUNKS} for b in range(PASSES)]
-        z_s = [{m0: held([P, w], U8, "z_s%d_%d" % (b, m0)) for m0, w in CHUNKS} for b in range(PASSES)]
+        halves = [slice(a * BANK, (a + 1) * BANK) for a in range(HALVES)]
+        z_w = [held([P, M_OUT], U32, "z_w%d" % b) for b in range(PASSES)]
+        z_s = [held([P, M_OUT], U8, "z_s%d" % b) for b in range(PASSES)]
 
         def blocks():
             return [slice(x, x + P) for x in range(0, BANK, P)]
 
-        def add_transposed(bank, first, second):
+        def add_transposed(bank, source, opens):
             for blk in blocks():
-                nc.tensor.matmul(bank[:, blk], first[:, blk], ident[:], start=True, stop=False, is_transpose=True)
-                nc.tensor.matmul(bank[:, blk], second[:, blk], ident[:], start=False, stop=True, is_transpose=True)
+                nc.tensor.matmul(
+                    bank[:, blk], source[:, blk], ident[:], is_transpose=True,
+                    start=(opens and blk.start == 0), stop=(not opens and blk.stop == BANK),
+                )
 
-        def high_and_low(i):
+        def operands(i):
             b, t = divmod(i, PACK)
             cols = slice(t * P, (t + 1) * P)
-            for a in range(HALVES):
-                nc.tensor.matmul_mx(
-                    high_bank[a][:], lhsT=wh_p[b][:, cols].bitcast(FP8X4), lhsT_scale=ws_p[b][WH_ROW:P, cols],
-                    rhs=v_w[a][:].bitcast(FP8X4), rhs_scale=v_s[a][:], start=True, stop=True,
-                )
-                nc.tensor.matmul_mx(
-                    low_bank[a][:], lhsT=wl_w[b][:, cols].bitcast(FP8X4), lhsT_scale=wl_s[b][:, cols],
-                    rhs=v_w[a][:].bitcast(FP8X4), rhs_scale=v_s[a][:], start=True, stop=True,
-                )
+            return (
+                (high_bank, wh_p[b][:, cols].bitcast(FP8X4), ws_p[b][WH_ROW:P, cols]),
+                (low_bank, wl_w[b][:, cols].bitcast(FP8X4), wl_s[b][:, cols]),
+                (gate_bank, wg_p[b][:, 2 * t * P : 2 * (t + 1) * P].bitcast(FP4X4), ws_p[b][:, cols]),
+            )
 
         def first_tile():
-            high_and_low(0)
             for a in range(HALVES):
-                nc.tensor.matmul_mx(
-                    diff_bank[a][:], lhsT=wg_p[0][:, 0 : 2 * P].bitcast(FP4X4), lhsT_scale=ws_p[0][:, 0:P],
-                    rhs=v_w[a][:].bitcast(FP8X4), rhs_scale=v_s[a][:], start=True, stop=True,
-                )
-            for a in range(HALVES):
-                nc.scalar.copy(low_t[0][a][:], low_bank[a][:])
-            for a in range(HALVES):
-                nc.scalar.activation(shared[0][a][:], diff_bank[a][:], ACT.Sigmoid)
-            for a in range(HALVES):
-                nc.vector.tensor_tensor(step_t[0][a][:], high_bank[a][:], low_t[0][a][:], ALU.subtract)
-            for a in range(HALVES):
-                nc.vector.tensor_tensor(step_t[0][a][:], step_t[0][a][:], shared[0][a][:], ALU.mult)
-            for a in range(HALVES):
-                nc.vector.tensor_tensor(step_t[0][a][:], step_t[0][a][:], low_t[0][a][:], ALU.add)
-            for a in range(HALVES):
-                cols = slice(a * BANK, (a + 1) * BANK)
-                nc.vector.tensor_tensor(h_sb[0][:, cols], step_t[0][a][:], wgs_t[0][:, cols], ALU.mult)
-
-        def products(i):
-            b, t = divmod(i, PACK)
-            cols = slice(t * P, (t + 1) * P)
-            high_and_low(i)
-            for a in range(HALVES):
-                nc.scalar.copy(high_sb[a][:], high_bank[a][:])
-                nc.scalar.activation(nlow_sb[a][:], low_bank[a][:], ACT.Copy, scale=-1.0)
-            for a in range(HALVES):
-                for blk in blocks():
+                for bank, words, scales in operands(0):
                     nc.tensor.matmul_mx(
-                        high_bank[a][:, blk], lhsT=v_w[a][:, blk].bitcast(FP8X4), lhsT_scale=v_s[a][:, blk],
-                        rhs=wg_p[b][:, 2 * t * P : 2 * (t + 1) * P].bitcast(FP4X4), rhs_scale=ws_p[b][:, cols],
-                        start=True, stop=True,
+                        bank[a][:], lhsT=words, lhsT_scale=scales,
+                        rhs=v_w[a][:].bitcast(FP8X4), rhs_scale=v_s[a][:], start=True, stop=True,
                     )
             for a in range(HALVES):
-                add_transposed(diff_bank[a], high_sb[a], nlow_sb[a])
+                nc.scalar.copy(low_t[0][:, halves[a]], low_bank[a][:])
             for a in range(HALVES):
-                for blk in blocks():
-                    nc.tensor.transpose(low_bank[a][:, blk], nlow_sb[a][:, blk], ident[:])
+                nc.scalar.activation(gate_t[0][:, halves[a]], gate_bank[a][:], ACT.Sigmoid)
             for a in range(HALVES):
-                nc.scalar.activation(shared[i % 2][a][:], high_bank[a][:], ACT.Sigmoid)
+                nc.vector.tensor_tensor(step_t[0][:, halves[a]], high_bank[a][:], low_t[0][:, halves[a]], ALU.subtract)
+            for other, op in ((gate_t[0], ALU.mult), (low_t[0], ALU.add)):
+                for a in range(HALVES):
+                    nc.vector.tensor_tensor(step_t[0][:, halves[a]], step_t[0][:, halves[a]], other[:, halves[a]], op)
             for a in range(HALVES):
-                nc.scalar.copy(diff_sb[a][:], diff_bank[a][:])
-            for a in range(HALVES):
-                nc.scalar.activation(low_t[i % 2][a][:], low_bank[a][:], ACT.Copy, scale=-1.0)
+                nc.vector.tensor_tensor(h_sb[0][:, halves[a]], step_t[0][:, halves[a]], wgs_t[0][:, halves[a]], ALU.mult)
 
-        def interpolate(i):
+        def products(i):
             for a in range(HALVES):
-                nc.gpsimd.tensor_tensor(step_t[i % 2][a][:], diff_sb[a][:], shared[i % 2][a][:], ALU.mult)
+                for bank, words, scales in operands(i):
+                    for blk in blocks():
+                        nc.tensor.matmul_mx(
+                            bank[a][:, blk], lhsT=v_w[a][:, blk].bitcast(FP8X4), lhsT_scale=v_s[a][:, blk],
+                            rhs=words, rhs_scale=scales, start=True, stop=True,
+                        )
             for a in range(HALVES):
-                cols = slice(a * BANK, (a + 1) * BANK)
-                add_transposed(h_bank[a], low_t[i % 2][a], step_t[i % 2][a])
-                nc.scalar.copy(h_sb[i % 2][:, cols], h_bank[a][:])
-                nc.gpsimd.tensor_tensor(h_sb[i % 2][:, cols], h_sb[i % 2][:, cols], wgs_t[i % PACK][:, cols], ALU.mult)
+                nc.scalar.copy(high_sb[:, halves[a]], high_bank[a][:])
+                nc.scalar.copy(low_t[i % 2][:, halves[a]], low_bank[a][:])
+            for a in range(HALVES):
+                nc.scalar.activation(gate_t[i % 2][:, halves[a]], gate_bank[a][:], ACT.Sigmoid)
+            nc.gpsimd.tensor_tensor(diff_sb[:], high_sb[:], low_t[i % 2][:], ALU.subtract)
+
+        def interpolate(i, staged, width):
+            for a in range(HALVES):
+                add_transposed(gate_bank[a], low_t[i % 2][:, halves[a]], True)
+            for a in range(HALVES):
+                nc.gpsimd.tensor_tensor(
+                    step_t[i % 2][:, halves[a]], diff_sb[:, halves[a]], gate_t[i % 2][:, halves[a]], ALU.mult
+                )
+            for a in range(HALVES):
+                add_transposed(gate_bank[a], step_t[i % 2][:, halves[a]], False)
+                nc.scalar.copy(staged[:, halves[a]], gate_bank[a][:])
+            for j0 in range(0, S, width):
+                cols = slice(j0, j0 + width)
+                nc.gpsimd.tensor_tensor(h_sb[i % 2][:, cols], staged[:, cols], wgs_t[i % PACK][:, cols], ALU.mult)
 
         def scatter(i, width):
             for j0 in range(0, S, width):
@@ -271,7 +247,8 @@ def tile_list_limb_cut_advice_kernel(
             )
 
         def quantise_z(b, m0, grouped):
-            nc.vector.quantize_mx(out=z_w[b][m0][:].bitcast(FP8X4), scales=z_s[b][m0][:], in_=grouped)
+            cols = slice(m0, m0 + grouped.shape[1] // PACK)
+            nc.vector.quantize_mx(out=z_w[b][:, cols].bitcast(FP8X4), scales=z_s[b][:, cols], in_=grouped)
 
         def score_pass(b, m0, width):
             per_bank = BANK // width
@@ -281,81 +258,97 @@ def tile_list_limb_cut_advice_kernel(
                 nc.tensor.matmul_mx(
                     banks[m0 // P + part][:, side * width : (side + 1) * width],
                     lhsT=wd_w[b][:, cols].bitcast(FP8X4), lhsT_scale=wd_s[b][:, cols],
-                    rhs=z_w[b][m0][:].bitcast(FP8X4), rhs_scale=z_s[b][m0][:],
+                    rhs=z_w[b][:, m0 : m0 + width].bitcast(FP8X4), rhs_scale=z_s[b][:, m0 : m0 + width],
                     start=(b == 0 and side == 0), stop=(b == PASSES - 1 and side == per_bank - 1),
                 )
 
-        def store(m0, width):
+        def store(m0, width, part, copy, staged):
             per_bank = BANK // width
             out_rows = out.rearrange("(a s p) m -> a p s m", s=per_bank, p=P)
-            for part in range(width // P):
-                staged = ring.tile([P, BANK], F32, name="staged", bufs=4)
-                if m0 + width == M_OUT or (m0 == 512 and part == 1):
-                    nc.vector.tensor_copy(staged[:], banks[m0 // P + part][:])
-                else:
-                    nc.scalar.copy(staged[:], banks[m0 // P + part][:])
-                nc.sync.dma_start(
-                    out=out_rows[part][:, :, m0 : m0 + width],
-                    in_=staged[:].rearrange("p (s m) -> p s m", s=per_bank),
-                )
+            copy(staged, banks[m0 // P + part][:])
+            nc.sync.dma_start(
+                out=out_rows[part][:, :, m0 : m0 + width], in_=staged.rearrange("p (s m) -> p s m", s=per_bank)
+            )
 
-        quantise_wl(0, 0, 1, nc.scalar.copy)
+        first_grouped = held([P, PASS * PACK], BF16, "first_grouped")
+        quantise_wl(0, 0, 1, nc.scalar.copy, first_grouped[:, 0:PASS])
         order_packed_weights(0)
-        quantise_wl(0, 1, 1, nc.vector.tensor_copy)
-        quantise_wl(0, 2, 2, nc.vector.tensor_copy)
+        quantise_wl(0, 1, 1, nc.scalar.copy, first_grouped[:, PASS : 2 * PASS])
+        quantise_wl(0, 2, 2, nc.scalar.copy, first_grouped[:, 2 * PASS : 4 * PASS])
+        order_packed_weights(1)
         first_tile()
         last = TILES - 1
+        products(1)
         for i in range(last):
-            products(i + 1)
             scatter(i, S)
-            interpolate(i + 1)
+            slot = early[i // PACK][:, i % PACK, :] if i < last - 1 else high_sb[:]
+            interpolate(i + 1, slot, S if i < last - 1 else BANK)
+            spent = step_t[(i + 1) % 2][:].bitcast(BF16)
+            if i == 0:
+                quantise_wl(1, 0, PACK, nc.scalar.copy, spent)
+                load_page(4)
+            if i in (1, 2):
+                quantise_wd(i - 1, spent)
+            if i in (4, 5):
+                m0 = (i - 4) * BANK
+                round_z(early[0][:, :, m0 : m0 + BANK], spent, slice(0, PACK))
+                quantise_z(0, m0, spent)
+            if i + 2 <= last:
+                products(i + 2)
             if i < last - 1:
                 for a in range(HALVES):
-                    fetch_bearers(i, a * BANK, step_t[i % 2][a][:])
+                    fetch_bearers(i, a * BANK, step_t[i % 2][:, halves[a]])
                 for a in range(HALVES):
-                    fetch_limbs(i, a * BANK, step_t[i % 2][a][:], early[i // PACK][:, i % PACK, a * BANK : (a + 1) * BANK])
-            if i == 0:
-                load_page(4)
-                load_page(5)
-            if i == 1:
-                order_packed_weights(1)
-                quantise_wl(1, 0, PACK, nc.scalar.copy)
-            if i in (2, 3):
-                quantise_wd(i - 2)
+                    fetch_limbs(i, a * BANK, step_t[i % 2][:, halves[a]], slot[:, halves[a]])
+            if i in (1, 2, 3):
                 load_page(i + 4)
-        spent = high_sb + nlow_sb
-        for m0, width in CHUNKS:
-            x = (m0 % CHUNK) * PACK
-            grouped = spent[m0 // CHUNK][:].bitcast(BF16)[:, x : x + width * PACK]
-            round_z(early[0][:, :, m0 : m0 + width], grouped, slice(0, PACK))
-            quantise_z(0, m0, grouped)
-        scatter(last, BANK)
+        scatter(last, S)
         late = {m0: held([P, w * PACK], BF16, "late%d" % m0) for m0, w in CHUNKS}
         for m0, width in CHUNKS:
             score_pass(0, m0, width)
             round_z(early[1][:, :, m0 : m0 + width], late[m0][:], slice(0, 2))
 
+        wide, narrow = CHUNKS[:3], CHUNKS[3:]
+        tail = {m0: held([P, 2, w], F32, "tail%d" % m0)[:] for m0, w in wide}
+        reused = late[wide[-1][0]][:].bitcast(F32)
+        for n, (m0, width) in enumerate(narrow):
+            tail[m0] = reused[:, 2 * n * width : 2 * (n + 1) * width].rearrange("p (s m) -> p s m", s=2)
+        staged = [held([P, BANK], F32, "staged%d" % n) for n in range(7)]
+
         def finish(m0, width):
-            round_z(tail[m0][:], late[m0][:], slice(2, PACK))
+            round_z(tail[m0], late[m0][:], slice(2, PACK))
             quantise_z(1, m0, late[m0][:])
             score_pass(1, m0, width)
 
-        bearers = {}
-        for c, (m0, width) in enumerate(CHUNKS):
-            if c >= 2:
-                finish(*CHUNKS[c - 2])
-            if m0 % CHUNK == 0:
-                for s, i in enumerate((last - 1, last)):
-                    source = step_t[0][s][:] if c < 2 else late[m0 - 2 * CHUNK][:].bitcast(F32)
-                    x = (m0 if c < 2 else s * CHUNK)
-                    bearers[i] = source[:, x : x + CHUNK]
-                    fetch_bearers(i, m0, bearers[i])
+        def fetch_all_bearers(m0, into):
             for s, i in enumerate((last - 1, last)):
-                x = m0 % CHUNK
-                fetch_limbs(i, m0, bearers[i][:, x : x + width], tail[m0][:, s, :])
+                fetch_bearers(i, m0, into[s])
+
+        def fetch_all_limbs(m0, width, bearers):
+            x = m0 % CHUNK
+            for s, i in enumerate((last - 1, last)):
+                fetch_limbs(i, m0, bearers[s][:, x : x + width], tail[m0][:, s, :])
+
+        for c in range(M_OUT // CHUNK):
+            m0 = c * CHUNK
+            if c < 2:
+                bearers = [step_t[0][:, s * BANK + m0 : s * BANK + m0 + CHUNK] for s in range(2)]
+            else:
+                finish(*CHUNKS[c - 2])
+                words = late[m0 - 2 * CHUNK][:].bitcast(F32)
+                bearers = [words[:, s * CHUNK : (s + 1) * CHUNK] for s in range(2)]
+            fetch_all_bearers(m0, bearers)
+            if c < len(wide):
+                fetch_all_limbs(m0, CHUNK, bearers)
             if c >= 2:
-                store(*CHUNKS[c - 2])
-        for m0, width in CHUNKS[-2:]:
+                for part in range(2):
+                    store(*CHUNKS[c - 2], part, nc.scalar.copy, staged[2 * (c - 2) + part][:])
+        finish(*wide[-1])
+        for m0, width in narrow:
+            fetch_all_limbs(m0, width, bearers)
+        for m0, width in narrow:
             finish(m0, width)
-        for m0, width in CHUNKS[-2:]:
-            store(m0, width)
+        store(*wide[-1], 0, nc.scalar.copy, reused)
+        store(*wide[-1], 1, nc.vector.tensor_copy, staged[4][:])
+        store(*narrow[0], 0, nc.scalar.copy, staged[5][:])
+        store(*narrow[1], 0, nc.vector.tensor_copy, staged[6][:])

@@ -64,7 +64,6 @@ def tile_list_limb_cut_advice_kernel(
 
         nc.gpsimd.memset(w_s[:].bitcast(I32), 0)
         nc.gpsimd.memset(warm[:, 0:8], 0.0)
-        nc.scalar.activation(warm[:, 8:16], warm[:, 0:8], ACT.Sigmoid)
 
         def load_scale_rows(plane, rows, first, queue):
             for q in range(QUADS):
@@ -93,25 +92,27 @@ def tile_list_limb_cut_advice_kernel(
         nc.sync.dma_start(lists["offs"][:], offs)
         for q in range(QUADS):
             rows = tab_scales[0, 4 * q : 4 * q + 4, :].bitcast(I32)
-            nc.sync.dma_start(out=tab_s[32 * q : 32 * q + 32, :].bitcast(I32), in_=rows.partition_broadcast(8))
+            nc.scalar.dma_start(out=tab_s[32 * q : 32 * q + 32, :].bitcast(I32), in_=rows.partition_broadcast(8))
         nc.sync.dma_start(out=tab_w[:].bitcast(I32), in_=tab_words[0].rearrange("p t i -> p (t i)").bitcast(I32))
         wl_raw = [load_f32_rows(wl[:, 0:PASS])]
         nc.sync.dma_start(out=wh_w[:].bitcast(I32), in_=wh_words[0].rearrange("p c i -> p (c i)").bitcast(I32))
         nc.sync.dma_start(out=wg_w[:].bitcast(I32), in_=wg_words[0].bitcast(I32))
-        load_scale_rows(w_s, wh_scales, WH_ROW, nc.sync)
-        load_scale_rows(w_s, wg_scales, 0, nc.gpsimd)
+        load_scale_rows(w_s, wh_scales, WH_ROW, nc.scalar)
+        load_scale_rows(w_s, wg_scales, 0, nc.scalar)
+        nc.scalar.activation(warm[:, 8:16], warm[:, 0:8], ACT.Sigmoid)
         make_identity(nc, ident[:])
         load_page(0)
         nc.sync.dma_start(lists["offs2"][:], offs2)
         load_wgs(0)
         nc.sync.dma_start(lists["offs4"][:], offs4)
         nc.sync.dma_start(lists["offs3"][:], offs3)
-        load_wgs(1)
-        load_page(1)
         wl_raw.append(load_f32_rows(wl[:, PASS : 2 * PASS]))
-        for i in (2, 3):
+        for i in (1, 2):
             load_wgs(i)
             load_page(i)
+        wd_raw = [load_f32_rows(wd[0:PASS, :])]
+        load_wgs(3)
+        load_page(3)
 
         v_w = [held([P, BANK], U32, "v_w%d" % a) for a in range(HALVES)]
         v_s = [held([P, BANK], U8, "v_s%d" % a) for a in range(HALVES)]
@@ -135,20 +136,22 @@ def tile_list_limb_cut_advice_kernel(
                 (wg_p[b][:].bitcast(U16), wg_w[:].bitcast(U16)[:, b * PASS : (b + 1) * PASS]),
             ):
                 nc.vector.tensor_copy(
-                    dst.rearrange("p (t m) -> p m t", t=PACK), src.rearrange("p (m t) -> p m t", t=PACK)
+                    dst.rearrange("p (t m) -> p t m", t=PACK), src.rearrange("p (m t) -> p t m", t=PACK)
                 )
 
-        def quantise_wl(b, t0, count, copy, grouped):
-            copy(
-                grouped.rearrange("p (t m j) -> p m j t", t=count, j=PACK),
-                wl_raw[b][:].rearrange("p j (m t) -> p m j t", t=PACK)[:, :, :, t0 : t0 + count],
+        def quantise_wl(b, t0, count, grouped):
+            nc.scalar.copy(
+                grouped.rearrange("p (t m j) -> p t m j", t=count, j=PACK),
+                wl_raw[b][:].rearrange("p j (m t) -> p t m j", t=PACK)[:, t0 : t0 + count],
             )
             cols = slice(t0 * P, (t0 + count) * P)
             nc.vector.quantize_mx(out=wl_w[b][:, cols].bitcast(FP8X4), scales=wl_s[b][:, cols], in_=grouped)
 
         def quantise_wd(b, grouped):
-            raw = load_f32_rows(wd[b * PASS : (b + 1) * PASS, :])
-            nc.scalar.copy(grouped.rearrange("p (n t) -> p n t", t=PACK), raw[:].rearrange("p t n -> p n t"))
+            nc.scalar.copy(
+                grouped.rearrange("p (c i t) -> p c t i", i=PACK, t=PACK),
+                wd_raw[b][:].rearrange("p t (c i) -> p c t i", i=PACK),
+            )
             nc.vector.quantize_mx(out=wd_w[b][:].bitcast(FP8X4), scales=wd_s[b][:], in_=grouped)
 
         high_sb = held([P, S], F32, "high_sb")
@@ -211,9 +214,9 @@ def tile_list_limb_cut_advice_kernel(
             for a in range(HALVES):
                 nc.scalar.copy(high_sb[:, halves[a]], high_bank[a][:])
                 nc.scalar.copy(low_t[i % 2][:, halves[a]], low_bank[a][:])
+            nc.gpsimd.tensor_tensor(diff_sb[:], high_sb[:], low_t[i % 2][:], ALU.subtract)
             for a in range(HALVES):
                 nc.scalar.activation(gate_t[i % 2][:, halves[a]], gate_bank[a][:], ACT.Sigmoid)
-            nc.gpsimd.tensor_tensor(diff_sb[:], high_sb[:], low_t[i % 2][:], ALU.subtract)
 
         def interpolate(i, staged, width):
             for a in range(HALVES):
@@ -243,7 +246,8 @@ def tile_list_limb_cut_advice_kernel(
 
         def round_z(source, grouped, slots):
             nc.scalar.activation(
-                grouped.rearrange("p (m t) -> p m t", t=PACK)[:, :, slots], source.rearrange("p t m -> p m t"), ACT.Abs
+                grouped.rearrange("p (c i t) -> p c t i", i=PACK, t=PACK)[:, :, slots, :],
+                source.rearrange("p t (c i) -> p c t i", i=PACK), ACT.Abs,
             )
 
         def quantise_z(b, m0, grouped):
@@ -271,12 +275,13 @@ def tile_list_limb_cut_advice_kernel(
             )
 
         first_grouped = held([P, PASS * PACK], BF16, "first_grouped")
-        quantise_wl(0, 0, 1, nc.scalar.copy, first_grouped[:, 0:PASS])
+        for t in range(2):
+            quantise_wl(0, t, 1, first_grouped[:, t * PASS : (t + 1) * PASS])
         order_packed_weights(0)
-        quantise_wl(0, 1, 1, nc.scalar.copy, first_grouped[:, PASS : 2 * PASS])
-        quantise_wl(0, 2, 2, nc.scalar.copy, first_grouped[:, 2 * PASS : 4 * PASS])
         order_packed_weights(1)
         first_tile()
+        for t in range(2, PACK):
+            quantise_wl(0, t, 1, first_grouped[:, t * PASS : (t + 1) * PASS])
         last = TILES - 1
         products(1)
         for i in range(last):
@@ -284,11 +289,12 @@ def tile_list_limb_cut_advice_kernel(
             slot = early[i // PACK][:, i % PACK, :] if i < last - 1 else high_sb[:]
             interpolate(i + 1, slot, S if i < last - 1 else BANK)
             spent = step_t[(i + 1) % 2][:].bitcast(BF16)
-            if i == 0:
-                quantise_wl(1, 0, PACK, nc.scalar.copy, spent)
-                load_page(4)
-            if i in (1, 2):
-                quantise_wd(i - 1, spent)
+            if i in (0, 1):
+                quantise_wl(1, 2 * i, 2, spent[:, 2 * PASS : 4 * PASS])
+            if i == 1:
+                wd_raw.append(load_f32_rows(wd[PASS : 2 * PASS, :]))
+            if i in (2, 3):
+                quantise_wd(i - 2, spent)
             if i in (4, 5):
                 m0 = (i - 4) * BANK
                 round_z(early[0][:, :, m0 : m0 + BANK], spent, slice(0, PACK))
@@ -300,8 +306,8 @@ def tile_list_limb_cut_advice_kernel(
                     fetch_bearers(i, a * BANK, step_t[i % 2][:, halves[a]])
                 for a in range(HALVES):
                     fetch_limbs(i, a * BANK, step_t[i % 2][:, halves[a]], slot[:, halves[a]])
-            if i in (1, 2, 3):
-                load_page(i + 4)
+            if i + PACK <= last:
+                load_page(i + PACK)
         scatter(last, S)
         late = {m0: held([P, w * PACK], BF16, "late%d" % m0) for m0, w in CHUNKS}
         for m0, width in CHUNKS:

@@ -21,14 +21,15 @@ P = 128
 PACK = 4
 PASS = P * PACK
 BANK = 512
-QUADS = 4
-PASSES = H // PASS
+QUAD = 32
+QUADS = P // QUAD
+RUN = 8
 TILES = H // P
-HALVES = S // BANK
+LAST = TILES - 1
 CHUNK = 256
-CHUNKS = ((0, 256), (256, 256), (512, 256), (768, 128), (896, 128))
-PAGE_BUFS = 6
-WH_ROW = 4
+PIECES = ((0, 256), (256, 256), (512, 256), (768, 128), (896, 128))
+PAGE_BUFS = 5
+STEP_BUFS = 4
 
 
 def tile_list_limb_cut_advice_kernel(
@@ -38,323 +39,352 @@ def tile_list_limb_cut_advice_kernel(
     nc = tc.nc
     with ExitStack() as ctx:
         keep = ctx.enter_context(tc.tile_pool(name="keep", bufs=1))
-        ring = ctx.enter_context(tc.tile_pool(name="ring", bufs=2))
+        ring = ctx.enter_context(tc.tile_pool(name="ring", bufs=PAGE_BUFS))
         psum = ctx.enter_context(tc.psum_pool(name="psum", bufs=1))
 
         def held(shape, dtype, name):
             return keep.tile(shape, dtype, name=name, align_bytes=64)
 
         banks = [psum.tile([P, BANK], F32, name="bank%d" % i) for i in range(8)]
-        low_bank, high_bank, gate_bank = banks[0:2], banks[2:4], banks[4:6]
+        high_bank, gate_bank, first_bank, sum_bank = banks[0:2], banks[2:4], banks[4:6], banks[6:8]
+        halves = [slice(0, BANK), slice(BANK, 2 * BANK)]
+        blocks = [slice(x, x + P) for x in range(0, BANK, P)]
 
-        lists = {}
-        for name in ("offs", "offs2", "offs3", "offs4"):
-            lists[name] = held([P, S // 16], U16, name)
+        lists = {name: held([P, S // 16], U16, name) for name in ("offs", "offs2", "offs3", "offs4")}
 
         def offsets(name, start, count):
             return lists[name][:, start // 16 : (start + count) // 16]
 
-        tab_w = held([P, T], U32, "tab_w")
-        tab_s = held([P, T], U8, "tab_s")
-        w_s = held([P, H], U8, "w_s")
-        wh_w = held([P, H], U32, "wh_w")
-        wg_w = held([P, 2 * H], U8, "wg_w")
-        ident = held([P, P], F32, "ident")
-        warm = held([P, 16], F32, "warm")
-
-        nc.gpsimd.memset(w_s[:].bitcast(I32), 0)
-        nc.gpsimd.memset(warm[:, 0:8], 0.0)
-
-        def load_scale_rows(plane, rows, first, queue):
+        def load_scale_rows(name, rows, queues):
+            plane = held([P, rows.shape[2]], U8, name)
             for q in range(QUADS):
-                p0 = 32 * q + first
-                queue.dma_start(out=plane[p0 : p0 + 4, :].bitcast(I32), in_=rows[0, 4 * q : 4 * q + 4, :].bitcast(I32))
+                queues[q % len(queues)].dma_start(
+                    out=plane[QUAD * q : QUAD * (q + 1), :].bitcast(I32),
+                    in_=rows[0, 4 * q : 4 * q + 4, :].bitcast(I32).partition_broadcast(QUAD // 4),
+                )
+            return plane
 
-        def load_f32_rows(src):
-            raw = ring.tile([P, PACK, BANK], F32, name="raw")
+        def load_rows_of_four(name, src):
+            raw = held([P, PACK, src.shape[1]], F32, name)
             nc.sync.dma_start(out=raw[:], in_=src.rearrange("(p j) c -> p j c", j=PACK))
             return raw
 
-        page_rows = page0.rearrange("(b p t) c -> b t p c", p=P, t=PACK)
+        wh_i32 = wh_words[0].rearrange("p c i -> p (c i)").bitcast(I32)
+        wg_i32 = wg_words[0].bitcast(I32)
+
+        def load_words(name, src):
+            words = held([P, src.shape[1]], I32, name)
+            nc.sync.dma_start(out=words[:], in_=src)
+            return words
+
+        def dealt_rows(src, t):
+            return src.rearrange("(q t s) c -> t q s c", t=PACK, s=RUN)[t]
+
         pages = {}
 
         def load_page(i):
-            pages[i] = ring.tile([P, T2], F32, name="page", bufs=PAGE_BUFS)
-            nc.sync.dma_start(out=pages[i][:], in_=page_rows[i // PACK, i % PACK])
+            pages[i] = ring.tile([P, T2], F32, name="page")
+            rows = page0[P * i : P * (i + 1), :] if i < PACK else dealt_rows(page0[PASS:H, :], i - PACK)
+            nc.sync.dma_start(out=pages[i][:], in_=rows)
 
-        wgs_rows = wgs.rearrange("(s t) j -> t s j", t=PACK)
-        wgs_t = [held([P, S], F32, "wgs%d" % t) for t in range(PACK)]
-
-        def load_wgs(t):
+        def load_wgs_dealt(t):
+            rows = held([P, S], F32, "wgs_dealt%d" % t)
             for q in range(QUADS):
-                nc.sync.dma_start(out=wgs_t[t][32 * q : 32 * q + 32, :], in_=wgs_rows[t])
+                nc.sync.dma_start(out=rows[QUAD * q : QUAD * (q + 1), :], in_=dealt_rows(wgs, t))
+            return rows
 
         nc.sync.dma_start(lists["offs"][:], offs)
-        for q in range(QUADS):
-            rows = tab_scales[0, 4 * q : 4 * q + 4, :].bitcast(I32)
-            nc.scalar.dma_start(out=tab_s[32 * q : 32 * q + 32, :].bitcast(I32), in_=rows.partition_broadcast(8))
-        nc.sync.dma_start(out=tab_w[:].bitcast(I32), in_=tab_words[0].rearrange("p t i -> p (t i)").bitcast(I32))
-        wl_raw = [load_f32_rows(wl[:, 0:PASS])]
-        nc.sync.dma_start(out=wh_w[:].bitcast(I32), in_=wh_words[0].rearrange("p c i -> p (c i)").bitcast(I32))
-        nc.sync.dma_start(out=wg_w[:].bitcast(I32), in_=wg_words[0].bitcast(I32))
-        load_scale_rows(w_s, wh_scales, WH_ROW, nc.scalar)
-        load_scale_rows(w_s, wg_scales, 0, nc.scalar)
-        nc.scalar.activation(warm[:, 8:16], warm[:, 0:8], ACT.Sigmoid)
-        make_identity(nc, ident[:])
+        tab_s = load_scale_rows("tab_s", tab_scales, (nc.scalar, nc.sync))
+        tab_w = held([P, T], U32, "tab_w")
+        nc.scalar.dma_start(out=tab_w[:].bitcast(I32), in_=tab_words[0].rearrange("p t i -> p (t i)").bitcast(I32))
+        wl_raw0 = load_rows_of_four("wl_raw0", wl[:, 0:P])
+        wg_s = load_scale_rows("wg_s", wg_scales, (nc.sync,))
+        wg_a = load_words("wg_a", wg_i32[:, 0:P])
+        wh_a = load_words("wh_a", wh_i32[:, 0 : 2 * P])
+        wh_s = load_scale_rows("wh_s", wh_scales, (nc.gpsimd, nc.sync))
+        wl_raw12 = load_rows_of_four("wl_raw12", wl[:, P : 3 * P])
+        wgs_natural = held([P, S], F32, "wgs_natural")
+        nc.sync.dma_start(out=wgs_natural[:], in_=wgs)
         load_page(0)
         nc.sync.dma_start(lists["offs2"][:], offs2)
-        load_wgs(0)
+        wl_raw3 = load_rows_of_four("wl_raw3", wl[:, 3 * P : PASS])
+        wh_b = load_words("wh_b", wh_i32[:, 2 * P : PASS])
+        wg_b = load_words("wg_b", wg_i32[:, P : 2 * P])
         nc.sync.dma_start(lists["offs4"][:], offs4)
         nc.sync.dma_start(lists["offs3"][:], offs3)
-        wl_raw.append(load_f32_rows(wl[:, PASS : 2 * PASS]))
-        for i in (1, 2):
-            load_wgs(i)
-            load_page(i)
-        wd_raw = [load_f32_rows(wd[0:PASS, :])]
-        load_wgs(3)
+        wl_raw_dealt = load_rows_of_four("wl_raw_dealt", wl[:, PASS:H])
+        load_page(1)
+        wh_c = load_words("wh_c", wh_i32[:, PASS:H])
+        wg_c = load_words("wg_c", wg_i32[:, 2 * P : PASS])
+        load_page(2)
         load_page(3)
+        wgs_rows = [wgs_natural] * PACK
+        wd_raw = {}
 
-        v_w = [held([P, BANK], U32, "v_w%d" % a) for a in range(HALVES)]
-        v_s = [held([P, BANK], U8, "v_s%d" % a) for a in range(HALVES)]
-        for a in range(HALVES):
-            nc.vector.tensor_copy(v_s[a][:], tab_s[:].indirect(offsets("offs", a * BANK, BANK)))
-        for a in range(HALVES):
-            nc.vector.tensor_copy(v_w[a][:], tab_w[:].indirect(offsets("offs", a * BANK, BANK)))
+        def load_later(i):
+            if i == 0:
+                wd_raw[1] = held([P, PACK, N], F32, "wd_raw1")
+                for t in range(PACK):
+                    nc.sync.dma_start(out=wd_raw[1][:, t, :], in_=dealt_rows(wd[PASS:H, :], t))
+            if i == 1:
+                wd_raw[0] = load_rows_of_four("wd_raw0", wd[0:PASS, :])
+            wgs_rows.append(load_wgs_dealt(i))
+            load_page(i + PACK)
 
-        wl_w = [held([P, PASS], U32, "wl_w%d" % b) for b in range(PASSES)]
-        wl_s = [held([P, PASS], U8, "wl_s%d" % b) for b in range(PASSES)]
-        wh_p = [held([P, PASS], U32, "wh_p%d" % b) for b in range(PASSES)]
-        wg_p = [held([P, 2 * PASS], U8, "wg_p%d" % b) for b in range(PASSES)]
-        ws_p = [held([P, PASS], U8, "ws_p%d" % b) for b in range(PASSES)]
-        wd_w = [held([P, N], U32, "wd_w%d" % b) for b in range(PASSES)]
-        wd_s = [held([P, N], U8, "wd_s%d" % b) for b in range(PASSES)]
+        ident = held([P, P], F32, "ident")
+        make_identity(nc, ident[:])
 
-        def order_packed_weights(b):
-            for dst, src in (
-                (wh_p[b][:], wh_w[:, b * PASS : (b + 1) * PASS]),
-                (ws_p[b][:], w_s[:, b * PASS : (b + 1) * PASS]),
-                (wg_p[b][:].bitcast(U16), wg_w[:].bitcast(U16)[:, b * PASS : (b + 1) * PASS]),
-            ):
-                nc.vector.tensor_copy(
-                    dst.rearrange("p (t m) -> p t m", t=PACK), src.rearrange("p (m t) -> p t m", t=PACK)
+        v_s = held([P, S], U8, "v_s")
+        wl_w = held([P, H], U32, "wl_w")
+        wl_s = held([P, H], U8, "wl_s")
+        wd_s = [held([P, N], U8, "wd_s%d" % b)[:] for b in range(2)]
+        z_w = held([P, 2 * M_OUT], U32, "z_w")
+        z_s = held([P, 2 * M_OUT], U8, "z_s")
+        wl_grouped = held([P, PASS * PACK], BF16, "wl_grouped")
+
+        def by_four(grouped):
+            return grouped.rearrange("p (c i j) -> p c j i", i=PACK, j=PACK)
+
+        def rows_by_four(raw):
+            return raw.rearrange("p j (c i) -> p c j i", i=PACK)
+
+        def quantise(words, scales, c0, grouped):
+            cols = slice(c0, c0 + grouped.shape[1] // PACK)
+            nc.vector.quantize_mx(out=words[:, cols].bitcast(FP8X4), scales=scales[:, cols], in_=grouped)
+
+        def round_on_gpsimd(into, source):
+            nc.gpsimd.tensor_scalar(into, source, 1.0, 0.0, ALU.mult, ALU.add)
+
+        def prepare_wl(raw, c0, copy):
+            grouped = wl_grouped[:, c0 * PACK : (c0 + raw.shape[2]) * PACK]
+            copy(by_four(grouped), rows_by_four(raw[:]))
+            quantise(wl_w, wl_s, c0, grouped)
+
+        def round_wl_dealt(grouped):
+            for t in range(PACK):
+                nc.scalar.copy(
+                    grouped[:, t * PASS : (t + 1) * PASS].rearrange("p (q h i j) -> p q h j i", h=2, i=PACK, j=PACK),
+                    wl_raw_dealt[:].rearrange("p j (q t h i) -> p t q h j i", t=PACK, h=2, i=PACK)[:, t],
                 )
 
-        def quantise_wl(b, t0, count, grouped):
-            nc.scalar.copy(
-                grouped.rearrange("p (t m j) -> p t m j", t=count, j=PACK),
-                wl_raw[b][:].rearrange("p j (m t) -> p t m j", t=PACK)[:, t0 : t0 + count],
+        def deal_columns(engine, into, source):
+            run = source.shape[1] * RUN // PASS
+            engine.tensor_copy(
+                into.rearrange("p (t q s) -> p t q s", t=PACK, s=run), source.rearrange("p (q t s) -> p t q s", t=PACK, s=run)
             )
-            cols = slice(t0 * P, (t0 + count) * P)
-            nc.vector.quantize_mx(out=wl_w[b][:, cols].bitcast(FP8X4), scales=wl_s[b][:, cols], in_=grouped)
 
-        def quantise_wd(b, grouped):
-            nc.scalar.copy(
-                grouped.rearrange("p (c i t) -> p c t i", i=PACK, t=PACK),
-                wd_raw[b][:].rearrange("p t (c i) -> p c t i", i=PACK),
-            )
-            nc.vector.quantize_mx(out=wd_w[b][:].bitcast(FP8X4), scales=wd_s[b][:], in_=grouped)
+        nc.vector.tensor_copy(v_s[:], tab_s[:].indirect(lists["offs"][:]))
+        v_w = [held([P, BANK], U32, "v_w%d" % a) for a in range(2)]
+        nc.vector.tensor_copy(v_w[0][:], tab_w[:].indirect(offsets("offs", 0, BANK)))
+        prepare_wl(wl_raw0, 0, nc.scalar.copy)
+        nc.vector.tensor_copy(v_w[1][:], tab_w[:].indirect(offsets("offs", BANK, BANK)))
+        wh_sd = held([P, PASS], U8, "wh_sd")
+        wg_sd = held([P, PASS], U8, "wg_sd")
+        wh_d = held([P, PASS], I32, "wh_d")
+        wg_d = held([P, PASS // 2], I32, "wg_d")
+        deal_columns(nc.gpsimd, wh_sd[:].bitcast(I32), wh_s[:, PASS:H].bitcast(I32))
+        deal_columns(nc.gpsimd, wg_sd[:].bitcast(I32), wg_s[:, PASS:H].bitcast(I32))
 
-        high_sb = held([P, S], F32, "high_sb")
-        diff_sb = held([P, S], F32, "diff_sb")
-        step_t = [held([P, S], F32, "step_t%d" % s) for s in range(2)]
-        low_t = [held([P, S], F32, "low_t%d" % s) for s in range(2)]
-        gate_t = [held([P, S], F32, "gate_t%d" % s) for s in range(2)]
-        h_sb = [held([P, S], F32, "h_sb%d" % s) for s in range(2)]
-        early = [held([P, PACK, M_OUT], F32, "early0"), held([P, 2, M_OUT], F32, "early1")]
-        halves = [slice(a * BANK, (a + 1) * BANK) for a in range(HALVES)]
-        z_w = [held([P, M_OUT], U32, "z_w%d" % b) for b in range(PASSES)]
-        z_s = [held([P, M_OUT], U8, "z_s%d" % b) for b in range(PASSES)]
+        def weights(i):
+            cols = slice(P * i, P * (i + 1))
+            if i < PACK:
+                wh_t, wg_t, x = (wh_a, wg_a, i) if i < 2 else (wh_b, wg_b, i - 2)
+                high_scales, gate_scales = wh_s[:, cols], wg_s[:, cols]
+            else:
+                wh_t, wg_t, x = wh_d, wg_d, i - PACK
+                high_scales, gate_scales = wh_sd[:, P * x : P * (x + 1)], wg_sd[:, P * x : P * (x + 1)]
+            return {
+                "gate": (wg_t[:, x * P // 2 : (x + 1) * P // 2].bitcast(U8).bitcast(FP4X4), gate_scales),
+                "low": (wl_w[:, cols].bitcast(FP8X4), wl_s[:, cols]),
+                "high": (wh_t[:, x * P : (x + 1) * P].bitcast(FP8X4), high_scales),
+            }
 
-        def blocks():
-            return [slice(x, x + P) for x in range(0, BANK, P)]
+        def order(i):
+            return (0, 1) if i % 2 == 0 else (1, 0)
+
+        high = held([P, S], F32, "high")
+        low = held([P, S], F32, "low")
+        sig = held([P, S], F32, "sig")
+        step = [held([P, S], F32, "step%d" % s) for s in range(STEP_BUFS)]
+        tail = held([P, 2, S], F32, "tail")
+        weighted = [held([P, S], F32, "weighted0")[:], tail[:, 0, :]]
+        wd_w = {1: held([P, N], U32, "wd_w1")[:]}
+        shared = held([P, 2 * S + BANK], F32, "shared")
+        bearers = [shared[:, 0:S], shared[:, S + BANK : 2 * S + BANK]]
+        h_late = shared[:, S : S + BANK]
+        h_early = held([P, BANK], F32, "h_early")
+        diff = held([P, (LAST - 1) * M_OUT], F32, "diff")
+        dealt = held([P, PACK * M_OUT], F32, "dealt")
+
+        def first_tile():
+            w = weights(0)
+            low0, sig0, h0 = weighted[1], tail[:, 1, :], step[0]
+            for a in range(2):
+                for bank, name in ((gate_bank, "gate"), (first_bank, "low"), (high_bank, "high")):
+                    nc.tensor.matmul_mx(
+                        bank[a][:], lhsT=w[name][0], lhsT_scale=w[name][1],
+                        rhs=v_w[a][:].bitcast(FP8X4), rhs_scale=v_s[:, halves[a]], start=True, stop=True,
+                    )
+                nc.scalar.activation(sig0[:, halves[a]], gate_bank[a][:], ACT.Sigmoid)
+                nc.scalar.copy(low0[:, halves[a]], first_bank[a][:])
+            for a in range(2):
+                nc.vector.tensor_tensor(h0[:, halves[a]], high_bank[a][:], low0[:, halves[a]], ALU.subtract)
+                nc.vector.tensor_tensor(h0[:, halves[a]], h0[:, halves[a]], sig0[:, halves[a]], ALU.mult)
+                nc.vector.tensor_tensor(h0[:, halves[a]], h0[:, halves[a]], first_bank[a][:], ALU.add)
+                nc.vector.tensor_tensor(weighted[0][:, halves[a]], h0[:, halves[a]], wgs_natural[:, halves[a]], ALU.mult)
+
+        def products(i):
+            w = weights(i)
+            for bank, name in ((high_bank, "high"), (sum_bank, "low"), (gate_bank, "gate")):
+                for a in order(i):
+                    for blk in blocks:
+                        nc.tensor.matmul_mx(
+                            bank[a][:, blk], lhsT=v_w[a][:, blk].bitcast(FP8X4),
+                            lhsT_scale=v_s[:, a * BANK + blk.start : a * BANK + blk.stop],
+                            rhs=w[name][0], rhs_scale=w[name][1], start=True, stop=True,
+                        )
+            for a in order(i):
+                nc.scalar.copy(high[:, halves[a]], high_bank[a][:])
+            for a in order(i):
+                nc.scalar.copy(low[:, halves[a]], sum_bank[a][:])
+            for a in order(i):
+                nc.scalar.activation(sig[:, halves[a]], gate_bank[a][:], ACT.Sigmoid)
 
         def add_transposed(bank, source, opens):
-            for blk in blocks():
+            for blk in blocks:
                 nc.tensor.matmul(
                     bank[:, blk], source[:, blk], ident[:], is_transpose=True,
                     start=(opens and blk.start == 0), stop=(not opens and blk.stop == BANK),
                 )
 
-        def operands(i):
-            b, t = divmod(i, PACK)
-            cols = slice(t * P, (t + 1) * P)
-            return (
-                (high_bank, wh_p[b][:, cols].bitcast(FP8X4), ws_p[b][WH_ROW:P, cols]),
-                (low_bank, wl_w[b][:, cols].bitcast(FP8X4), wl_s[b][:, cols]),
-                (gate_bank, wg_p[b][:, 2 * t * P : 2 * (t + 1) * P].bitcast(FP4X4), ws_p[b][:, cols]),
-            )
+        def interpolate(i):
+            d0 = BANK if i % 2 == 0 else S
+            span = shared[:, d0 : d0 + S]
+            nc.gpsimd.tensor_tensor(span, high[:], low[:], ALU.subtract)
+            for a in order(i):
+                add_transposed(sum_bank[a], low[:, halves[a]], True)
+            for a, staged in zip(order(i), (h_early[:], h_late)):
+                nc.gpsimd.tensor_tensor(step[i % STEP_BUFS][:, halves[a]], span[:, halves[a]], sig[:, halves[a]], ALU.mult)
+                add_transposed(sum_bank[a], step[i % STEP_BUFS][:, halves[a]], False)
+            for a, staged in zip(order(i), (h_early[:], h_late)):
+                nc.scalar.copy(staged, sum_bank[a][:])
+            for a, staged in zip(order(i), (h_early[:], h_late)):
+                nc.gpsimd.tensor_tensor(weighted[i % 2][:, halves[a]], staged, wgs_rows[i][:, halves[a]], ALU.mult)
 
-        def first_tile():
-            for a in range(HALVES):
-                for bank, words, scales in operands(0):
-                    nc.tensor.matmul_mx(
-                        bank[a][:], lhsT=words, lhsT_scale=scales,
-                        rhs=v_w[a][:].bitcast(FP8X4), rhs_scale=v_s[a][:], start=True, stop=True,
-                    )
-            for a in range(HALVES):
-                nc.scalar.copy(low_t[0][:, halves[a]], low_bank[a][:])
-            for a in range(HALVES):
-                nc.scalar.activation(gate_t[0][:, halves[a]], gate_bank[a][:], ACT.Sigmoid)
-            for a in range(HALVES):
-                nc.vector.tensor_tensor(step_t[0][:, halves[a]], high_bank[a][:], low_t[0][:, halves[a]], ALU.subtract)
-            for other, op in ((gate_t[0], ALU.mult), (low_t[0], ALU.add)):
-                for a in range(HALVES):
-                    nc.vector.tensor_tensor(step_t[0][:, halves[a]], step_t[0][:, halves[a]], other[:, halves[a]], op)
-            for a in range(HALVES):
-                nc.vector.tensor_tensor(h_sb[0][:, halves[a]], step_t[0][:, halves[a]], wgs_t[0][:, halves[a]], ALU.mult)
-
-        def products(i):
-            for a in range(HALVES):
-                for bank, words, scales in operands(i):
-                    for blk in blocks():
-                        nc.tensor.matmul_mx(
-                            bank[a][:, blk], lhsT=v_w[a][:, blk].bitcast(FP8X4), lhsT_scale=v_s[a][:, blk],
-                            rhs=words, rhs_scale=scales, start=True, stop=True,
-                        )
-            for a in range(HALVES):
-                nc.scalar.copy(high_sb[:, halves[a]], high_bank[a][:])
-                nc.scalar.copy(low_t[i % 2][:, halves[a]], low_bank[a][:])
-            nc.gpsimd.tensor_tensor(diff_sb[:], high_sb[:], low_t[i % 2][:], ALU.subtract)
-            for a in range(HALVES):
-                nc.scalar.activation(gate_t[i % 2][:, halves[a]], gate_bank[a][:], ACT.Sigmoid)
-
-        def interpolate(i, staged, width):
-            for a in range(HALVES):
-                add_transposed(gate_bank[a], low_t[i % 2][:, halves[a]], True)
-            for a in range(HALVES):
-                nc.gpsimd.tensor_tensor(
-                    step_t[i % 2][:, halves[a]], diff_sb[:, halves[a]], gate_t[i % 2][:, halves[a]], ALU.mult
-                )
-            for a in range(HALVES):
-                add_transposed(gate_bank[a], step_t[i % 2][:, halves[a]], False)
-                nc.scalar.copy(staged[:, halves[a]], gate_bank[a][:])
-            for j0 in range(0, S, width):
-                cols = slice(j0, j0 + width)
-                nc.gpsimd.tensor_tensor(h_sb[i % 2][:, cols], staged[:, cols], wgs_t[i % PACK][:, cols], ALU.mult)
-
-        def scatter(i, width):
-            for j0 in range(0, S, width):
-                nc.vector.tensor_copy(
-                    pages[i][:].indirect(offsets("offs2", j0, width)), h_sb[i % 2][:, j0 : j0 + width]
-                )
+        def scatter(i):
+            nc.vector.tensor_copy(pages[i][:].indirect(lists["offs2"][:]), weighted[i % 2])
 
         def fetch_bearers(i, m0, into):
             nc.vector.tensor_copy(into, pages[i][:].indirect(offsets("offs4", m0, into.shape[1])))
 
-        def fetch_limbs(i, m0, bearers, into):
-            nc.vector.tensor_tensor(into, pages[i][:].indirect(offsets("offs3", m0, into.shape[1])), bearers, ALU.subtract)
+        def fetch_limbs(i, m0, minus, into):
+            nc.vector.tensor_tensor(into, pages[i][:].indirect(offsets("offs3", m0, into.shape[1])), minus, ALU.subtract)
 
         def round_z(source, grouped, slots):
-            nc.scalar.activation(
-                grouped.rearrange("p (c i t) -> p c t i", i=PACK, t=PACK)[:, :, slots, :],
-                source.rearrange("p t (c i) -> p c t i", i=PACK), ACT.Abs,
-            )
+            nc.scalar.activation(by_four(grouped)[:, :, slots, :], rows_by_four(source), ACT.Abs)
 
-        def quantise_z(b, m0, grouped):
-            cols = slice(m0, m0 + grouped.shape[1] // PACK)
-            nc.vector.quantize_mx(out=z_w[b][:, cols].bitcast(FP8X4), scales=z_s[b][:, cols], in_=grouped)
+        dealt_rows_z = dealt[:].rearrange("p (t m) -> p t m", t=PACK)
+        diff_rows = diff[:].rearrange("p (t m) -> p t m", t=LAST - 1)
+
+        def stage(n):
+            spent = step[n % STEP_BUFS][:].bitcast(BF16)
+            if n == 1:
+                round_wl_dealt(spent)
+            if n in (3, 4):
+                nc.scalar.copy(by_four(spent), rows_by_four(wd_raw[4 - n][:]))
+            if n in (5, 6):
+                round_z(dealt_rows_z[:, :, halves[n - 5]], spent, slice(0, PACK))
+
+        def quantise_staged(n):
+            spent = step[n % STEP_BUFS][:].bitcast(BF16)
+            if n == 1:
+                quantise(wl_w, wl_s, PASS, spent)
+            if n == 3:
+                quantise(wd_w[1], wd_s[1], 0, spent)
+            if n in (5, 6):
+                quantise(z_w, z_s, (n - 5) * BANK, spent)
 
         def score_pass(b, m0, width):
             per_bank = BANK // width
             for nb in range(N // P):
                 part, side = divmod(nb, per_bank)
                 cols = slice(nb * P, (nb + 1) * P)
+                moving = slice(b * M_OUT + m0, b * M_OUT + m0 + width)
                 nc.tensor.matmul_mx(
                     banks[m0 // P + part][:, side * width : (side + 1) * width],
                     lhsT=wd_w[b][:, cols].bitcast(FP8X4), lhsT_scale=wd_s[b][:, cols],
-                    rhs=z_w[b][:, m0 : m0 + width].bitcast(FP8X4), rhs_scale=z_s[b][:, m0 : m0 + width],
-                    start=(b == 0 and side == 0), stop=(b == PASSES - 1 and side == per_bank - 1),
+                    rhs=z_w[:, moving].bitcast(FP8X4), rhs_scale=z_s[:, moving],
+                    start=(b == 0 and side == 0), stop=(b == 1 and side == per_bank - 1),
                 )
 
-        def store(m0, width, part, copy, staged):
+        prepare_wl(wl_raw12, P, round_on_gpsimd)
+        first_tile()
+        products(1)
+        prepare_wl(wl_raw3, 3 * P, nc.scalar.copy)
+
+        high_bf16 = high[:].bitcast(BF16)
+        late_bf16 = h_late.bitcast(BF16)
+        late = {
+            0: high_bf16[:, 0:S], 256: high_bf16[:, S : 2 * S], 512: h_early[:].bitcast(BF16),
+            768: late_bf16[:, 0:BANK], 896: late_bf16[:, BANK:S],
+        }
+
+        for i in range(LAST):
+            interpolate(i + 1)
+            scatter(i)
+            fetch_bearers(i, 0, bearers[i % 2])
+            if i < LAST - 1:
+                fetch_limbs(i, 0, bearers[i % 2], diff_rows[:, i, :])
+            if i < PACK:
+                nc.sync.dma_start(out=dealt_rows_z[QUAD * i : QUAD * (i + 1)], in_=diff_rows[:, i, :])
+                load_later(i)
+            quantise_staged(i)
+            if i == 0:
+                deal_columns(nc.vector, wh_d[:], wh_c[:])
+                deal_columns(nc.vector, wg_d[:], wg_c[:])
+            if i + 2 <= LAST:
+                products(i + 2)
+            stage(i + 1)
+        for m0, width in PIECES:
+            round_z(diff_rows[:, PACK : PACK + 2, m0 : m0 + width], late[m0], slice(0, 2))
+        wd_w[0] = held([P, N], U32, "step%d" % (LAST % STEP_BUFS))[:]
+        quantise(wd_w[0], wd_s[0], 0, step[4 % STEP_BUFS][:].bitcast(BF16))
+        scatter(LAST)
+        for m0, width in PIECES:
+            score_pass(0, m0, width)
+
+        spare = wl_raw_dealt[:].rearrange("p j c -> p (j c)")
+        staged = [spare[:, x * BANK : (x + 1) * BANK] for x in range(4)]
+        staged = staged + [dealt[:, 2 * M_OUT + x * BANK : 2 * M_OUT + (x + 1) * BANK] for x in range(4)]
+
+        def store(m0, width, copies):
             per_bank = BANK // width
             out_rows = out.rearrange("(a s p) m -> a p s m", s=per_bank, p=P)
-            copy(staged, banks[m0 // P + part][:])
-            nc.sync.dma_start(
-                out=out_rows[part][:, :, m0 : m0 + width], in_=staged.rearrange("p (s m) -> p s m", s=per_bank)
-            )
+            for part in range(width // P):
+                bank = m0 // P + part
+                copies[part](staged[bank], banks[bank][:])
+                nc.sync.dma_start(
+                    out=out_rows[part][:, :, m0 : m0 + width],
+                    in_=staged[bank].rearrange("p (s m) -> p s m", s=per_bank),
+                )
 
-        first_grouped = held([P, PASS * PACK], BF16, "first_grouped")
-        for t in range(2):
-            quantise_wl(0, t, 1, first_grouped[:, t * PASS : (t + 1) * PASS])
-        order_packed_weights(0)
-        order_packed_weights(1)
-        first_tile()
-        for t in range(2, PACK):
-            quantise_wl(0, t, 1, first_grouped[:, t * PASS : (t + 1) * PASS])
-        last = TILES - 1
-        products(1)
-        for i in range(last):
-            scatter(i, S)
-            slot = early[i // PACK][:, i % PACK, :] if i < last - 1 else high_sb[:]
-            interpolate(i + 1, slot, S if i < last - 1 else BANK)
-            spent = step_t[(i + 1) % 2][:].bitcast(BF16)
-            if i in (0, 1):
-                quantise_wl(1, 2 * i, 2, spent[:, 2 * PASS : 4 * PASS])
-            if i == 1:
-                wd_raw.append(load_f32_rows(wd[PASS : 2 * PASS, :]))
-            if i in (2, 3):
-                quantise_wd(i - 2, spent)
-            if i in (4, 5):
-                m0 = (i - 4) * BANK
-                round_z(early[0][:, :, m0 : m0 + BANK], spent, slice(0, PACK))
-                quantise_z(0, m0, spent)
-            if i + 2 <= last:
-                products(i + 2)
-            if i < last - 1:
-                for a in range(HALVES):
-                    fetch_bearers(i, a * BANK, step_t[i % 2][:, halves[a]])
-                for a in range(HALVES):
-                    fetch_limbs(i, a * BANK, step_t[i % 2][:, halves[a]], slot[:, halves[a]])
-            if i + PACK <= last:
-                load_page(i + PACK)
-        scatter(last, S)
-        late = {m0: held([P, w * PACK], BF16, "late%d" % m0) for m0, w in CHUNKS}
-        for m0, width in CHUNKS:
-            score_pass(0, m0, width)
-            round_z(early[1][:, :, m0 : m0 + width], late[m0][:], slice(0, 2))
-
-        wide, narrow = CHUNKS[:3], CHUNKS[3:]
-        tail = {m0: held([P, 2, w], F32, "tail%d" % m0)[:] for m0, w in wide}
-        reused = late[wide[-1][0]][:].bitcast(F32)
-        for n, (m0, width) in enumerate(narrow):
-            tail[m0] = reused[:, 2 * n * width : 2 * (n + 1) * width].rearrange("p (s m) -> p s m", s=2)
-        staged = [held([P, BANK], F32, "staged%d" % n) for n in range(7)]
-
-        def finish(m0, width):
-            round_z(tail[m0], late[m0][:], slice(2, PACK))
-            quantise_z(1, m0, late[m0][:])
+        def finish(m0, width, copies):
+            quantise(z_w, z_s, M_OUT + m0, late[m0])
             score_pass(1, m0, width)
+            store(m0, width, copies)
 
-        def fetch_all_bearers(m0, into):
-            for s, i in enumerate((last - 1, last)):
-                fetch_bearers(i, m0, into[s])
-
-        def fetch_all_limbs(m0, width, bearers):
-            x = m0 % CHUNK
-            for s, i in enumerate((last - 1, last)):
-                fetch_limbs(i, m0, bearers[s][:, x : x + width], tail[m0][:, s, :])
-
-        for c in range(M_OUT // CHUNK):
-            m0 = c * CHUNK
-            if c < 2:
-                bearers = [step_t[0][:, s * BANK + m0 : s * BANK + m0 + CHUNK] for s in range(2)]
-            else:
-                finish(*CHUNKS[c - 2])
-                words = late[m0 - 2 * CHUNK][:].bitcast(F32)
-                bearers = [words[:, s * CHUNK : (s + 1) * CHUNK] for s in range(2)]
-            fetch_all_bearers(m0, bearers)
-            if c < len(wide):
-                fetch_all_limbs(m0, CHUNK, bearers)
-            if c >= 2:
-                for part in range(2):
-                    store(*CHUNKS[c - 2], part, nc.scalar.copy, staged[2 * (c - 2) + part][:])
-        finish(*wide[-1])
-        for m0, width in narrow:
-            fetch_all_limbs(m0, width, bearers)
-        for m0, width in narrow:
-            finish(m0, width)
-        store(*wide[-1], 0, nc.scalar.copy, reused)
-        store(*wide[-1], 1, nc.vector.tensor_copy, staged[4][:])
-        store(*narrow[0], 0, nc.scalar.copy, staged[5][:])
-        store(*narrow[1], 0, nc.vector.tensor_copy, staged[6][:])
+        last_bearers = {}
+        for x, (m0, width) in enumerate(PIECES):
+            c0 = m0 - m0 % CHUNK
+            if m0 == c0:
+                if c0 < 2 * CHUNK:
+                    last_bearers[c0] = bearers[LAST % 2][:, c0 : c0 + CHUNK]
+                else:
+                    last_bearers[c0] = late[c0 - 2 * CHUNK].bitcast(F32)[:, 0:CHUNK]
+                fetch_bearers(LAST, c0, last_bearers[c0])
+            fetch_limbs(LAST - 1, m0, bearers[(LAST - 1) % 2][:, m0 : m0 + width], tail[:, 0, m0 : m0 + width])
+            fetch_limbs(LAST, m0, last_bearers[c0][:, m0 - c0 : m0 - c0 + width], tail[:, 1, m0 : m0 + width])
+            round_z(tail[:, :, m0 : m0 + width], late[m0], slice(2, PACK))
+            if x > 0:
+                finish(*PIECES[x - 1], (nc.scalar.copy, nc.scalar.copy if x < 3 else nc.vector.tensor_copy))
+        finish(*PIECES[-1], (nc.vector.tensor_copy,))

@@ -112,10 +112,10 @@ def tile_list_limb_cut_advice_kernel(
         wg_b = load_words("wg_b", wg_i32[:, P : 2 * P])
         nc.sync.dma_start(lists["offs4"][:], offs4)
         nc.sync.dma_start(lists["offs3"][:], offs3)
-        wl_raw_dealt = load_rows_of_four("wl_raw_dealt", wl[:, PASS:H])
-        load_page(1)
         wh_c = load_words("wh_c", wh_i32[:, PASS:H])
         wg_c = load_words("wg_c", wg_i32[:, 2 * P : PASS])
+        load_page(1)
+        wl_raw_dealt = load_rows_of_four("wl_raw_dealt", wl[:, PASS:H])
         load_page(2)
         load_page(3)
         wgs_rows = [wgs_natural] * PACK
@@ -127,7 +127,7 @@ def tile_list_limb_cut_advice_kernel(
                 for t in range(PACK):
                     nc.sync.dma_start(out=wd_raw[1][:, t, :], in_=dealt_rows(wd[PASS:H, :], t))
             if i == 1:
-                wd_raw[0] = load_rows_of_four("wd_raw0", wd[0:PASS, :])
+                wd_raw[0] = load_rows_of_four("tab_w", wd[0:PASS, :])
             wgs_rows.append(load_wgs_dealt(i))
             load_page(i + PACK)
 
@@ -200,18 +200,20 @@ def tile_list_limb_cut_advice_kernel(
             }
 
         def order(i):
-            return (0, 1) if i % 2 == 0 else (1, 0)
+            return (0, 1) if i % 2 == 1 else (1, 0)
 
         high = held([P, S], F32, "high")
         low = held([P, S], F32, "low")
         sig = held([P, S], F32, "sig")
-        step = [held([P, S], F32, "step%d" % s) for s in range(STEP_BUFS)]
+        wide_step = held([P, 2 * S], F32, "wide_step")
+        step = [held([P, S], F32, "step%d" % s)[:] if s != 2 else wide_step[:, BANK : BANK + S] for s in range(STEP_BUFS)]
         tail = held([P, 2, S], F32, "tail")
         weighted = [held([P, S], F32, "weighted0")[:], tail[:, 0, :]]
         wd_w = {1: held([P, N], U32, "wd_w1")[:]}
-        shared = held([P, 2 * S + BANK], F32, "shared")
-        bearers = [shared[:, 0:S], shared[:, S + BANK : 2 * S + BANK]]
-        h_late = shared[:, S : S + BANK]
+        shared = held([P, 2 * S + CHUNK], F32, "shared")
+        bearers = [shared[:, 0:S], shared[:, S + CHUNK : 2 * S + CHUNK]]
+        h_late = shared[:, S : S + CHUNK]
+        h_last = held([P, CHUNK], F32, "h_last")
         h_early = held([P, BANK], F32, "h_early")
         diff = held([P, (LAST - 1) * M_OUT], F32, "diff")
         dealt = held([P, PACK * M_OUT], F32, "dealt")
@@ -258,18 +260,22 @@ def tile_list_limb_cut_advice_kernel(
                 )
 
         def interpolate(i):
-            d0 = BANK if i % 2 == 0 else S
+            d0 = CHUNK if i % 2 == 1 else S
             span = shared[:, d0 : d0 + S]
             nc.gpsimd.tensor_tensor(span, high[:], low[:], ALU.subtract)
             for a in order(i):
                 add_transposed(sum_bank[a], low[:, halves[a]], True)
-            for a, staged in zip(order(i), (h_early[:], h_late)):
+            for a in order(i):
                 nc.gpsimd.tensor_tensor(step[i % STEP_BUFS][:, halves[a]], span[:, halves[a]], sig[:, halves[a]], ALU.mult)
                 add_transposed(sum_bank[a], step[i % STEP_BUFS][:, halves[a]], False)
-            for a, staged in zip(order(i), (h_early[:], h_late)):
-                nc.scalar.copy(staged, sum_bank[a][:])
-            for a, staged in zip(order(i), (h_early[:], h_late)):
-                nc.gpsimd.tensor_tensor(weighted[i % 2][:, halves[a]], staged, wgs_rows[i][:, halves[a]], ALU.mult)
+            early, behind = order(i)
+            closing = diff_rows[:, i - 1, 0:CHUNK] if i < LAST else h_last[:]
+            parts = ((early, 0, h_early[:]), (behind, 0, h_late), (behind, CHUNK, closing))
+            for a, x, staged in parts:
+                nc.scalar.copy(staged, sum_bank[a][:, x : x + staged.shape[1]])
+            for a, x, staged in parts:
+                cols = slice(a * BANK + x, a * BANK + x + staged.shape[1])
+                nc.gpsimd.tensor_tensor(weighted[i % 2][:, cols], staged, wgs_rows[i][:, cols], ALU.mult)
 
         def scatter(i):
             nc.vector.tensor_copy(pages[i][:].indirect(lists["offs2"][:]), weighted[i % 2])
@@ -287,22 +293,23 @@ def tile_list_limb_cut_advice_kernel(
         diff_rows = diff[:].rearrange("p (t m) -> p t m", t=LAST - 1)
 
         def stage(n):
-            spent = step[n % STEP_BUFS][:].bitcast(BF16)
+            spent = step[n % STEP_BUFS].bitcast(BF16)
             if n == 1:
                 round_wl_dealt(spent)
             if n in (3, 4):
                 nc.scalar.copy(by_four(spent), rows_by_four(wd_raw[4 - n][:]))
-            if n in (5, 6):
-                round_z(dealt_rows_z[:, :, halves[n - 5]], spent, slice(0, PACK))
+            if n == 6:
+                for a in range(2):
+                    round_z(dealt_rows_z[:, :, halves[a]], wide_step[:, a * S : (a + 1) * S].bitcast(BF16), slice(0, PACK))
 
         def quantise_staged(n):
-            spent = step[n % STEP_BUFS][:].bitcast(BF16)
+            spent = step[n % STEP_BUFS].bitcast(BF16)
             if n == 1:
                 quantise(wl_w, wl_s, PASS, spent)
             if n == 3:
                 quantise(wd_w[1], wd_s[1], 0, spent)
-            if n in (5, 6):
-                quantise(z_w, z_s, (n - 5) * BANK, spent)
+            if n == 6:
+                quantise(z_w, z_s, 0, wide_step[:].bitcast(BF16))
 
         def score_pass(b, m0, width):
             per_bank = BANK // width
@@ -322,33 +329,33 @@ def tile_list_limb_cut_advice_kernel(
         products(1)
         prepare_wl(wl_raw3, 3 * P, nc.scalar.copy)
 
-        high_bf16 = high[:].bitcast(BF16)
-        late_bf16 = h_late.bitcast(BF16)
-        late = {
-            0: high_bf16[:, 0:S], 256: high_bf16[:, S : 2 * S], 512: h_early[:].bitcast(BF16),
-            768: late_bf16[:, 0:BANK], 896: late_bf16[:, BANK:S],
-        }
-
         for i in range(LAST):
             interpolate(i + 1)
             scatter(i)
-            fetch_bearers(i, 0, bearers[i % 2])
+            if i > 0:
+                fetch_limbs(i - 1, 0, bearers[(i - 1) % 2], diff_rows[:, i - 1, :])
+            if 0 < i <= PACK:
+                nc.sync.dma_start(out=dealt_rows_z[QUAD * (i - 1) : QUAD * i], in_=diff_rows[:, i - 1, :])
+                load_later(i - 1)
             if i < LAST - 1:
-                fetch_limbs(i, 0, bearers[i % 2], diff_rows[:, i, :])
-            if i < PACK:
-                nc.sync.dma_start(out=dealt_rows_z[QUAD * i : QUAD * (i + 1)], in_=diff_rows[:, i, :])
-                load_later(i)
-            quantise_staged(i)
+                quantise_staged(i)
             if i == 0:
                 deal_columns(nc.vector, wh_d[:], wh_c[:])
                 deal_columns(nc.vector, wg_d[:], wg_c[:])
+            fetch_bearers(i, 0, bearers[i % 2])
             if i + 2 <= LAST:
                 products(i + 2)
             stage(i + 1)
+        quantise_staged(LAST - 1)
+        last_wgs = wgs_rows[LAST][:].bitcast(BF16)
+        late = {
+            0: last_wgs[:, 0:S], 256: last_wgs[:, S : 2 * S], 512: h_early[:].bitcast(BF16),
+            768: h_late.bitcast(BF16), 896: h_last[:].bitcast(BF16),
+        }
         for m0, width in PIECES:
             round_z(diff_rows[:, PACK : PACK + 2, m0 : m0 + width], late[m0], slice(0, 2))
         wd_w[0] = held([P, N], U32, "step%d" % (LAST % STEP_BUFS))[:]
-        quantise(wd_w[0], wd_s[0], 0, step[4 % STEP_BUFS][:].bitcast(BF16))
+        quantise(wd_w[0], wd_s[0], 0, step[4 % STEP_BUFS].bitcast(BF16))
         scatter(LAST)
         for m0, width in PIECES:
             score_pass(0, m0, width)

@@ -46,7 +46,7 @@ def tile_list_limb_cut_advice_kernel(
             return keep.tile(shape, dtype, name=name, align_bytes=64)
 
         banks = [psum.tile([P, BANK], F32, name="bank%d" % i) for i in range(8)]
-        high_bank, gate_bank, first_bank, sum_bank = banks[0:2], banks[2:4], banks[4:6], banks[6:8]
+        high_bank, gate_bank, low_bank, sum_bank = banks[0:2], banks[2:4], banks[4:6], banks[6:8]
         halves = [slice(0, BANK), slice(BANK, 2 * BANK)]
         blocks = [slice(x, x + P) for x in range(0, BANK, P)]
 
@@ -102,34 +102,33 @@ def tile_list_limb_cut_advice_kernel(
         wg_a = load_words("wg_a", wg_i32[:, 0:P])
         wh_a = load_words("wh_a", wh_i32[:, 0 : 2 * P])
         wh_s = load_scale_rows("wh_s", wh_scales, (nc.gpsimd, nc.sync))
-        wl_raw12 = load_rows_of_four("wl_raw12", wl[:, P : 3 * P])
+        wl_raw123 = load_rows_of_four("wl_raw123", wl[:, P:PASS])
         wgs_natural = held([P, S], F32, "wgs_natural")
         nc.sync.dma_start(out=wgs_natural[:], in_=wgs)
         load_page(0)
         nc.sync.dma_start(lists["offs2"][:], offs2)
-        wl_raw3 = load_rows_of_four("wl_raw3", wl[:, 3 * P : PASS])
         wh_b = load_words("wh_b", wh_i32[:, 2 * P : PASS])
         wg_b = load_words("wg_b", wg_i32[:, P : 2 * P])
         nc.sync.dma_start(lists["offs4"][:], offs4)
         nc.sync.dma_start(lists["offs3"][:], offs3)
         wh_c = load_words("wh_c", wh_i32[:, PASS:H])
         wg_c = load_words("wg_c", wg_i32[:, 2 * P : PASS])
-        load_page(1)
         wl_raw_dealt = load_rows_of_four("wl_raw_dealt", wl[:, PASS:H])
+        load_page(1)
         load_page(2)
         load_page(3)
         wgs_rows = [wgs_natural] * PACK
         wd_raw = {}
 
         def load_later(i):
+            wgs_rows.append(load_wgs_dealt(i))
+            load_page(i + PACK)
             if i == 0:
                 wd_raw[1] = held([P, PACK, N], F32, "wd_raw1")
                 for t in range(PACK):
                     nc.sync.dma_start(out=wd_raw[1][:, t, :], in_=dealt_rows(wd[PASS:H, :], t))
             if i == 1:
                 wd_raw[0] = load_rows_of_four("tab_w", wd[0:PASS, :])
-            wgs_rows.append(load_wgs_dealt(i))
-            load_page(i + PACK)
 
         ident = held([P, P], F32, "ident")
         make_identity(nc, ident[:])
@@ -157,7 +156,7 @@ def tile_list_limb_cut_advice_kernel(
 
         def prepare_wl(raw, c0, copy):
             grouped = wl_grouped[:, c0 * PACK : (c0 + raw.shape[2]) * PACK]
-            copy(by_four(grouped), rows_by_four(raw[:]))
+            copy(by_four(grouped), rows_by_four(raw))
             quantise(wl_w, wl_s, c0, grouped)
 
         def round_wl_dealt(grouped):
@@ -176,7 +175,7 @@ def tile_list_limb_cut_advice_kernel(
         nc.vector.tensor_copy(v_s[:], tab_s[:].indirect(lists["offs"][:]))
         v_w = [held([P, BANK], U32, "v_w%d" % a) for a in range(2)]
         nc.vector.tensor_copy(v_w[0][:], tab_w[:].indirect(offsets("offs", 0, BANK)))
-        prepare_wl(wl_raw0, 0, nc.scalar.copy)
+        prepare_wl(wl_raw0[:], 0, nc.scalar.copy)
         nc.vector.tensor_copy(v_w[1][:], tab_w[:].indirect(offsets("offs", BANK, BANK)))
         wh_sd = held([P, PASS], U8, "wh_sd")
         wg_sd = held([P, PASS], U8, "wg_sd")
@@ -199,22 +198,15 @@ def tile_list_limb_cut_advice_kernel(
                 "high": (wh_t[:, x * P : (x + 1) * P].bitcast(FP8X4), high_scales),
             }
 
-        def order(i):
-            return (0, 1) if i % 2 == 1 else (1, 0)
-
         high = held([P, S], F32, "high")
         low = held([P, S], F32, "low")
         sig = held([P, S], F32, "sig")
-        wide_step = held([P, 2 * S], F32, "wide_step")
-        step = [held([P, S], F32, "step%d" % s)[:] if s != 2 else wide_step[:, BANK : BANK + S] for s in range(STEP_BUFS)]
+        span = held([P, S], F32, "span")
+        step = [held([P, S if s != 2 else 2 * S], F32, "step%d" % s) for s in range(STEP_BUFS)]
         tail = held([P, 2, S], F32, "tail")
         weighted = [held([P, S], F32, "weighted0")[:], tail[:, 0, :]]
         wd_w = {1: held([P, N], U32, "wd_w1")[:]}
-        shared = held([P, 2 * S + CHUNK], F32, "shared")
-        bearers = [shared[:, 0:S], shared[:, S + CHUNK : 2 * S + CHUNK]]
-        h_late = shared[:, S : S + CHUNK]
-        h_last = held([P, CHUNK], F32, "h_last")
-        h_early = held([P, BANK], F32, "h_early")
+        bearers = [held([P, S], F32, "bearers%d" % s)[:] for s in range(2)]
         diff = held([P, (LAST - 1) * M_OUT], F32, "diff")
         dealt = held([P, PACK * M_OUT], F32, "dealt")
 
@@ -222,35 +214,40 @@ def tile_list_limb_cut_advice_kernel(
             w = weights(0)
             low0, sig0, h0 = weighted[1], tail[:, 1, :], step[0]
             for a in range(2):
-                for bank, name in ((gate_bank, "gate"), (first_bank, "low"), (high_bank, "high")):
+                for bank, name in ((gate_bank, "gate"), (sum_bank, "low"), (high_bank, "high")):
                     nc.tensor.matmul_mx(
                         bank[a][:], lhsT=w[name][0], lhsT_scale=w[name][1],
                         rhs=v_w[a][:].bitcast(FP8X4), rhs_scale=v_s[:, halves[a]], start=True, stop=True,
                     )
                 nc.scalar.activation(sig0[:, halves[a]], gate_bank[a][:], ACT.Sigmoid)
-                nc.scalar.copy(low0[:, halves[a]], first_bank[a][:])
+                nc.scalar.copy(low0[:, halves[a]], sum_bank[a][:])
             for a in range(2):
                 nc.vector.tensor_tensor(h0[:, halves[a]], high_bank[a][:], low0[:, halves[a]], ALU.subtract)
                 nc.vector.tensor_tensor(h0[:, halves[a]], h0[:, halves[a]], sig0[:, halves[a]], ALU.mult)
-                nc.vector.tensor_tensor(h0[:, halves[a]], h0[:, halves[a]], first_bank[a][:], ALU.add)
+                nc.vector.tensor_tensor(h0[:, halves[a]], h0[:, halves[a]], sum_bank[a][:], ALU.add)
                 nc.vector.tensor_tensor(weighted[0][:, halves[a]], h0[:, halves[a]], wgs_natural[:, halves[a]], ALU.mult)
 
-        def products(i):
-            w = weights(i)
-            for bank, name in ((high_bank, "high"), (sum_bank, "low"), (gate_bank, "gate")):
-                for a in order(i):
-                    for blk in blocks:
-                        nc.tensor.matmul_mx(
-                            bank[a][:, blk], lhsT=v_w[a][:, blk].bitcast(FP8X4),
-                            lhsT_scale=v_s[:, a * BANK + blk.start : a * BANK + blk.stop],
-                            rhs=w[name][0], rhs_scale=w[name][1], start=True, stop=True,
-                        )
-            for a in order(i):
-                nc.scalar.copy(high[:, halves[a]], high_bank[a][:])
-            for a in order(i):
-                nc.scalar.copy(low[:, halves[a]], sum_bank[a][:])
-            for a in order(i):
-                nc.scalar.activation(sig[:, halves[a]], gate_bank[a][:], ACT.Sigmoid)
+        def product(i, name, bank, empty, into):
+            words, scales = weights(i)[name]
+            for a in range(2):
+                for blk in blocks:
+                    nc.tensor.matmul_mx(
+                        bank[a][:, blk], lhsT=v_w[a][:, blk].bitcast(FP8X4),
+                        lhsT_scale=v_s[:, a * BANK + blk.start : a * BANK + blk.stop],
+                        rhs=words, rhs_scale=scales, start=True, stop=True,
+                    )
+            for a in range(2):
+                empty(into[:, halves[a]], bank[a][:])
+
+        def sigmoid(into, source):
+            nc.scalar.activation(into, source, ACT.Sigmoid)
+
+        def readings(i):
+            product(i, "high", high_bank, nc.scalar.copy, high)
+            product(i, "low", low_bank, nc.scalar.copy, low)
+
+        def gate(i):
+            product(i, "gate", gate_bank, sigmoid, sig)
 
         def add_transposed(bank, source, opens):
             for blk in blocks:
@@ -259,23 +256,29 @@ def tile_list_limb_cut_advice_kernel(
                     start=(opens and blk.start == 0), stop=(not opens and blk.stop == BANK),
                 )
 
-        def interpolate(i):
-            d0 = CHUNK if i % 2 == 1 else S
-            span = shared[:, d0 : d0 + S]
-            nc.gpsimd.tensor_tensor(span, high[:], low[:], ALU.subtract)
-            for a in order(i):
+        def difference():
+            nc.gpsimd.tensor_tensor(span[:], high[:], low[:], ALU.subtract)
+
+        def staged_h(i):
+            return (sig[:, halves[0]], diff_rows[:, i - 1, halves[1]] if i < LAST else span[:, halves[1]])
+
+        def open_sums():
+            for a in range(2):
                 add_transposed(sum_bank[a], low[:, halves[a]], True)
-            for a in order(i):
-                nc.gpsimd.tensor_tensor(step[i % STEP_BUFS][:, halves[a]], span[:, halves[a]], sig[:, halves[a]], ALU.mult)
-                add_transposed(sum_bank[a], step[i % STEP_BUFS][:, halves[a]], False)
-            early, behind = order(i)
-            closing = diff_rows[:, i - 1, 0:CHUNK] if i < LAST else h_last[:]
-            parts = ((early, 0, h_early[:]), (behind, 0, h_late), (behind, CHUNK, closing))
-            for a, x, staged in parts:
-                nc.scalar.copy(staged, sum_bank[a][:, x : x + staged.shape[1]])
-            for a, x, staged in parts:
-                cols = slice(a * BANK + x, a * BANK + x + staged.shape[1])
-                nc.gpsimd.tensor_tensor(weighted[i % 2][:, cols], staged, wgs_rows[i][:, cols], ALU.mult)
+
+        def interpolate(i):
+            ring_step = step[i % STEP_BUFS]
+            middle = (ring_step.shape[1] - BANK) // 2
+            steps = (bearers[(i + 1) % 2][:, 0:BANK], ring_step[:, middle : middle + BANK])
+            for a in range(2):
+                nc.gpsimd.tensor_tensor(steps[a], span[:, halves[a]], sig[:, halves[a]], ALU.mult)
+                add_transposed(sum_bank[a], steps[a], False)
+            for a in range(2):
+                nc.scalar.copy(staged_h(i)[a], sum_bank[a][:])
+
+        def weigh(i):
+            for a in range(2):
+                nc.gpsimd.tensor_tensor(weighted[i % 2][:, halves[a]], staged_h(i)[a], wgs_rows[i][:, halves[a]], ALU.mult)
 
         def scatter(i):
             nc.vector.tensor_copy(pages[i][:].indirect(lists["offs2"][:]), weighted[i % 2])
@@ -293,23 +296,21 @@ def tile_list_limb_cut_advice_kernel(
         diff_rows = diff[:].rearrange("p (t m) -> p t m", t=LAST - 1)
 
         def stage(n):
-            spent = step[n % STEP_BUFS].bitcast(BF16)
-            if n == 1:
-                round_wl_dealt(spent)
-            if n in (3, 4):
-                nc.scalar.copy(by_four(spent), rows_by_four(wd_raw[4 - n][:]))
+            spent = step[n % STEP_BUFS][:].bitcast(BF16)
+            if n in (4, 5):
+                nc.scalar.copy(by_four(spent), rows_by_four(wd_raw[5 - n][:]))
             if n == 6:
                 for a in range(2):
-                    round_z(dealt_rows_z[:, :, halves[a]], wide_step[:, a * S : (a + 1) * S].bitcast(BF16), slice(0, PACK))
+                    round_z(dealt_rows_z[:, :, halves[a]], spent[:, 2 * a * S : 2 * (a + 1) * S], slice(0, PACK))
 
         def quantise_staged(n):
-            spent = step[n % STEP_BUFS].bitcast(BF16)
-            if n == 1:
-                quantise(wl_w, wl_s, PASS, spent)
-            if n == 3:
+            spent = step[n % STEP_BUFS][:].bitcast(BF16)
+            if n == 0:
+                quantise(wl_w, wl_s, PASS, step[3][:].bitcast(BF16))
+            if n == 4:
                 quantise(wd_w[1], wd_s[1], 0, spent)
             if n == 6:
-                quantise(z_w, z_s, 0, wide_step[:].bitcast(BF16))
+                quantise(z_w, z_s, 0, spent)
 
         def score_pass(b, m0, width):
             per_bank = BANK // width
@@ -324,13 +325,18 @@ def tile_list_limb_cut_advice_kernel(
                     start=(b == 0 and side == 0), stop=(b == 1 and side == per_bank - 1),
                 )
 
-        prepare_wl(wl_raw12, P, round_on_gpsimd)
+        prepare_wl(wl_raw123[:, :, 0:P], P, round_on_gpsimd)
+        prepare_wl(wl_raw123[:, :, P : 3 * P], 2 * P, round_on_gpsimd)
         first_tile()
-        products(1)
-        prepare_wl(wl_raw3, 3 * P, nc.scalar.copy)
+        readings(1)
+        gate(1)
+        difference()
+        open_sums()
+        readings(2)
+        round_wl_dealt(step[3][:].bitcast(BF16))
 
         for i in range(LAST):
-            interpolate(i + 1)
+            n = i + 1
             scatter(i)
             if i > 0:
                 fetch_limbs(i - 1, 0, bearers[(i - 1) % 2], diff_rows[:, i - 1, :])
@@ -342,20 +348,28 @@ def tile_list_limb_cut_advice_kernel(
             if i == 0:
                 deal_columns(nc.vector, wh_d[:], wh_c[:])
                 deal_columns(nc.vector, wg_d[:], wg_c[:])
+            interpolate(n)
             fetch_bearers(i, 0, bearers[i % 2])
-            if i + 2 <= LAST:
-                products(i + 2)
-            stage(i + 1)
+            if n < LAST:
+                difference()
+            weigh(n)
+            if n < LAST:
+                open_sums()
+                gate(n + 1)
+            if n + 1 < LAST:
+                readings(n + 2)
+            stage(n)
         quantise_staged(LAST - 1)
         last_wgs = wgs_rows[LAST][:].bitcast(BF16)
+        last_h = [part.bitcast(BF16) for part in staged_h(LAST)]
         late = {
-            0: last_wgs[:, 0:S], 256: last_wgs[:, S : 2 * S], 512: h_early[:].bitcast(BF16),
-            768: h_late.bitcast(BF16), 896: h_last[:].bitcast(BF16),
+            0: last_wgs[:, 0:S], 256: last_wgs[:, S : 2 * S], 512: last_h[1],
+            768: last_h[0][:, 0:BANK], 896: last_h[0][:, BANK:S],
         }
         for m0, width in PIECES:
             round_z(diff_rows[:, PACK : PACK + 2, m0 : m0 + width], late[m0], slice(0, 2))
         wd_w[0] = held([P, N], U32, "step%d" % (LAST % STEP_BUFS))[:]
-        quantise(wd_w[0], wd_s[0], 0, step[4 % STEP_BUFS].bitcast(BF16))
+        quantise(wd_w[0], wd_s[0], 0, step[5 % STEP_BUFS][:].bitcast(BF16))
         scatter(LAST)
         for m0, width in PIECES:
             score_pass(0, m0, width)

@@ -55,14 +55,12 @@ def tile_list_limb_cut_advice_kernel(
         def offsets(name, start, count):
             return lists[name][:, start // 16 : (start + count) // 16]
 
-        def load_scale_rows(name, rows, queues):
-            plane = held([P, rows.shape[2]], U8, name)
-            for q in range(QUADS):
+        def load_scale_rows(plane, rows, queues, quads=range(QUADS)):
+            for q in quads:
                 queues[q % len(queues)].dma_start(
                     out=plane[QUAD * q : QUAD * (q + 1), :].bitcast(I32),
                     in_=rows[0, 4 * q : 4 * q + 4, :].bitcast(I32).partition_broadcast(QUAD // 4),
                 )
-            return plane
 
         def load_rows_of_four(name, src):
             raw = held([P, PACK, src.shape[1]], F32, name)
@@ -94,14 +92,18 @@ def tile_list_limb_cut_advice_kernel(
             return rows
 
         nc.sync.dma_start(lists["offs"][:], offs)
-        tab_s = load_scale_rows("tab_s", tab_scales, (nc.scalar, nc.sync))
+        tab_s = held([P, T], U8, "tab_s")
+        load_scale_rows(tab_s, tab_scales, (nc.scalar, nc.sync))
         tab_w = held([P, T], U32, "tab_w")
         nc.scalar.dma_start(out=tab_w[:].bitcast(I32), in_=tab_words[0].rearrange("p t i -> p (t i)").bitcast(I32))
+        wg_s = held([P, H], U8, "wg_s")
+        wh_s = held([P, H], U8, "wh_s")
+        load_scale_rows(wg_s, wg_scales, (nc.sync,), (0, 1))
         wl_raw0 = load_rows_of_four("wl_raw0", wl[:, 0:P])
-        wg_s = load_scale_rows("wg_s", wg_scales, (nc.sync,))
+        load_scale_rows(wg_s, wg_scales, (nc.sync,), (2, 3))
         wg_a = load_words("wg_a", wg_i32[:, 0:P])
+        load_scale_rows(wh_s, wh_scales, (nc.sync,))
         wh_a = load_words("wh_a", wh_i32[:, 0 : 2 * P])
-        wh_s = load_scale_rows("wh_s", wh_scales, (nc.gpsimd, nc.sync))
         wl_raw123 = load_rows_of_four("wl_raw123", wl[:, P:PASS])
         wgs_natural = held([P, S], F32, "wgs_natural")
         nc.sync.dma_start(out=wgs_natural[:], in_=wgs)
@@ -151,8 +153,11 @@ def tile_list_limb_cut_advice_kernel(
             cols = slice(c0, c0 + grouped.shape[1] // PACK)
             nc.vector.quantize_mx(out=words[:, cols].bitcast(FP8X4), scales=scales[:, cols], in_=grouped)
 
+        def negated(into, source):
+            nc.scalar.activation(into, source, ACT.Copy, scale=-1.0)
+
         def round_on_gpsimd(into, source):
-            nc.gpsimd.tensor_scalar(into, source, 1.0, 0.0, ALU.mult, ALU.add)
+            nc.gpsimd.tensor_scalar(into, source, -1.0, 0.0, ALU.mult, ALU.add)
 
         def prepare_wl(raw, c0, copy):
             grouped = wl_grouped[:, c0 * PACK : (c0 + raw.shape[2]) * PACK]
@@ -161,9 +166,9 @@ def tile_list_limb_cut_advice_kernel(
 
         def round_wl_dealt(grouped):
             for t in range(PACK):
-                nc.scalar.copy(
-                    grouped[:, t * PASS : (t + 1) * PASS].rearrange("p (q h i j) -> p q h j i", h=2, i=PACK, j=PACK),
-                    wl_raw_dealt[:].rearrange("p j (q t h i) -> p t q h j i", t=PACK, h=2, i=PACK)[:, t],
+                negated(
+                    grouped[:, t * PASS : (t + 1) * PASS].rearrange("p (q s j) -> p q s j", s=RUN, j=PACK),
+                    wl_raw_dealt[:].rearrange("p j (q t s) -> p t q s j", t=PACK, s=RUN)[:, t],
                 )
 
         def deal_columns(engine, into, source):
@@ -175,14 +180,12 @@ def tile_list_limb_cut_advice_kernel(
         nc.vector.tensor_copy(v_s[:], tab_s[:].indirect(lists["offs"][:]))
         v_w = [held([P, BANK], U32, "v_w%d" % a) for a in range(2)]
         nc.vector.tensor_copy(v_w[0][:], tab_w[:].indirect(offsets("offs", 0, BANK)))
-        prepare_wl(wl_raw0[:], 0, nc.scalar.copy)
+        prepare_wl(wl_raw0[:], 0, negated)
         nc.vector.tensor_copy(v_w[1][:], tab_w[:].indirect(offsets("offs", BANK, BANK)))
         wh_sd = held([P, PASS], U8, "wh_sd")
         wg_sd = held([P, PASS], U8, "wg_sd")
         wh_d = held([P, PASS], I32, "wh_d")
         wg_d = held([P, PASS // 2], I32, "wg_d")
-        deal_columns(nc.gpsimd, wh_sd[:].bitcast(I32), wh_s[:, PASS:H].bitcast(I32))
-        deal_columns(nc.gpsimd, wg_sd[:].bitcast(I32), wg_s[:, PASS:H].bitcast(I32))
 
         def weights(i):
             cols = slice(P * i, P * (i + 1))
@@ -220,34 +223,42 @@ def tile_list_limb_cut_advice_kernel(
                         rhs=v_w[a][:].bitcast(FP8X4), rhs_scale=v_s[:, halves[a]], start=True, stop=True,
                     )
                 nc.scalar.activation(sig0[:, halves[a]], gate_bank[a][:], ACT.Sigmoid)
-                nc.scalar.copy(low0[:, halves[a]], sum_bank[a][:])
+                negated(low0[:, halves[a]], sum_bank[a][:])
             for a in range(2):
                 nc.vector.tensor_tensor(h0[:, halves[a]], high_bank[a][:], low0[:, halves[a]], ALU.subtract)
                 nc.vector.tensor_tensor(h0[:, halves[a]], h0[:, halves[a]], sig0[:, halves[a]], ALU.mult)
-                nc.vector.tensor_tensor(h0[:, halves[a]], h0[:, halves[a]], sum_bank[a][:], ALU.add)
+                nc.vector.tensor_tensor(h0[:, halves[a]], h0[:, halves[a]], sum_bank[a][:], ALU.subtract)
                 nc.vector.tensor_tensor(weighted[0][:, halves[a]], h0[:, halves[a]], wgs_natural[:, halves[a]], ALU.mult)
 
-        def product(i, name, bank, empty, into):
-            words, scales = weights(i)[name]
-            for a in range(2):
-                for blk in blocks:
+        def product(i, names, a, bank, empty, into):
+            for blk in blocks:
+                for name in names:
+                    words, scales = weights(i)[name]
                     nc.tensor.matmul_mx(
-                        bank[a][:, blk], lhsT=v_w[a][:, blk].bitcast(FP8X4),
+                        bank[:, blk], lhsT=v_w[a][:, blk].bitcast(FP8X4),
                         lhsT_scale=v_s[:, a * BANK + blk.start : a * BANK + blk.stop],
-                        rhs=words, rhs_scale=scales, start=True, stop=True,
+                        rhs=words, rhs_scale=scales, start=(name == names[0]), stop=(name == names[-1]),
                     )
-            for a in range(2):
-                empty(into[:, halves[a]], bank[a][:])
+            empty(into[:, halves[a]], bank[:])
 
         def sigmoid(into, source):
             nc.scalar.activation(into, source, ACT.Sigmoid)
 
         def readings(i):
-            product(i, "high", high_bank, nc.scalar.copy, high)
-            product(i, "low", low_bank, nc.scalar.copy, low)
+            for a in subtracted(i):
+                product(i, ("high",), a, high_bank[a], nc.scalar.copy, high)
+            for a in (1, 0):
+                product(i, ("low",), a, (low_bank if i < 3 else gate_bank)[a], negated, low)
+
+        def folded_difference(i):
+            product(i, ("high", "low"), 0, sum_bank[0], nc.scalar.copy, span)
 
         def gate(i):
-            product(i, "gate", gate_bank, sigmoid, sig)
+            for a in range(2):
+                product(i, ("gate",), a, gate_bank[a], sigmoid, sig)
+
+        def subtracted(i):
+            return (0, 1) if i == 1 else (1,)
 
         def add_transposed(bank, source, opens):
             for blk in blocks:
@@ -256,11 +267,13 @@ def tile_list_limb_cut_advice_kernel(
                     start=(opens and blk.start == 0), stop=(not opens and blk.stop == BANK),
                 )
 
-        def difference():
-            nc.gpsimd.tensor_tensor(span[:], high[:], low[:], ALU.subtract)
+        def difference(i):
+            for a in subtracted(i):
+                nc.gpsimd.tensor_tensor(span[:, halves[a]], high[:, halves[a]], low[:, halves[a]], ALU.subtract)
 
         def staged_h(i):
-            return (sig[:, halves[0]], diff_rows[:, i - 1, halves[1]] if i < LAST else span[:, halves[1]])
+            closing = diff_rows[:, i - 1, 0:CHUNK] if i < LAST else span[:, BANK : BANK + CHUNK]
+            return ((0, sig[:, 0:BANK]), (BANK, sig[:, BANK : BANK + CHUNK]), (BANK + CHUNK, closing))
 
         def open_sums():
             for a in range(2):
@@ -273,12 +286,13 @@ def tile_list_limb_cut_advice_kernel(
             for a in range(2):
                 nc.gpsimd.tensor_tensor(steps[a], span[:, halves[a]], sig[:, halves[a]], ALU.mult)
                 add_transposed(sum_bank[a], steps[a], False)
-            for a in range(2):
-                nc.scalar.copy(staged_h(i)[a], sum_bank[a][:])
+            for j0, part in staged_h(i):
+                nc.scalar.copy(part, sum_bank[j0 // BANK][:, j0 % BANK : j0 % BANK + part.shape[1]])
 
         def weigh(i):
-            for a in range(2):
-                nc.gpsimd.tensor_tensor(weighted[i % 2][:, halves[a]], staged_h(i)[a], wgs_rows[i][:, halves[a]], ALU.mult)
+            for j0, part in staged_h(i):
+                cols = slice(j0, j0 + part.shape[1])
+                nc.gpsimd.tensor_tensor(weighted[i % 2][:, cols], part, wgs_rows[i][:, cols], ALU.mult)
 
         def scatter(i):
             nc.vector.tensor_copy(pages[i][:].indirect(lists["offs2"][:]), weighted[i % 2])
@@ -297,6 +311,8 @@ def tile_list_limb_cut_advice_kernel(
 
         def stage(n):
             spent = step[n % STEP_BUFS][:].bitcast(BF16)
+            if n == 1:
+                round_wl_dealt(spent)
             if n in (4, 5):
                 nc.scalar.copy(by_four(spent), rows_by_four(wd_raw[5 - n][:]))
             if n == 6:
@@ -305,8 +321,8 @@ def tile_list_limb_cut_advice_kernel(
 
         def quantise_staged(n):
             spent = step[n % STEP_BUFS][:].bitcast(BF16)
-            if n == 0:
-                quantise(wl_w, wl_s, PASS, step[3][:].bitcast(BF16))
+            if n == 1:
+                quantise(wl_w, wl_s, PASS, spent)
             if n == 4:
                 quantise(wd_w[1], wd_s[1], 0, spent)
             if n == 6:
@@ -330,10 +346,9 @@ def tile_list_limb_cut_advice_kernel(
         first_tile()
         readings(1)
         gate(1)
-        difference()
+        difference(1)
         open_sums()
         readings(2)
-        round_wl_dealt(step[3][:].bitcast(BF16))
 
         for i in range(LAST):
             n = i + 1
@@ -348,12 +363,15 @@ def tile_list_limb_cut_advice_kernel(
             if i == 0:
                 deal_columns(nc.vector, wh_d[:], wh_c[:])
                 deal_columns(nc.vector, wg_d[:], wg_c[:])
+                deal_columns(nc.vector, wh_sd[:].bitcast(I32), wh_s[:, PASS:H].bitcast(I32))
+                deal_columns(nc.vector, wg_sd[:].bitcast(I32), wg_s[:, PASS:H].bitcast(I32))
             interpolate(n)
             fetch_bearers(i, 0, bearers[i % 2])
             if n < LAST:
-                difference()
+                difference(n + 1)
             weigh(n)
             if n < LAST:
+                folded_difference(n + 1)
                 open_sums()
                 gate(n + 1)
             if n + 1 < LAST:
@@ -361,10 +379,10 @@ def tile_list_limb_cut_advice_kernel(
             stage(n)
         quantise_staged(LAST - 1)
         last_wgs = wgs_rows[LAST][:].bitcast(BF16)
-        last_h = [part.bitcast(BF16) for part in staged_h(LAST)]
+        last_h = [part.bitcast(BF16) for j0, part in staged_h(LAST)]
         late = {
-            0: last_wgs[:, 0:S], 256: last_wgs[:, S : 2 * S], 512: last_h[1],
-            768: last_h[0][:, 0:BANK], 896: last_h[0][:, BANK:S],
+            0: last_wgs[:, 0:S], 256: last_wgs[:, S : 2 * S], 512: last_h[0],
+            768: last_h[1], 896: last_h[2],
         }
         for m0, width in PIECES:
             round_z(diff_rows[:, PACK : PACK + 2, m0 : m0 + width], late[m0], slice(0, 2))

@@ -139,7 +139,7 @@ def tile_list_limb_cut_advice_kernel(
         wl_w = held([P, H], U32, "wl_w")
         wl_s = held([P, H], U8, "wl_s")
         wd_s = [held([P, N], U8, "wd_s%d" % b)[:] for b in range(2)]
-        z_w = held([P, 2 * M_OUT], U32, "z_w")
+        z_w = {(0, 0): held([P, BANK], U32, "z_w00"), (1, 0): held([P, BANK], U32, "z_w10"), (1, 1): held([P, BANK], U32, "z_w11")}
         z_s = held([P, 2 * M_OUT], U8, "z_s")
         wl_grouped = held([P, PASS * PACK], BF16, "wl_grouped")
 
@@ -152,6 +152,10 @@ def tile_list_limb_cut_advice_kernel(
         def quantise(words, scales, c0, grouped):
             cols = slice(c0, c0 + grouped.shape[1] // PACK)
             nc.vector.quantize_mx(out=words[:, cols].bitcast(FP8X4), scales=scales[:, cols], in_=grouped)
+
+        def z_operand(b, m0, width):
+            x = m0 % BANK
+            return z_w[b, m0 // BANK][:, x : x + width], z_s[:, b * M_OUT + m0 : b * M_OUT + m0 + width]
 
         def negated(into, source):
             nc.scalar.activation(into, source, ACT.Copy, scale=-1.0)
@@ -187,6 +191,9 @@ def tile_list_limb_cut_advice_kernel(
         wh_d = held([P, PASS], I32, "wh_d")
         wg_d = held([P, PASS // 2], I32, "wg_d")
 
+        deal_columns(nc.gpsimd, wh_sd[:].bitcast(I32), wh_s[:, PASS:H].bitcast(I32))
+        deal_columns(nc.gpsimd, wg_sd[:].bitcast(I32), wg_s[:, PASS:H].bitcast(I32))
+
         def weights(i):
             cols = slice(P * i, P * (i + 1))
             if i < PACK:
@@ -205,7 +212,7 @@ def tile_list_limb_cut_advice_kernel(
         low = held([P, S], F32, "low")
         sig = held([P, S], F32, "sig")
         span = held([P, S], F32, "span")
-        step = [held([P, S if s != 2 else 2 * S], F32, "step%d" % s) for s in range(STEP_BUFS)]
+        step = [held([P, S], F32, "step%d" % s) for s in range(STEP_BUFS)]
         tail = held([P, 2, S], F32, "tail")
         weighted = [held([P, S], F32, "weighted0")[:], tail[:, 0, :]]
         wd_w = {1: held([P, N], U32, "wd_w1")[:]}
@@ -271,28 +278,21 @@ def tile_list_limb_cut_advice_kernel(
             for a in subtracted(i):
                 nc.gpsimd.tensor_tensor(span[:, halves[a]], high[:, halves[a]], low[:, halves[a]], ALU.subtract)
 
-        def staged_h(i):
-            closing = diff_rows[:, i - 1, 0:CHUNK] if i < LAST else span[:, BANK : BANK + CHUNK]
-            return ((0, sig[:, 0:BANK]), (BANK, sig[:, BANK : BANK + CHUNK]), (BANK + CHUNK, closing))
-
         def open_sums():
             for a in range(2):
                 add_transposed(sum_bank[a], low[:, halves[a]], True)
 
         def interpolate(i):
-            ring_step = step[i % STEP_BUFS]
-            middle = (ring_step.shape[1] - BANK) // 2
-            steps = (bearers[(i + 1) % 2][:, 0:BANK], ring_step[:, middle : middle + BANK])
+            steps = (bearers[i % 2][:, halves[0]], step[i % STEP_BUFS][:, halves[1]])
             for a in range(2):
                 nc.gpsimd.tensor_tensor(steps[a], span[:, halves[a]], sig[:, halves[a]], ALU.mult)
                 add_transposed(sum_bank[a], steps[a], False)
-            for j0, part in staged_h(i):
-                nc.scalar.copy(part, sum_bank[j0 // BANK][:, j0 % BANK : j0 % BANK + part.shape[1]])
+            for a in range(2):
+                nc.scalar.copy(sig[:, halves[a]], sum_bank[a][:])
 
         def weigh(i):
-            for j0, part in staged_h(i):
-                cols = slice(j0, j0 + part.shape[1])
-                nc.gpsimd.tensor_tensor(weighted[i % 2][:, cols], part, wgs_rows[i][:, cols], ALU.mult)
+            for a in range(2):
+                nc.gpsimd.tensor_tensor(weighted[i % 2][:, halves[a]], sig[:, halves[a]], wgs_rows[i][:, halves[a]], ALU.mult)
 
         def scatter(i):
             nc.vector.tensor_copy(pages[i][:].indirect(lists["offs2"][:]), weighted[i % 2])
@@ -313,31 +313,30 @@ def tile_list_limb_cut_advice_kernel(
             spent = step[n % STEP_BUFS][:].bitcast(BF16)
             if n == 1:
                 round_wl_dealt(spent)
-            if n in (4, 5):
-                nc.scalar.copy(by_four(spent), rows_by_four(wd_raw[5 - n][:]))
-            if n == 6:
-                for a in range(2):
-                    round_z(dealt_rows_z[:, :, halves[a]], spent[:, 2 * a * S : 2 * (a + 1) * S], slice(0, PACK))
+            if n in (3, 4):
+                nc.scalar.copy(by_four(spent), rows_by_four(wd_raw[4 - n][:]))
+            if n in (5, 6):
+                round_z(dealt_rows_z[:, :, halves[n - 5]], spent, slice(0, PACK))
 
         def quantise_staged(n):
             spent = step[n % STEP_BUFS][:].bitcast(BF16)
             if n == 1:
                 quantise(wl_w, wl_s, PASS, spent)
-            if n == 4:
+            if n == 3:
                 quantise(wd_w[1], wd_s[1], 0, spent)
-            if n == 6:
-                quantise(z_w, z_s, 0, spent)
+            if n == 5:
+                quantise(*z_operand(0, 0, BANK), 0, spent)
 
         def score_pass(b, m0, width):
             per_bank = BANK // width
             for nb in range(N // P):
                 part, side = divmod(nb, per_bank)
                 cols = slice(nb * P, (nb + 1) * P)
-                moving = slice(b * M_OUT + m0, b * M_OUT + m0 + width)
+                words, scales = z_operand(b, m0, width)
                 nc.tensor.matmul_mx(
                     banks[m0 // P + part][:, side * width : (side + 1) * width],
                     lhsT=wd_w[b][:, cols].bitcast(FP8X4), lhsT_scale=wd_s[b][:, cols],
-                    rhs=z_w[:, moving].bitcast(FP8X4), rhs_scale=z_s[:, moving],
+                    rhs=words.bitcast(FP8X4), rhs_scale=scales,
                     start=(b == 0 and side == 0), stop=(b == 1 and side == per_bank - 1),
                 )
 
@@ -352,24 +351,21 @@ def tile_list_limb_cut_advice_kernel(
 
         for i in range(LAST):
             n = i + 1
-            scatter(i)
-            if i > 0:
-                fetch_limbs(i - 1, 0, bearers[(i - 1) % 2], diff_rows[:, i - 1, :])
-            if 0 < i <= PACK:
-                nc.sync.dma_start(out=dealt_rows_z[QUAD * (i - 1) : QUAD * i], in_=diff_rows[:, i - 1, :])
-                load_later(i - 1)
-            if i < LAST - 1:
-                quantise_staged(i)
-            if i == 0:
-                deal_columns(nc.vector, wh_d[:], wh_c[:])
-                deal_columns(nc.vector, wg_d[:], wg_c[:])
-                deal_columns(nc.vector, wh_sd[:].bitcast(I32), wh_s[:, PASS:H].bitcast(I32))
-                deal_columns(nc.vector, wg_sd[:].bitcast(I32), wg_s[:, PASS:H].bitcast(I32))
             interpolate(n)
-            fetch_bearers(i, 0, bearers[i % 2])
             if n < LAST:
                 difference(n + 1)
             weigh(n)
+            scatter(i)
+            fetch_bearers(i, 0, bearers[i % 2])
+            if i < LAST - 1:
+                fetch_limbs(i, 0, bearers[i % 2], diff_rows[:, i, :])
+            if i < PACK:
+                nc.sync.dma_start(out=dealt_rows_z[QUAD * i : QUAD * (i + 1)], in_=diff_rows[:, i, :])
+                load_later(i)
+            quantise_staged(i)
+            if i == 0:
+                deal_columns(nc.gpsimd, wh_d[:], wh_c[:])
+                deal_columns(nc.gpsimd, wg_d[:], wg_c[:])
             if n < LAST:
                 folded_difference(n + 1)
                 open_sums()
@@ -377,17 +373,17 @@ def tile_list_limb_cut_advice_kernel(
             if n + 1 < LAST:
                 readings(n + 2)
             stage(n)
-        quantise_staged(LAST - 1)
-        last_wgs = wgs_rows[LAST][:].bitcast(BF16)
-        last_h = [part.bitcast(BF16) for j0, part in staged_h(LAST)]
+        last_wgs, last_h = wgs_rows[LAST][:].bitcast(BF16), sig[:].bitcast(BF16)
         late = {
-            0: last_wgs[:, 0:S], 256: last_wgs[:, S : 2 * S], 512: last_h[0],
-            768: last_h[1], 896: last_h[2],
+            0: last_wgs[:, 0:S], 256: last_wgs[:, S : 2 * S], 512: last_h[:, 0:S],
+            768: last_h[:, S : S + BANK], 896: last_h[:, S + BANK : 2 * S],
         }
         for m0, width in PIECES:
             round_z(diff_rows[:, PACK : PACK + 2, m0 : m0 + width], late[m0], slice(0, 2))
+        z_w[0, 1] = held([P, BANK], U32, "span")
+        quantise(*z_operand(0, BANK, BANK), 0, step[6 % STEP_BUFS][:].bitcast(BF16))
         wd_w[0] = held([P, N], U32, "step%d" % (LAST % STEP_BUFS))[:]
-        quantise(wd_w[0], wd_s[0], 0, step[5 % STEP_BUFS][:].bitcast(BF16))
+        quantise(wd_w[0], wd_s[0], 0, step[4 % STEP_BUFS][:].bitcast(BF16))
         scatter(LAST)
         for m0, width in PIECES:
             score_pass(0, m0, width)
@@ -396,34 +392,40 @@ def tile_list_limb_cut_advice_kernel(
         staged = [spare[:, x * BANK : (x + 1) * BANK] for x in range(4)]
         staged = staged + [dealt[:, 2 * M_OUT + x * BANK : 2 * M_OUT + (x + 1) * BANK] for x in range(4)]
 
-        def store(m0, width, copies):
+        def store(m0, width, part, copy):
             per_bank = BANK // width
             out_rows = out.rearrange("(a s p) m -> a p s m", s=per_bank, p=P)
-            for part in range(width // P):
-                bank = m0 // P + part
-                copies[part](staged[bank], banks[bank][:])
-                nc.sync.dma_start(
-                    out=out_rows[part][:, :, m0 : m0 + width],
-                    in_=staged[bank].rearrange("p (s m) -> p s m", s=per_bank),
-                )
+            bank = m0 // P + part
+            copy(staged[bank], banks[bank][:])
+            nc.sync.dma_start(
+                out=out_rows[part][:, :, m0 : m0 + width], in_=staged[bank].rearrange("p (s m) -> p s m", s=per_bank)
+            )
 
-        def finish(m0, width, copies):
-            quantise(z_w, z_s, M_OUT + m0, late[m0])
+        def finish(m0, width):
+            quantise(*z_operand(1, m0, width), 0, late[m0])
             score_pass(1, m0, width)
-            store(m0, width, copies)
 
-        last_bearers = {}
         for x, (m0, width) in enumerate(PIECES):
             c0 = m0 - m0 % CHUNK
+            if c0 < 2 * CHUNK:
+                last_bearers = bearers[LAST % 2][:, c0 : c0 + CHUNK]
+                pair = tail[:, :, c0 : c0 + CHUNK]
+            else:
+                last_bearers = tail[:, 0, c0 - 2 * CHUNK : c0 - CHUNK]
+                pair = late[c0 - 2 * CHUNK].bitcast(F32).rearrange("p (s m) -> p s m", s=2)
+            cols = slice(m0 - c0, m0 - c0 + width)
             if m0 == c0:
-                if c0 < 2 * CHUNK:
-                    last_bearers[c0] = bearers[LAST % 2][:, c0 : c0 + CHUNK]
-                else:
-                    last_bearers[c0] = late[c0 - 2 * CHUNK].bitcast(F32)[:, 0:CHUNK]
-                fetch_bearers(LAST, c0, last_bearers[c0])
-            fetch_limbs(LAST - 1, m0, bearers[(LAST - 1) % 2][:, m0 : m0 + width], tail[:, 0, m0 : m0 + width])
-            fetch_limbs(LAST, m0, last_bearers[c0][:, m0 - c0 : m0 - c0 + width], tail[:, 1, m0 : m0 + width])
-            round_z(tail[:, :, m0 : m0 + width], late[m0], slice(2, PACK))
+                fetch_bearers(LAST, c0, last_bearers)
+            fetch_limbs(LAST - 1, m0, bearers[(LAST - 1) % 2][:, m0 : m0 + width], pair[:, 0, cols])
+            fetch_limbs(LAST, m0, last_bearers[:, cols], pair[:, 1, cols])
+            round_z(pair[:, :, cols], late[m0], slice(2, PACK))
             if x > 0:
-                finish(*PIECES[x - 1], (nc.scalar.copy, nc.scalar.copy if x < 3 else nc.vector.tensor_copy))
-        finish(*PIECES[-1], (nc.vector.tensor_copy,))
+                finish(*PIECES[x - 1])
+            if 0 < x < 3:
+                for part in range(2):
+                    store(*PIECES[x - 1], part, nc.scalar.copy)
+        finish(*PIECES[4])
+        for part in range(2):
+            store(*PIECES[2], part, nc.scalar.copy)
+        store(*PIECES[3], 0, nc.scalar.copy)
+        store(*PIECES[4], 0, nc.vector.tensor_copy)

@@ -29,7 +29,7 @@ LAST = TILES - 1
 CHUNK = 256
 PIECES = ((0, 256), (256, 256), (512, 256), (768, 128), (896, 128))
 PAGE_BUFS = 5
-STEP_BUFS = 4
+LOW_BUFS = 4
 
 
 def tile_list_limb_cut_advice_kernel(
@@ -113,10 +113,10 @@ def tile_list_limb_cut_advice_kernel(
         wg_b = load_words("wg_b", wg_i32[:, P : 2 * P])
         nc.sync.dma_start(lists["offs4"][:], offs4)
         nc.sync.dma_start(lists["offs3"][:], offs3)
-        wh_c = load_words("wh_c", wh_i32[:, PASS:H])
-        wg_c = load_words("wg_c", wg_i32[:, 2 * P : PASS])
         wl_raw_dealt = load_rows_of_four("wl_raw_dealt", wl[:, PASS:H])
         load_page(1)
+        wh_c = load_words("wh_c", wh_i32[:, PASS:H])
+        wg_c = load_words("wg_c", wg_i32[:, 2 * P : PASS])
         load_page(2)
         load_page(3)
         wgs_rows = [wgs_natural] * PACK
@@ -209,10 +209,9 @@ def tile_list_limb_cut_advice_kernel(
             }
 
         high = held([P, S], F32, "high")
-        low = held([P, S], F32, "low")
         sig = held([P, S], F32, "sig")
         span = held([P, S], F32, "span")
-        step = [held([P, S], F32, "step%d" % s) for s in range(STEP_BUFS)]
+        low = [held([P, S], F32, "low%d" % s) for s in range(LOW_BUFS)]
         tail = held([P, 2, S], F32, "tail")
         weighted = [held([P, S], F32, "weighted0")[:], tail[:, 0, :]]
         wd_w = {1: held([P, N], U32, "wd_w1")[:]}
@@ -220,9 +219,8 @@ def tile_list_limb_cut_advice_kernel(
         diff = held([P, (LAST - 1) * M_OUT], F32, "diff")
         dealt = held([P, PACK * M_OUT], F32, "dealt")
 
-        def first_tile():
+        def first_products():
             w = weights(0)
-            low0, sig0, h0 = weighted[1], tail[:, 1, :], step[0]
             for a in range(2):
                 for bank, name in ((gate_bank, "gate"), (sum_bank, "low"), (high_bank, "high")):
                     nc.tensor.matmul_mx(
@@ -231,11 +229,18 @@ def tile_list_limb_cut_advice_kernel(
                     )
                 nc.scalar.activation(sig0[:, halves[a]], gate_bank[a][:], ACT.Sigmoid)
                 negated(low0[:, halves[a]], sum_bank[a][:])
+
+        def first_interpolation():
             for a in range(2):
                 nc.vector.tensor_tensor(h0[:, halves[a]], high_bank[a][:], low0[:, halves[a]], ALU.subtract)
                 nc.vector.tensor_tensor(h0[:, halves[a]], h0[:, halves[a]], sig0[:, halves[a]], ALU.mult)
                 nc.vector.tensor_tensor(h0[:, halves[a]], h0[:, halves[a]], sum_bank[a][:], ALU.subtract)
+
+        def first_weighing():
+            for a in range(2):
                 nc.vector.tensor_tensor(weighted[0][:, halves[a]], h0[:, halves[a]], wgs_natural[:, halves[a]], ALU.mult)
+
+        low0, sig0, h0 = weighted[1], tail[:, 1, :], low[0]
 
         def product(i, names, a, bank, empty, into):
             for blk in blocks:
@@ -248,24 +253,25 @@ def tile_list_limb_cut_advice_kernel(
                     )
             empty(into[:, halves[a]], bank[:])
 
+        def minus(subtrahend):
+            return lambda into, source: nc.vector.tensor_tensor(into, source, subtrahend, ALU.subtract)
+
         def sigmoid(into, source):
             nc.scalar.activation(into, source, ACT.Sigmoid)
 
-        def readings(i):
-            for a in subtracted(i):
-                product(i, ("high",), a, high_bank[a], nc.scalar.copy, high)
+        def high_reading(i):
+            product(i, ("high",), 1, (high_bank if i < 3 else sum_bank)[1], nc.scalar.copy, high)
+
+        def low_reading(i):
             for a in (1, 0):
-                product(i, ("low",), a, (low_bank if i < 3 else gate_bank)[a], negated, low)
+                product(i, ("low",), a, (low_bank if i < 3 else gate_bank)[a], negated, low[i % LOW_BUFS])
 
         def folded_difference(i):
             product(i, ("high", "low"), 0, sum_bank[0], nc.scalar.copy, span)
 
         def gate(i):
-            for a in range(2):
+            for a in (1, 0):
                 product(i, ("gate",), a, gate_bank[a], sigmoid, sig)
-
-        def subtracted(i):
-            return (0, 1) if i == 1 else (1,)
 
         def add_transposed(bank, source, opens):
             for blk in blocks:
@@ -275,23 +281,22 @@ def tile_list_limb_cut_advice_kernel(
                 )
 
         def difference(i):
-            for a in subtracted(i):
-                nc.gpsimd.tensor_tensor(span[:, halves[a]], high[:, halves[a]], low[:, halves[a]], ALU.subtract)
+            nc.gpsimd.tensor_tensor(span[:, halves[1]], high[:, halves[1]], low[i % LOW_BUFS][:, halves[1]], ALU.subtract)
 
-        def open_sums():
-            for a in range(2):
-                add_transposed(sum_bank[a], low[:, halves[a]], True)
+        def open_sums(i):
+            for a in (1, 0):
+                add_transposed(sum_bank[a], low[i % LOW_BUFS][:, halves[a]], True)
 
         def interpolate(i):
-            steps = (bearers[i % 2][:, halves[0]], step[i % STEP_BUFS][:, halves[1]])
-            for a in range(2):
+            steps = [bearers[i % 2][:, halves[a]] for a in range(2)]
+            for a in (1, 0):
                 nc.gpsimd.tensor_tensor(steps[a], span[:, halves[a]], sig[:, halves[a]], ALU.mult)
                 add_transposed(sum_bank[a], steps[a], False)
-            for a in range(2):
+            for a in (1, 0):
                 nc.scalar.copy(sig[:, halves[a]], sum_bank[a][:])
 
         def weigh(i):
-            for a in range(2):
+            for a in (1, 0):
                 nc.gpsimd.tensor_tensor(weighted[i % 2][:, halves[a]], sig[:, halves[a]], wgs_rows[i][:, halves[a]], ALU.mult)
 
         def scatter(i):
@@ -310,16 +315,21 @@ def tile_list_limb_cut_advice_kernel(
         diff_rows = diff[:].rearrange("p (t m) -> p t m", t=LAST - 1)
 
         def stage(n):
-            spent = step[n % STEP_BUFS][:].bitcast(BF16)
+            spent = low[(n + 1) % LOW_BUFS][:].bitcast(BF16)
             if n == 1:
                 round_wl_dealt(spent)
             if n in (3, 4):
-                nc.scalar.copy(by_four(spent), rows_by_four(wd_raw[4 - n][:]))
+                for x in range(0, N, CHUNK):
+                    nc.scalar.copy(
+                        by_four(spent[:, x * PACK : (x + CHUNK) * PACK]), rows_by_four(wd_raw[4 - n][:, :, x : x + CHUNK])
+                    )
             if n in (5, 6):
-                round_z(dealt_rows_z[:, :, halves[n - 5]], spent, slice(0, PACK))
+                for x in range(0, BANK, CHUNK):
+                    m0 = (n - 5) * BANK + x
+                    round_z(dealt_rows_z[:, :, m0 : m0 + CHUNK], spent[:, x * PACK : (x + CHUNK) * PACK], slice(0, PACK))
 
         def quantise_staged(n):
-            spent = step[n % STEP_BUFS][:].bitcast(BF16)
+            spent = low[(n + 1) % LOW_BUFS][:].bitcast(BF16)
             if n == 1:
                 quantise(wl_w, wl_s, PASS, spent)
             if n == 3:
@@ -342,12 +352,16 @@ def tile_list_limb_cut_advice_kernel(
 
         prepare_wl(wl_raw123[:, :, 0:P], P, round_on_gpsimd)
         prepare_wl(wl_raw123[:, :, P : 3 * P], 2 * P, round_on_gpsimd)
-        first_tile()
-        readings(1)
+        first_products()
+        first_interpolation()
+        first_weighing()
+        low_reading(1)
+        for a in (1, 0):
+            product(1, ("high",), a, high_bank[a], minus(low[1][:, halves[a]]), span)
         gate(1)
-        difference(1)
-        open_sums()
-        readings(2)
+        open_sums(1)
+        high_reading(2)
+        low_reading(2)
 
         for i in range(LAST):
             n = i + 1
@@ -364,14 +378,16 @@ def tile_list_limb_cut_advice_kernel(
                 load_later(i)
             quantise_staged(i)
             if i == 0:
-                deal_columns(nc.gpsimd, wh_d[:], wh_c[:])
-                deal_columns(nc.gpsimd, wg_d[:], wg_c[:])
+                deal_columns(nc.vector, wh_d[:], wh_c[:])
+                deal_columns(nc.vector, wg_d[:], wg_c[:])
+            if n + 1 < LAST:
+                high_reading(n + 2)
             if n < LAST:
                 folded_difference(n + 1)
-                open_sums()
+                open_sums(n + 1)
                 gate(n + 1)
             if n + 1 < LAST:
-                readings(n + 2)
+                low_reading(n + 2)
             stage(n)
         last_wgs, last_h = wgs_rows[LAST][:].bitcast(BF16), sig[:].bitcast(BF16)
         late = {
@@ -381,9 +397,9 @@ def tile_list_limb_cut_advice_kernel(
         for m0, width in PIECES:
             round_z(diff_rows[:, PACK : PACK + 2, m0 : m0 + width], late[m0], slice(0, 2))
         z_w[0, 1] = held([P, BANK], U32, "span")
-        quantise(*z_operand(0, BANK, BANK), 0, step[6 % STEP_BUFS][:].bitcast(BF16))
-        wd_w[0] = held([P, N], U32, "step%d" % (LAST % STEP_BUFS))[:]
-        quantise(wd_w[0], wd_s[0], 0, step[4 % STEP_BUFS][:].bitcast(BF16))
+        quantise(*z_operand(0, BANK, BANK), 0, low[7 % LOW_BUFS][:].bitcast(BF16))
+        wd_w[0] = held([P, N], U32, "bearers%d" % (LAST % 2))[:]
+        quantise(wd_w[0], wd_s[0], 0, low[5 % LOW_BUFS][:].bitcast(BF16))
         scatter(LAST)
         for m0, width in PIECES:
             score_pass(0, m0, width)
@@ -408,7 +424,7 @@ def tile_list_limb_cut_advice_kernel(
         for x, (m0, width) in enumerate(PIECES):
             c0 = m0 - m0 % CHUNK
             if c0 < 2 * CHUNK:
-                last_bearers = bearers[LAST % 2][:, c0 : c0 + CHUNK]
+                last_bearers = diff_rows[:, 0, c0 : c0 + CHUNK]
                 pair = tail[:, :, c0 : c0 + CHUNK]
             else:
                 last_bearers = tail[:, 0, c0 - 2 * CHUNK : c0 - CHUNK]

@@ -29,6 +29,7 @@ LAST = TILES - 1
 CHUNK = 256
 PIECES = ((0, 256), (256, 256), (512, 256), (768, 128), (896, 128))
 PAGE_BUFS = 5
+WH_ROW = 4
 LOW_BUFS = 4
 
 
@@ -61,6 +62,11 @@ def tile_list_limb_cut_advice_kernel(
                     out=plane[QUAD * q : QUAD * (q + 1), :].bitcast(I32),
                     in_=rows[0, 4 * q : 4 * q + 4, :].bitcast(I32).partition_broadcast(QUAD // 4),
                 )
+
+        def load_live_rows(rows, first):
+            for q in range(QUADS):
+                p0 = QUAD * q + first
+                nc.sync.dma_start(out=w_s[p0 : p0 + 4, :].bitcast(I32), in_=rows[0, 4 * q : 4 * q + 4, :].bitcast(I32))
 
         def load_rows_of_four(name, src):
             raw = held([P, PACK, src.shape[1]], F32, name)
@@ -96,14 +102,13 @@ def tile_list_limb_cut_advice_kernel(
         load_scale_rows(tab_s, tab_scales, (nc.scalar, nc.sync))
         tab_w = held([P, T], U32, "tab_w")
         nc.scalar.dma_start(out=tab_w[:].bitcast(I32), in_=tab_words[0].rearrange("p t i -> p (t i)").bitcast(I32))
-        wg_s = held([P, H], U8, "wg_s")
-        wh_s = held([P, H], U8, "wh_s")
-        load_scale_rows(wg_s, wg_scales, (nc.sync,), (0, 1))
+        w_s = held([P, H], U8, "w_s")
+        nc.gpsimd.memset(w_s[:].bitcast(I32), 0)
         wl_raw0 = load_rows_of_four("wl_raw0", wl[:, 0:P])
-        load_scale_rows(wg_s, wg_scales, (nc.sync,), (2, 3))
         wg_a = load_words("wg_a", wg_i32[:, 0:P])
-        load_scale_rows(wh_s, wh_scales, (nc.sync,))
+        load_live_rows(wg_scales, 0)
         wh_a = load_words("wh_a", wh_i32[:, 0 : 2 * P])
+        load_live_rows(wh_scales, WH_ROW)
         wl_raw123 = load_rows_of_four("wl_raw123", wl[:, P:PASS])
         wgs_natural = held([P, S], F32, "wgs_natural")
         nc.sync.dma_start(out=wgs_natural[:], in_=wgs)
@@ -139,7 +144,7 @@ def tile_list_limb_cut_advice_kernel(
         wl_w = held([P, H], U32, "wl_w")
         wl_s = held([P, H], U8, "wl_s")
         wd_s = [held([P, N], U8, "wd_s%d" % b)[:] for b in range(2)]
-        z_w = {(0, 0): held([P, BANK], U32, "z_w00"), (1, 0): held([P, BANK], U32, "z_w10"), (1, 1): held([P, BANK], U32, "z_w11")}
+        z_w = {1: held([P, M_OUT], U32, "z_w1")}
         z_s = held([P, 2 * M_OUT], U8, "z_s")
         wl_grouped = held([P, PASS * PACK], BF16, "wl_grouped")
 
@@ -154,18 +159,22 @@ def tile_list_limb_cut_advice_kernel(
             nc.vector.quantize_mx(out=words[:, cols].bitcast(FP8X4), scales=scales[:, cols], in_=grouped)
 
         def z_operand(b, m0, width):
-            x = m0 % BANK
-            return z_w[b, m0 // BANK][:, x : x + width], z_s[:, b * M_OUT + m0 : b * M_OUT + m0 + width]
+            return z_w[b][:, m0 : m0 + width], z_s[:, b * M_OUT + m0 : b * M_OUT + m0 + width]
 
         def negated(into, source):
             nc.scalar.activation(into, source, ACT.Copy, scale=-1.0)
 
-        def round_on_gpsimd(into, source):
-            nc.gpsimd.tensor_scalar(into, source, -1.0, 0.0, ALU.mult, ALU.add)
+        def round_on_scalar(grouped, raw):
+            negated(by_four(grouped), rows_by_four(raw))
 
-        def prepare_wl(raw, c0, copy):
+        def round_on_gpsimd(grouped, raw):
+            nc.gpsimd.tensor_scalar(
+                grouped.rearrange("p (c j) -> p c j", j=PACK), raw.rearrange("p j c -> p c j"), -1.0, 0.0, ALU.mult, ALU.add
+            )
+
+        def prepare_wl(raw, c0, rounding):
             grouped = wl_grouped[:, c0 * PACK : (c0 + raw.shape[2]) * PACK]
-            copy(by_four(grouped), rows_by_four(raw))
+            rounding(grouped, raw)
             quantise(wl_w, wl_s, c0, grouped)
 
         def round_wl_dealt(grouped):
@@ -184,24 +193,22 @@ def tile_list_limb_cut_advice_kernel(
         nc.vector.tensor_copy(v_s[:], tab_s[:].indirect(lists["offs"][:]))
         v_w = [held([P, BANK], U32, "v_w%d" % a) for a in range(2)]
         nc.vector.tensor_copy(v_w[0][:], tab_w[:].indirect(offsets("offs", 0, BANK)))
-        prepare_wl(wl_raw0[:], 0, negated)
+        prepare_wl(wl_raw0[:], 0, round_on_scalar)
         nc.vector.tensor_copy(v_w[1][:], tab_w[:].indirect(offsets("offs", BANK, BANK)))
-        wh_sd = held([P, PASS], U8, "wh_sd")
-        wg_sd = held([P, PASS], U8, "wg_sd")
+        w_sd = held([P, PASS], U8, "w_sd")
         wh_d = held([P, PASS], I32, "wh_d")
         wg_d = held([P, PASS // 2], I32, "wg_d")
 
-        deal_columns(nc.gpsimd, wh_sd[:].bitcast(I32), wh_s[:, PASS:H].bitcast(I32))
-        deal_columns(nc.gpsimd, wg_sd[:].bitcast(I32), wg_s[:, PASS:H].bitcast(I32))
+        deal_columns(nc.gpsimd, w_sd[:].bitcast(I32), w_s[:, PASS:H].bitcast(I32))
 
         def weights(i):
             cols = slice(P * i, P * (i + 1))
             if i < PACK:
                 wh_t, wg_t, x = (wh_a, wg_a, i) if i < 2 else (wh_b, wg_b, i - 2)
-                high_scales, gate_scales = wh_s[:, cols], wg_s[:, cols]
+                high_scales, gate_scales = w_s[WH_ROW:P, cols], w_s[:, cols]
             else:
                 wh_t, wg_t, x = wh_d, wg_d, i - PACK
-                high_scales, gate_scales = wh_sd[:, P * x : P * (x + 1)], wg_sd[:, P * x : P * (x + 1)]
+                high_scales, gate_scales = w_sd[WH_ROW:P, P * x : P * (x + 1)], w_sd[:, P * x : P * (x + 1)]
             return {
                 "gate": (wg_t[:, x * P // 2 : (x + 1) * P // 2].bitcast(U8).bitcast(FP4X4), gate_scales),
                 "low": (wl_w[:, cols].bitcast(FP8X4), wl_s[:, cols]),
@@ -211,7 +218,8 @@ def tile_list_limb_cut_advice_kernel(
         high = held([P, S], F32, "high")
         sig = held([P, S], F32, "sig")
         span = held([P, S], F32, "span")
-        low = [held([P, S], F32, "low%d" % s) for s in range(LOW_BUFS)]
+        wide_low = held([P, 2 * S], F32, "wide_low")
+        low = [held([P, S], F32, "low%d" % s)[:] for s in range(LOW_BUFS - 1)] + [wide_low[:, BANK : BANK + S]]
         tail = held([P, 2, S], F32, "tail")
         weighted = [held([P, S], F32, "weighted0")[:], tail[:, 0, :]]
         wd_w = {1: held([P, N], U32, "wd_w1")[:]}
@@ -315,7 +323,7 @@ def tile_list_limb_cut_advice_kernel(
         diff_rows = diff[:].rearrange("p (t m) -> p t m", t=LAST - 1)
 
         def stage(n):
-            spent = low[(n + 1) % LOW_BUFS][:].bitcast(BF16)
+            spent = low[(n + 1) % LOW_BUFS].bitcast(BF16)
             if n == 1:
                 round_wl_dealt(spent)
             if n in (3, 4):
@@ -323,19 +331,17 @@ def tile_list_limb_cut_advice_kernel(
                     nc.scalar.copy(
                         by_four(spent[:, x * PACK : (x + CHUNK) * PACK]), rows_by_four(wd_raw[4 - n][:, :, x : x + CHUNK])
                     )
-            if n in (5, 6):
-                for x in range(0, BANK, CHUNK):
-                    m0 = (n - 5) * BANK + x
-                    round_z(dealt_rows_z[:, :, m0 : m0 + CHUNK], spent[:, x * PACK : (x + CHUNK) * PACK], slice(0, PACK))
+            if n == 6:
+                for a in (1, 0):
+                    grouped = wide_low[:, a * S : (a + 1) * S].bitcast(BF16)
+                    round_z(dealt_rows_z[:, :, halves[a]], grouped, slice(0, PACK))
 
         def quantise_staged(n):
-            spent = low[(n + 1) % LOW_BUFS][:].bitcast(BF16)
+            spent = low[(n + 1) % LOW_BUFS].bitcast(BF16)
             if n == 1:
                 quantise(wl_w, wl_s, PASS, spent)
             if n == 3:
                 quantise(wd_w[1], wd_s[1], 0, spent)
-            if n == 5:
-                quantise(*z_operand(0, 0, BANK), 0, spent)
 
         def score_pass(b, m0, width):
             per_bank = BANK // width
@@ -396,10 +402,10 @@ def tile_list_limb_cut_advice_kernel(
         }
         for m0, width in PIECES:
             round_z(diff_rows[:, PACK : PACK + 2, m0 : m0 + width], late[m0], slice(0, 2))
-        z_w[0, 1] = held([P, BANK], U32, "span")
-        quantise(*z_operand(0, BANK, BANK), 0, low[7 % LOW_BUFS][:].bitcast(BF16))
+        z_w[0] = held([P, M_OUT], U32, "span")
+        quantise(*z_operand(0, 0, M_OUT), 0, wide_low[:].bitcast(BF16))
         wd_w[0] = held([P, N], U32, "bearers%d" % (LAST % 2))[:]
-        quantise(wd_w[0], wd_s[0], 0, low[5 % LOW_BUFS][:].bitcast(BF16))
+        quantise(wd_w[0], wd_s[0], 0, low[5 % LOW_BUFS].bitcast(BF16))
         scatter(LAST)
         for m0, width in PIECES:
             score_pass(0, m0, width)

@@ -28,7 +28,7 @@ TILES = H // P
 LAST = TILES - 1
 CHUNK = 256
 PIECES = ((0, 256), (256, 256), (512, 256), (768, 128), (896, 128))
-PAGE_BUFS = 5
+PAGE_BUFS = 8
 WH_ROW = 4
 LOW_BUFS = 4
 
@@ -123,19 +123,18 @@ def tile_list_limb_cut_advice_kernel(
         wh_c = load_words("wh_c", wh_i32[:, PASS:H])
         wg_c = load_words("wg_c", wg_i32[:, 2 * P : PASS])
         load_page(2)
+        wd_raw = {1: held([P, PACK, N], F32, "wd_raw1")}
+        for t in range(PACK):
+            nc.sync.dma_start(out=wd_raw[1][:, t, :], in_=dealt_rows(wd[PASS:H, :], t))
         load_page(3)
-        wgs_rows = [wgs_natural] * PACK
-        wd_raw = {}
+        wgs_rows = [wgs_natural] * PACK + [load_wgs_dealt(0)]
 
-        def load_later(i):
-            wgs_rows.append(load_wgs_dealt(i))
-            load_page(i + PACK)
-            if i == 0:
-                wd_raw[1] = held([P, PACK, N], F32, "wd_raw1")
-                for t in range(PACK):
-                    nc.sync.dma_start(out=wd_raw[1][:, t, :], in_=dealt_rows(wd[PASS:H, :], t))
-            if i == 1:
-                wd_raw[0] = load_rows_of_four("tab_w", wd[0:PASS, :])
+        def load_rest():
+            wd_raw[0] = load_rows_of_four("tab_w", wd[0:PASS, :])
+            for t in range(1, PACK):
+                load_page(PACK + t - 1)
+                wgs_rows.append(load_wgs_dealt(t))
+            load_page(LAST)
 
         ident = held([P, P], F32, "ident")
         make_identity(nc, ident[:])
@@ -199,6 +198,7 @@ def tile_list_limb_cut_advice_kernel(
         wh_d = held([P, PASS], I32, "wh_d")
         wg_d = held([P, PASS // 2], I32, "wg_d")
 
+        load_rest()
         deal_columns(nc.gpsimd, w_sd[:].bitcast(I32), w_s[:, PASS:H].bitcast(I32))
 
         def weights(i):
@@ -218,14 +218,14 @@ def tile_list_limb_cut_advice_kernel(
         high = held([P, S], F32, "high")
         sig = held([P, S], F32, "sig")
         span = held([P, S], F32, "span")
-        wide_low = held([P, 2 * S], F32, "wide_low")
-        low = [held([P, S], F32, "low%d" % s)[:] for s in range(LOW_BUFS - 1)] + [wide_low[:, BANK : BANK + S]]
+        low = [held([P, S], F32, "low%d" % s)[:] for s in range(LOW_BUFS)]
         tail = held([P, 2, S], F32, "tail")
         weighted = [held([P, S], F32, "weighted0")[:], tail[:, 0, :]]
         wd_w = {1: held([P, N], U32, "wd_w1")[:]}
         bearers = [held([P, S], F32, "bearers%d" % s)[:] for s in range(2)]
-        diff = held([P, (LAST - 1) * M_OUT], F32, "diff")
-        dealt = held([P, PACK * M_OUT], F32, "dealt")
+        diff = held([P, PACK * M_OUT], F32, "diff")
+        turned = held([P, TILES * PASS], BF16, "turned")
+        z0_grouped = held([P, M_OUT * PACK], BF16, "z0_grouped")
 
         def first_products():
             w = weights(0)
@@ -319,8 +319,26 @@ def tile_list_limb_cut_advice_kernel(
         def round_z(source, grouped, slots):
             nc.scalar.activation(by_four(grouped)[:, :, slots, :], rows_by_four(source), ACT.Abs)
 
-        dealt_rows_z = dealt[:].rearrange("p (t m) -> p t m", t=PACK)
-        diff_rows = diff[:].rearrange("p (t m) -> p t m", t=LAST - 1)
+        diff_rows = diff[:].rearrange("p (t m) -> p t m", t=PACK)
+
+        def turn_z(i):
+            rows = turned[:].rearrange("p (g r) -> p g r", r=PASS)[:, :, P * i : P * (i + 1)]
+            for a in range(2):
+                for blk in blocks:
+                    nc.tensor.transpose(gate_bank[a][:, blk], diff_rows[:, i, halves[a]][:, blk], ident[:])
+                nc.scalar.activation(
+                    rows[:, PACK * a : PACK * (a + 1), :], gate_bank[a][:].rearrange("p (g r) -> p g r", r=P), ACT.Abs
+                )
+
+        def turn_back_z():
+            pairs = turned[:].bitcast(F32).rearrange("p (g q u) -> p g u q", u=2, q=P)
+            for x, bank in enumerate(high_bank + low_bank):
+                for y, blk in enumerate(blocks):
+                    nc.tensor.transpose(bank[:, blk], pairs[:, 2 * x + y // 2, y % 2, :], ident[:])
+                nc.scalar.copy(
+                    z0_grouped[:].bitcast(F32)[:, x * BANK : (x + 1) * BANK].rearrange("p (g m u) -> p g m u", g=2, u=2),
+                    bank[:].rearrange("p (g u m) -> p g m u", g=2, u=2),
+                )
 
         def stage(n):
             spent = low[(n + 1) % LOW_BUFS].bitcast(BF16)
@@ -331,10 +349,6 @@ def tile_list_limb_cut_advice_kernel(
                     nc.scalar.copy(
                         by_four(spent[:, x * PACK : (x + CHUNK) * PACK]), rows_by_four(wd_raw[4 - n][:, :, x : x + CHUNK])
                     )
-            if n == 6:
-                for a in (1, 0):
-                    grouped = wide_low[:, a * S : (a + 1) * S].bitcast(BF16)
-                    round_z(dealt_rows_z[:, :, halves[a]], grouped, slice(0, PACK))
 
         def quantise_staged(n):
             spent = low[(n + 1) % LOW_BUFS].bitcast(BF16)
@@ -375,13 +389,14 @@ def tile_list_limb_cut_advice_kernel(
             if n < LAST:
                 difference(n + 1)
             weigh(n)
+            if 0 < i <= PACK:
+                turn_z(i - 1)
+            if i > 1:
+                stage(i)
             scatter(i)
             fetch_bearers(i, 0, bearers[i % 2])
             if i < LAST - 1:
-                fetch_limbs(i, 0, bearers[i % 2], diff_rows[:, i, :])
-            if i < PACK:
-                nc.sync.dma_start(out=dealt_rows_z[QUAD * i : QUAD * (i + 1)], in_=diff_rows[:, i, :])
-                load_later(i)
+                fetch_limbs(i, 0, bearers[i % 2], diff_rows[:, i % PACK, :])
             quantise_staged(i)
             if i == 0:
                 deal_columns(nc.vector, wh_d[:], wh_c[:])
@@ -394,16 +409,18 @@ def tile_list_limb_cut_advice_kernel(
                 gate(n + 1)
             if n + 1 < LAST:
                 low_reading(n + 2)
-            stage(n)
+            if n == 1:
+                stage(n)
+        turn_back_z()
         last_wgs, last_h = wgs_rows[LAST][:].bitcast(BF16), sig[:].bitcast(BF16)
         late = {
             0: last_wgs[:, 0:S], 256: last_wgs[:, S : 2 * S], 512: last_h[:, 0:S],
             768: last_h[:, S : S + BANK], 896: last_h[:, S + BANK : 2 * S],
         }
         for m0, width in PIECES:
-            round_z(diff_rows[:, PACK : PACK + 2, m0 : m0 + width], late[m0], slice(0, 2))
+            round_z(diff_rows[:, 0:2, m0 : m0 + width], late[m0], slice(0, 2))
         z_w[0] = held([P, M_OUT], U32, "span")
-        quantise(*z_operand(0, 0, M_OUT), 0, wide_low[:].bitcast(BF16))
+        quantise(*z_operand(0, 0, M_OUT), 0, z0_grouped[:])
         wd_w[0] = held([P, N], U32, "bearers%d" % (LAST % 2))[:]
         quantise(wd_w[0], wd_s[0], 0, low[5 % LOW_BUFS].bitcast(BF16))
         scatter(LAST)
@@ -412,7 +429,7 @@ def tile_list_limb_cut_advice_kernel(
 
         spare = wl_raw_dealt[:].rearrange("p j c -> p (j c)")
         staged = [spare[:, x * BANK : (x + 1) * BANK] for x in range(4)]
-        staged = staged + [dealt[:, 2 * M_OUT + x * BANK : 2 * M_OUT + (x + 1) * BANK] for x in range(4)]
+        staged = staged + [turned[:].bitcast(F32)[:, x * BANK : (x + 1) * BANK] for x in range(4)]
 
         def store(m0, width, part, copy):
             per_bank = BANK // width
@@ -430,7 +447,7 @@ def tile_list_limb_cut_advice_kernel(
         for x, (m0, width) in enumerate(PIECES):
             c0 = m0 - m0 % CHUNK
             if c0 < 2 * CHUNK:
-                last_bearers = diff_rows[:, 0, c0 : c0 + CHUNK]
+                last_bearers = diff_rows[:, 2, c0 : c0 + CHUNK]
                 pair = tail[:, :, c0 : c0 + CHUNK]
             else:
                 last_bearers = tail[:, 0, c0 - 2 * CHUNK : c0 - CHUNK]

@@ -29,7 +29,7 @@ LAST = TILES - 1
 CHUNK = 256
 PIECES = ((0, 256), (256, 256), (512, 256), (768, 128), (896, 128))
 PAGE_BUFS = 8
-WH_ROW = 4
+FOLDED = 4
 LOW_BUFS = 4
 
 
@@ -62,11 +62,6 @@ def tile_list_limb_cut_advice_kernel(
                     out=plane[QUAD * q : QUAD * (q + 1), :].bitcast(I32),
                     in_=rows[0, 4 * q : 4 * q + 4, :].bitcast(I32).partition_broadcast(QUAD // 4),
                 )
-
-        def load_live_rows(rows, first):
-            for q in range(QUADS):
-                p0 = QUAD * q + first
-                nc.sync.dma_start(out=w_s[p0 : p0 + 4, :].bitcast(I32), in_=rows[0, 4 * q : 4 * q + 4, :].bitcast(I32))
 
         def load_rows_of_four(name, src):
             raw = held([P, PACK, src.shape[1]], F32, name)
@@ -102,18 +97,20 @@ def tile_list_limb_cut_advice_kernel(
         load_scale_rows(tab_s, tab_scales, (nc.scalar, nc.sync))
         tab_w = held([P, T], U32, "tab_w")
         nc.scalar.dma_start(out=tab_w[:].bitcast(I32), in_=tab_words[0].rearrange("p t i -> p (t i)").bitcast(I32))
-        w_s = held([P, H], U8, "w_s")
-        nc.gpsimd.memset(w_s[:].bitcast(I32), 0)
-        wl_raw0 = load_rows_of_four("wl_raw0", wl[:, 0:P])
+        wg_s = held([P, H], U8, "wg_s")
+        wh_s = held([P, H], U8, "wh_s")
+        load_scale_rows(wh_s, wh_scales, (nc.gpsimd,), (3,))
+        load_scale_rows(wg_s, wg_scales, (nc.sync,), (0, 1))
+        wl_raw01 = load_rows_of_four("wl_raw01", wl[:, 0 : 2 * P])
+        load_scale_rows(wg_s, wg_scales, (nc.sync,), (2, 3))
         wg_a = load_words("wg_a", wg_i32[:, 0:P])
-        load_live_rows(wg_scales, 0)
         wh_a = load_words("wh_a", wh_i32[:, 0 : 2 * P])
-        load_live_rows(wh_scales, WH_ROW)
-        wl_raw123 = load_rows_of_four("wl_raw123", wl[:, P:PASS])
+        load_scale_rows(wh_s, wh_scales, (nc.sync,), (0, 1, 2))
+        wl_raw23 = load_rows_of_four("wl_raw23", wl[:, 2 * P : PASS])
         wgs_natural = held([P, S], F32, "wgs_natural")
         nc.sync.dma_start(out=wgs_natural[:], in_=wgs)
-        load_page(0)
         nc.sync.dma_start(lists["offs2"][:], offs2)
+        load_page(0)
         wh_b = load_words("wh_b", wh_i32[:, 2 * P : PASS])
         wg_b = load_words("wg_b", wg_i32[:, P : 2 * P])
         nc.sync.dma_start(lists["offs4"][:], offs4)
@@ -142,10 +139,10 @@ def tile_list_limb_cut_advice_kernel(
         v_s = held([P, S], U8, "v_s")
         wl_w = held([P, H], U32, "wl_w")
         wl_s = held([P, H], U8, "wl_s")
-        wd_s = [held([P, N], U8, "wd_s%d" % b)[:] for b in range(2)]
+        wd_s = held([P, 2 * N], U8, "wd_s")
         z_w = {1: held([P, M_OUT], U32, "z_w1")}
         z_s = held([P, 2 * M_OUT], U8, "z_s")
-        wl_grouped = held([P, PASS * PACK], BF16, "wl_grouped")
+        wl_grouped = held([P, 2 * P * PACK], BF16, "wl_grouped")
 
         def by_four(grouped):
             return grouped.rearrange("p (c i j) -> p c j i", i=PACK, j=PACK)
@@ -166,16 +163,6 @@ def tile_list_limb_cut_advice_kernel(
         def round_on_scalar(grouped, raw):
             negated(by_four(grouped), rows_by_four(raw))
 
-        def round_on_gpsimd(grouped, raw):
-            nc.gpsimd.tensor_scalar(
-                grouped.rearrange("p (c j) -> p c j", j=PACK), raw.rearrange("p j c -> p c j"), -1.0, 0.0, ALU.mult, ALU.add
-            )
-
-        def prepare_wl(raw, c0, rounding):
-            grouped = wl_grouped[:, c0 * PACK : (c0 + raw.shape[2]) * PACK]
-            rounding(grouped, raw)
-            quantise(wl_w, wl_s, c0, grouped)
-
         def round_wl_dealt(grouped):
             for t in range(PACK):
                 negated(
@@ -192,23 +179,26 @@ def tile_list_limb_cut_advice_kernel(
         nc.vector.tensor_copy(v_s[:], tab_s[:].indirect(lists["offs"][:]))
         v_w = [held([P, BANK], U32, "v_w%d" % a) for a in range(2)]
         nc.vector.tensor_copy(v_w[0][:], tab_w[:].indirect(offsets("offs", 0, BANK)))
-        prepare_wl(wl_raw0[:], 0, round_on_scalar)
+        round_on_scalar(wl_grouped[:, 0:PASS], wl_raw01[:, :, 0:P])
+        quantise(wl_w, wl_s, 0, wl_grouped[:, 0:PASS])
         nc.vector.tensor_copy(v_w[1][:], tab_w[:].indirect(offsets("offs", BANK, BANK)))
-        w_sd = held([P, PASS], U8, "w_sd")
+        wh_sd = held([P, PASS], U8, "wh_sd")
+        wg_sd = held([P, PASS], U8, "wg_sd")
         wh_d = held([P, PASS], I32, "wh_d")
         wg_d = held([P, PASS // 2], I32, "wg_d")
 
         load_rest()
-        deal_columns(nc.gpsimd, w_sd[:].bitcast(I32), w_s[:, PASS:H].bitcast(I32))
+        deal_columns(nc.gpsimd, wh_sd[:].bitcast(I32), wh_s[:, PASS:H].bitcast(I32))
+        deal_columns(nc.gpsimd, wg_sd[:].bitcast(I32), wg_s[:, PASS:H].bitcast(I32))
 
         def weights(i):
             cols = slice(P * i, P * (i + 1))
             if i < PACK:
                 wh_t, wg_t, x = (wh_a, wg_a, i) if i < 2 else (wh_b, wg_b, i - 2)
-                high_scales, gate_scales = w_s[WH_ROW:P, cols], w_s[:, cols]
+                high_scales, gate_scales = wh_s[:, cols], wg_s[:, cols]
             else:
                 wh_t, wg_t, x = wh_d, wg_d, i - PACK
-                high_scales, gate_scales = w_sd[WH_ROW:P, P * x : P * (x + 1)], w_sd[:, P * x : P * (x + 1)]
+                high_scales, gate_scales = wh_sd[:, P * x : P * (x + 1)], wg_sd[:, P * x : P * (x + 1)]
             return {
                 "gate": (wg_t[:, x * P // 2 : (x + 1) * P // 2].bitcast(U8).bitcast(FP4X4), gate_scales),
                 "low": (wl_w[:, cols].bitcast(FP8X4), wl_s[:, cols]),
@@ -218,10 +208,10 @@ def tile_list_limb_cut_advice_kernel(
         high = held([P, S], F32, "high")
         sig = held([P, S], F32, "sig")
         span = held([P, S], F32, "span")
-        low = [held([P, S], F32, "low%d" % s)[:] for s in range(LOW_BUFS)]
+        low_pair = held([P, 2 * S], F32, "low_pair")
+        low = [low_pair[:, 0:S], low_pair[:, S : 2 * S]] + [held([P, S], F32, "low%d" % s)[:] for s in range(2, LOW_BUFS)]
         tail = held([P, 2, S], F32, "tail")
         weighted = [held([P, S], F32, "weighted0")[:], tail[:, 0, :]]
-        wd_w = {1: held([P, N], U32, "wd_w1")[:]}
         bearers = [held([P, S], F32, "bearers%d" % s)[:] for s in range(2)]
         diff = held([P, PACK * M_OUT], F32, "diff")
         turned = held([P, TILES * PASS], BF16, "turned")
@@ -230,25 +220,25 @@ def tile_list_limb_cut_advice_kernel(
         def first_products():
             w = weights(0)
             for a in range(2):
-                for bank, name in ((gate_bank, "gate"), (sum_bank, "low"), (high_bank, "high")):
-                    nc.tensor.matmul_mx(
-                        bank[a][:], lhsT=w[name][0], lhsT_scale=w[name][1],
-                        rhs=v_w[a][:].bitcast(FP8X4), rhs_scale=v_s[:, halves[a]], start=True, stop=True,
-                    )
+                for bank, names in ((gate_bank, ("gate",)), (high_bank, ("high", "low")), (sum_bank, ("low",))):
+                    for name in names:
+                        nc.tensor.matmul_mx(
+                            bank[a][:], lhsT=w[name][0], lhsT_scale=w[name][1],
+                            rhs=v_w[a][:].bitcast(FP8X4), rhs_scale=v_s[:, halves[a]],
+                            start=(name == names[0]), stop=(name == names[-1]),
+                        )
                 nc.scalar.activation(sig0[:, halves[a]], gate_bank[a][:], ACT.Sigmoid)
-                negated(low0[:, halves[a]], sum_bank[a][:])
 
         def first_interpolation():
             for a in range(2):
-                nc.vector.tensor_tensor(h0[:, halves[a]], high_bank[a][:], low0[:, halves[a]], ALU.subtract)
-                nc.vector.tensor_tensor(h0[:, halves[a]], h0[:, halves[a]], sig0[:, halves[a]], ALU.mult)
+                nc.vector.tensor_tensor(h0[:, halves[a]], high_bank[a][:], sig0[:, halves[a]], ALU.mult)
                 nc.vector.tensor_tensor(h0[:, halves[a]], h0[:, halves[a]], sum_bank[a][:], ALU.subtract)
 
         def first_weighing():
             for a in range(2):
                 nc.vector.tensor_tensor(weighted[0][:, halves[a]], h0[:, halves[a]], wgs_natural[:, halves[a]], ALU.mult)
 
-        low0, sig0, h0 = weighted[1], tail[:, 1, :], low[0]
+        sig0, h0 = tail[:, 1, :], low[0]
 
         def product(i, names, a, bank, empty, into):
             for blk in blocks:
@@ -261,21 +251,23 @@ def tile_list_limb_cut_advice_kernel(
                     )
             empty(into[:, halves[a]], bank[:])
 
-        def minus(subtrahend):
-            return lambda into, source: nc.vector.tensor_tensor(into, source, subtrahend, ALU.subtract)
-
         def sigmoid(into, source):
             nc.scalar.activation(into, source, ACT.Sigmoid)
 
+        def subtracted(i):
+            return (1,) if i <= FOLDED else (1, 0)
+
         def high_reading(i):
-            product(i, ("high",), 1, (high_bank if i < 3 else sum_bank)[1], nc.scalar.copy, high)
+            for a in subtracted(i):
+                product(i, ("high",), a, (high_bank if i < 3 else sum_bank)[a], nc.scalar.copy, high)
 
         def low_reading(i):
             for a in (1, 0):
                 product(i, ("low",), a, (low_bank if i < 3 else gate_bank)[a], negated, low[i % LOW_BUFS])
 
         def folded_difference(i):
-            product(i, ("high", "low"), 0, sum_bank[0], nc.scalar.copy, span)
+            if i <= FOLDED:
+                product(i, ("high", "low"), 0, (high_bank if i < 2 else sum_bank)[0], nc.scalar.copy, span)
 
         def gate(i):
             for a in (1, 0):
@@ -289,7 +281,8 @@ def tile_list_limb_cut_advice_kernel(
                 )
 
         def difference(i):
-            nc.gpsimd.tensor_tensor(span[:, halves[1]], high[:, halves[1]], low[i % LOW_BUFS][:, halves[1]], ALU.subtract)
+            cols = halves[1] if i <= FOLDED else slice(0, S)
+            nc.gpsimd.tensor_tensor(span[:, cols], high[:, cols], low[i % LOW_BUFS][:, cols], ALU.subtract)
 
         def open_sums(i):
             for a in (1, 0):
@@ -354,31 +347,33 @@ def tile_list_limb_cut_advice_kernel(
             spent = low[(n + 1) % LOW_BUFS].bitcast(BF16)
             if n == 1:
                 quantise(wl_w, wl_s, PASS, spent)
-            if n == 3:
-                quantise(wd_w[1], wd_s[1], 0, spent)
 
         def score_pass(b, m0, width):
             per_bank = BANK // width
             for nb in range(N // P):
                 part, side = divmod(nb, per_bank)
-                cols = slice(nb * P, (nb + 1) * P)
+                cols = slice((1 - b) * N + nb * P, (1 - b) * N + (nb + 1) * P)
                 words, scales = z_operand(b, m0, width)
                 nc.tensor.matmul_mx(
                     banks[m0 // P + part][:, side * width : (side + 1) * width],
-                    lhsT=wd_w[b][:, cols].bitcast(FP8X4), lhsT_scale=wd_s[b][:, cols],
+                    lhsT=wd_w[0][:, cols].bitcast(FP8X4), lhsT_scale=wd_s[:, cols],
                     rhs=words.bitcast(FP8X4), rhs_scale=scales,
                     start=(b == 0 and side == 0), stop=(b == 1 and side == per_bank - 1),
                 )
 
-        prepare_wl(wl_raw123[:, :, 0:P], P, round_on_gpsimd)
-        prepare_wl(wl_raw123[:, :, P : 3 * P], 2 * P, round_on_gpsimd)
+        round_on_scalar(wl_grouped[:, PASS : 2 * PASS], wl_raw01[:, :, P : 2 * P])
+        quantise(wl_w, wl_s, P, wl_grouped[:, PASS : 2 * PASS])
         first_products()
         first_interpolation()
         first_weighing()
+        spent_sigmoid = sig0[:, halves[0]].bitcast(BF16)
+        round_on_scalar(spent_sigmoid, wl_raw23[:])
+        quantise(wl_w, wl_s, 2 * P, spent_sigmoid)
+        high_reading(1)
         low_reading(1)
-        for a in (1, 0):
-            product(1, ("high",), a, high_bank[a], minus(low[1][:, halves[a]]), span)
+        difference(1)
         gate(1)
+        folded_difference(1)
         open_sums(1)
         high_reading(2)
         low_reading(2)
@@ -394,13 +389,17 @@ def tile_list_limb_cut_advice_kernel(
             if i > 1:
                 stage(i)
             scatter(i)
-            fetch_bearers(i, 0, bearers[i % 2])
             if i < LAST - 1:
-                fetch_limbs(i, 0, bearers[i % 2], diff_rows[:, i % PACK, :])
+                for a in range(2):
+                    fetch_bearers(i, a * BANK, bearers[i % 2][:, halves[a]])
+                for a in range(2):
+                    fetch_limbs(i, a * BANK, bearers[i % 2][:, halves[a]], diff_rows[:, i % PACK, halves[a]])
+            else:
+                fetch_bearers(i, 0, bearers[i % 2])
             quantise_staged(i)
             if i == 0:
                 deal_columns(nc.vector, wh_d[:], wh_c[:])
-                deal_columns(nc.vector, wg_d[:], wg_c[:])
+                deal_columns(nc.gpsimd, wg_d[:], wg_c[:])
             if n + 1 < LAST:
                 high_reading(n + 2)
             if n < LAST:
@@ -421,8 +420,9 @@ def tile_list_limb_cut_advice_kernel(
             round_z(diff_rows[:, 0:2, m0 : m0 + width], late[m0], slice(0, 2))
         z_w[0] = held([P, M_OUT], U32, "span")
         quantise(*z_operand(0, 0, M_OUT), 0, z0_grouped[:])
-        wd_w[0] = held([P, N], U32, "bearers%d" % (LAST % 2))[:]
-        quantise(wd_w[0], wd_s[0], 0, low[5 % LOW_BUFS].bitcast(BF16))
+        wd_w = [held([P, 2 * N], U32, "bearers%d" % (LAST % 2))]
+        quantise(wd_w[0], wd_s, 0, low_pair[:].bitcast(BF16))
+
         scatter(LAST)
         for m0, width in PIECES:
             score_pass(0, m0, width)

@@ -28,9 +28,8 @@ TILES = H // P
 LAST = TILES - 1
 CHUNK = 256
 PIECES = ((0, 256), (256, 256), (512, 256), (768, 128), (896, 128))
-PAGE_BUFS = 8
+PAGE_BUFS = TILES
 FOLDED = 4
-LOW_BUFS = 4
 
 
 def tile_list_limb_cut_advice_kernel(
@@ -99,13 +98,12 @@ def tile_list_limb_cut_advice_kernel(
         nc.scalar.dma_start(out=tab_w[:].bitcast(I32), in_=tab_words[0].rearrange("p t i -> p (t i)").bitcast(I32))
         wg_s = held([P, H], U8, "wg_s")
         wh_s = held([P, H], U8, "wh_s")
-        load_scale_rows(wh_s, wh_scales, (nc.gpsimd,), (3,))
+        load_scale_rows(wh_s, wh_scales, (nc.gpsimd,))
         load_scale_rows(wg_s, wg_scales, (nc.sync,), (0, 1))
         wl_raw01 = load_rows_of_four("wl_raw01", wl[:, 0 : 2 * P])
         load_scale_rows(wg_s, wg_scales, (nc.sync,), (2, 3))
         wg_a = load_words("wg_a", wg_i32[:, 0:P])
         wh_a = load_words("wh_a", wh_i32[:, 0 : 2 * P])
-        load_scale_rows(wh_s, wh_scales, (nc.sync,), (0, 1, 2))
         wl_raw23 = load_rows_of_four("wl_raw23", wl[:, 2 * P : PASS])
         wgs_natural = held([P, S], F32, "wgs_natural")
         nc.sync.dma_start(out=wgs_natural[:], in_=wgs)
@@ -208,31 +206,36 @@ def tile_list_limb_cut_advice_kernel(
         high = held([P, S], F32, "high")
         sig = held([P, S], F32, "sig")
         span = held([P, S], F32, "span")
+        minus_low = held([P, BANK], F32, "minus_low")
         low_pair = held([P, 2 * S], F32, "low_pair")
-        low = [low_pair[:, 0:S], low_pair[:, S : 2 * S]] + [held([P, S], F32, "low%d" % s)[:] for s in range(2, LOW_BUFS)]
         tail = held([P, 2, S], F32, "tail")
         weighted = [held([P, S], F32, "weighted0")[:], tail[:, 0, :]]
         bearers = [held([P, S], F32, "bearers%d" % s)[:] for s in range(2)]
         diff = held([P, PACK * M_OUT], F32, "diff")
         turned = held([P, TILES * PASS], BF16, "turned")
         z0_grouped = held([P, M_OUT * PACK], BF16, "z0_grouped")
+        low_odd, low_even = held([P, S], F32, "low_odd")[:], held([P, S], F32, "low_even")[:]
+        low = {i: low_odd if i % 2 else low_even for i in range(TILES)}
+        low[2] = z0_grouped[:].bitcast(F32)[:, 0:S]
+        low[3], low[4] = low_pair[:, 0:S], low_pair[:, S : 2 * S]
 
         def first_products():
             w = weights(0)
             for a in range(2):
-                for bank, names in ((gate_bank, ("gate",)), (high_bank, ("high", "low")), (sum_bank, ("low",))):
+                for bank, names in ((gate_bank, ("gate",)), (high_bank, ("high", "low")), (gate_bank, ("low",))):
                     for name in names:
                         nc.tensor.matmul_mx(
                             bank[a][:], lhsT=w[name][0], lhsT_scale=w[name][1],
                             rhs=v_w[a][:].bitcast(FP8X4), rhs_scale=v_s[:, halves[a]],
                             start=(name == names[0]), stop=(name == names[-1]),
                         )
-                nc.scalar.activation(sig0[:, halves[a]], gate_bank[a][:], ACT.Sigmoid)
+                    if names == ("gate",):
+                        nc.scalar.activation(sig0[:, halves[a]], gate_bank[a][:], ACT.Sigmoid)
 
         def first_interpolation():
             for a in range(2):
                 nc.vector.tensor_tensor(h0[:, halves[a]], high_bank[a][:], sig0[:, halves[a]], ALU.mult)
-                nc.vector.tensor_tensor(h0[:, halves[a]], h0[:, halves[a]], sum_bank[a][:], ALU.subtract)
+                nc.vector.tensor_tensor(h0[:, halves[a]], h0[:, halves[a]], gate_bank[a][:], ALU.subtract)
 
         def first_weighing():
             for a in range(2):
@@ -254,20 +257,30 @@ def tile_list_limb_cut_advice_kernel(
         def sigmoid(into, source):
             nc.scalar.activation(into, source, ACT.Sigmoid)
 
-        def subtracted(i):
-            return (1,) if i <= FOLDED else (1, 0)
-
         def high_reading(i):
-            for a in subtracted(i):
-                product(i, ("high",), a, (high_bank if i < 3 else sum_bank)[a], nc.scalar.copy, high)
+            product(i, ("high",), 1, {1: low_bank, 2: high_bank}.get(i, sum_bank)[1], nc.scalar.copy, high)
+            if i > FOLDED:
+                words, scales = weights(i)["high"]
+                nc.tensor.matmul_mx(
+                    sum_bank[0][:], lhsT=words, lhsT_scale=scales,
+                    rhs=v_w[0][:].bitcast(FP8X4), rhs_scale=v_s[:, halves[0]], start=True, stop=True,
+                )
+                nc.scalar.copy(high[:, halves[0]], sum_bank[0][:])
 
         def low_reading(i):
             for a in (1, 0):
-                product(i, ("low",), a, (low_bank if i < 3 else gate_bank)[a], negated, low[i % LOW_BUFS])
+                product(i, ("low",), a, {1: high_bank, 2: low_bank}.get(i, gate_bank)[a], negated, low[i])
 
         def folded_difference(i):
             if i <= FOLDED:
                 product(i, ("high", "low"), 0, (high_bank if i < 2 else sum_bank)[0], nc.scalar.copy, span)
+            else:
+                for blk in blocks:
+                    nc.tensor.transpose(low_bank[0][:, blk], low[i][:, blk], ident[:])
+                negated(minus_low[:], low_bank[0][:])
+                add_transposed(high_bank[0], high[:, halves[0]], True)
+                add_transposed(high_bank[0], minus_low[:], False)
+                nc.scalar.copy(span[:, halves[0]], high_bank[0][:])
 
         def gate(i):
             for a in (1, 0):
@@ -281,12 +294,12 @@ def tile_list_limb_cut_advice_kernel(
                 )
 
         def difference(i):
-            cols = halves[1] if i <= FOLDED else slice(0, S)
-            nc.gpsimd.tensor_tensor(span[:, cols], high[:, cols], low[i % LOW_BUFS][:, cols], ALU.subtract)
+            cols = halves[1]
+            nc.gpsimd.tensor_tensor(span[:, cols], high[:, cols], low[i][:, cols], ALU.subtract)
 
         def open_sums(i):
             for a in (1, 0):
-                add_transposed(sum_bank[a], low[i % LOW_BUFS][:, halves[a]], True)
+                add_transposed(sum_bank[a], low[i][:, halves[a]], True)
 
         def interpolate(i):
             steps = [bearers[i % 2][:, halves[a]] for a in range(2)]
@@ -334,31 +347,33 @@ def tile_list_limb_cut_advice_kernel(
                 )
 
         def stage(n):
-            spent = low[(n + 1) % LOW_BUFS].bitcast(BF16)
+            spent = low[n + 1].bitcast(BF16)
             if n == 1:
                 round_wl_dealt(spent)
-            if n in (3, 4):
+            if n in (2, 3):
                 for x in range(0, N, CHUNK):
                     nc.scalar.copy(
-                        by_four(spent[:, x * PACK : (x + CHUNK) * PACK]), rows_by_four(wd_raw[4 - n][:, :, x : x + CHUNK])
+                        by_four(spent[:, x * PACK : (x + CHUNK) * PACK]), rows_by_four(wd_raw[3 - n][:, :, x : x + CHUNK])
                     )
 
         def quantise_staged(n):
-            spent = low[(n + 1) % LOW_BUFS].bitcast(BF16)
+            spent = low[n + 1].bitcast(BF16)
             if n == 1:
                 quantise(wl_w, wl_s, PASS, spent)
 
+        def score_bank(m0, part):
+            return banks[(2 * [start for start, width in PIECES].index(m0) + part) % len(banks)]
+
         def score_pass(b, m0, width):
-            per_bank = BANK // width
+            words, scales = z_operand(b, m0, width)
             for nb in range(N // P):
-                part, side = divmod(nb, per_bank)
+                part, side = divmod(nb, 2)
                 cols = slice((1 - b) * N + nb * P, (1 - b) * N + (nb + 1) * P)
-                words, scales = z_operand(b, m0, width)
                 nc.tensor.matmul_mx(
-                    banks[m0 // P + part][:, side * width : (side + 1) * width],
+                    score_bank(m0, part)[:, side * width : (side + 1) * width],
                     lhsT=wd_w[0][:, cols].bitcast(FP8X4), lhsT_scale=wd_s[:, cols],
                     rhs=words.bitcast(FP8X4), rhs_scale=scales,
-                    start=(b == 0 and side == 0), stop=(b == 1 and side == per_bank - 1),
+                    start=(b == 0 and side == 0), stop=(b == 1 and side == 1),
                 )
 
         round_on_scalar(wl_grouped[:, PASS : 2 * PASS], wl_raw01[:, :, P : 2 * P])
@@ -395,15 +410,18 @@ def tile_list_limb_cut_advice_kernel(
                 for a in range(2):
                     fetch_limbs(i, a * BANK, bearers[i % 2][:, halves[a]], diff_rows[:, i % PACK, halves[a]])
             else:
-                fetch_bearers(i, 0, bearers[i % 2])
+                fetch_bearers(i, 0, bearers[i % 2][:, halves[0]])
             quantise_staged(i)
             if i == 0:
                 deal_columns(nc.vector, wh_d[:], wh_c[:])
                 deal_columns(nc.gpsimd, wg_d[:], wg_c[:])
+            if FOLDED <= n < LAST:
+                folded_difference(n + 1)
             if n + 1 < LAST:
                 high_reading(n + 2)
-            if n < LAST:
+            if n < FOLDED:
                 folded_difference(n + 1)
+            if n < LAST:
                 open_sums(n + 1)
                 gate(n + 1)
             if n + 1 < LAST:
@@ -424,21 +442,16 @@ def tile_list_limb_cut_advice_kernel(
         quantise(wd_w[0], wd_s, 0, low_pair[:].bitcast(BF16))
 
         scatter(LAST)
-        for m0, width in PIECES:
+        for m0, width in PIECES[:-1]:
             score_pass(0, m0, width)
 
-        spare = wl_raw_dealt[:].rearrange("p j c -> p (j c)")
-        staged = [spare[:, x * BANK : (x + 1) * BANK] for x in range(4)]
-        staged = staged + [turned[:].bitcast(F32)[:, x * BANK : (x + 1) * BANK] for x in range(4)]
+        spare = (wl_raw_dealt[:].rearrange("p j c -> p (j c)"), turned[:].bitcast(F32))
+        out_rows = out.rearrange("(a s p) m -> a p s m", s=2, p=P)
 
         def store(m0, width, part, copy):
-            per_bank = BANK // width
-            out_rows = out.rearrange("(a s p) m -> a p s m", s=per_bank, p=P)
-            bank = m0 // P + part
-            copy(staged[bank], banks[bank][:])
-            nc.sync.dma_start(
-                out=out_rows[part][:, :, m0 : m0 + width], in_=staged[bank].rearrange("p (s m) -> p s m", s=per_bank)
-            )
+            staged = spare[part][:, 2 * m0 : 2 * (m0 + width)]
+            copy(staged, score_bank(m0, part)[:, 0 : 2 * width])
+            nc.sync.dma_start(out=out_rows[part][:, :, m0 : m0 + width], in_=staged.rearrange("p (s m) -> p s m", s=2))
 
         def finish(m0, width):
             quantise(*z_operand(1, m0, width), 0, late[m0])
@@ -446,25 +459,31 @@ def tile_list_limb_cut_advice_kernel(
 
         for x, (m0, width) in enumerate(PIECES):
             c0 = m0 - m0 % CHUNK
-            if c0 < 2 * CHUNK:
-                last_bearers = diff_rows[:, 2, c0 : c0 + CHUNK]
+            if c0 < BANK:
+                borne = (bearers[(LAST - 1) % 2][:, c0 : c0 + CHUNK], diff_rows[:, 2, c0 : c0 + CHUNK])
                 pair = tail[:, :, c0 : c0 + CHUNK]
             else:
-                last_bearers = tail[:, 0, c0 - 2 * CHUNK : c0 - CHUNK]
-                pair = late[c0 - 2 * CHUNK].bitcast(F32).rearrange("p (s m) -> p s m", s=2)
-            cols = slice(m0 - c0, m0 - c0 + width)
-            if m0 == c0:
-                fetch_bearers(LAST, c0, last_bearers)
-            fetch_limbs(LAST - 1, m0, bearers[(LAST - 1) % 2][:, m0 : m0 + width], pair[:, 0, cols])
-            fetch_limbs(LAST, m0, last_bearers[:, cols], pair[:, 1, cols])
-            round_z(pair[:, :, cols], late[m0], slice(2, PACK))
-            if x > 0:
+                borne = [tail[:, s, c0 - BANK : c0 - BANK + CHUNK] for s in range(2)]
+                spent = late[0 if c0 == BANK else BANK].bitcast(F32)[:, 2 * (m0 - c0) : 2 * (m0 - c0 + width)]
+                pair = spent.rearrange("p (s m) -> p s m", s=2)
+            for s in range(2):
+                if m0 == c0 and (s == 1 or c0 >= BANK):
+                    fetch_bearers(LAST - 1 + s, c0, borne[s])
+            if x == 3:
+                finish(*PIECES[2])
+                store(*PIECES[2], 0, nc.scalar.copy)
+            for s in range(2):
+                fetch_limbs(LAST - 1 + s, m0, borne[s][:, m0 - c0 : m0 - c0 + width], pair[:, s, :])
+            round_z(pair, late[m0], slice(2, PACK))
+            if x in (1, 2, 4):
                 finish(*PIECES[x - 1])
             if 0 < x < 3:
                 for part in range(2):
                     store(*PIECES[x - 1], part, nc.scalar.copy)
+            if x == 2:
+                score_pass(0, *PIECES[-1])
         finish(*PIECES[4])
-        for part in range(2):
-            store(*PIECES[2], part, nc.scalar.copy)
-        store(*PIECES[3], 0, nc.scalar.copy)
-        store(*PIECES[4], 0, nc.vector.tensor_copy)
+        store(*PIECES[2], 1, nc.scalar.copy)
+        for piece in PIECES[3:]:
+            store(*piece, 0, nc.vector.tensor_copy)
+            store(*piece, 1, nc.scalar.copy)

@@ -23,13 +23,12 @@ PASS = P * PACK
 BANK = 512
 QUAD = 32
 QUADS = P // QUAD
-RUN = 8
+RUN = 4
 TILES = H // P
 LAST = TILES - 1
-CHUNK = 256
 PIECES = ((0, 256), (256, 256), (512, 256), (768, 128), (896, 128))
 PAGE_BUFS = TILES
-FOLDED = 4
+FOLDED = 3
 
 
 def tile_list_limb_cut_advice_kernel(
@@ -46,7 +45,7 @@ def tile_list_limb_cut_advice_kernel(
             return keep.tile(shape, dtype, name=name, align_bytes=64)
 
         banks = [psum.tile([P, BANK], F32, name="bank%d" % i) for i in range(8)]
-        high_bank, gate_bank, low_bank, sum_bank = banks[0:2], banks[2:4], banks[4:6], banks[6:8]
+        gate_bank, low_bank, sum_bank, high_bank = banks[0:2], banks[2:4], banks[4:6], banks[6:8]
         halves = [slice(0, BANK), slice(BANK, 2 * BANK)]
         blocks = [slice(x, x + P) for x in range(0, BANK, P)]
 
@@ -85,62 +84,68 @@ def tile_list_limb_cut_advice_kernel(
             rows = page0[P * i : P * (i + 1), :] if i < PACK else dealt_rows(page0[PASS:H, :], i - PACK)
             nc.sync.dma_start(out=pages[i][:], in_=rows)
 
-        def load_wgs_dealt(t):
-            rows = held([P, S], F32, "wgs_dealt%d" % t)
+        def load_wgs_dealt(name, t, cols):
+            rows = held([P, cols.stop - cols.start], F32, name)
             for q in range(QUADS):
-                nc.sync.dma_start(out=rows[QUAD * q : QUAD * (q + 1), :], in_=dealt_rows(wgs, t))
+                nc.sync.dma_start(out=rows[QUAD * q : QUAD * (q + 1), :], in_=dealt_rows(wgs[:, cols], t))
             return rows
 
         nc.sync.dma_start(lists["offs"][:], offs)
         tab_s = held([P, T], U8, "tab_s")
         load_scale_rows(tab_s, tab_scales, (nc.scalar, nc.sync))
-        tab_w = held([P, T], U32, "tab_w")
-        nc.scalar.dma_start(out=tab_w[:].bitcast(I32), in_=tab_words[0].rearrange("p t i -> p (t i)").bitcast(I32))
         wg_s = held([P, H], U8, "wg_s")
         wh_s = held([P, H], U8, "wh_s")
-        load_scale_rows(wh_s, wh_scales, (nc.gpsimd,))
-        load_scale_rows(wg_s, wg_scales, (nc.sync,), (0, 1))
-        wl_raw01 = load_rows_of_four("wl_raw01", wl[:, 0 : 2 * P])
-        load_scale_rows(wg_s, wg_scales, (nc.sync,), (2, 3))
+        load_scale_rows(wh_s, wh_scales, (nc.gpsimd,), (0, 1, 2))
+        load_scale_rows(wg_s, wg_scales, (nc.sync,), (0,))
+        tab_w = held([P, T], U32, "tab_w")
+        nc.scalar.dma_start(out=tab_w[:].bitcast(I32), in_=tab_words[0].rearrange("p t i -> p (t i)").bitcast(I32))
+        wl_raw = [load_rows_of_four("wl_raw0", wl[:, 0:P])]
+        load_scale_rows(wg_s, wg_scales, (nc.sync,), (1, 2, 3))
         wg_a = load_words("wg_a", wg_i32[:, 0:P])
         wh_a = load_words("wh_a", wh_i32[:, 0 : 2 * P])
-        wl_raw23 = load_rows_of_four("wl_raw23", wl[:, 2 * P : PASS])
+        load_scale_rows(wh_s, wh_scales, (nc.sync,), (3,))
+        wl_raw.append(load_rows_of_four("wl_raw12", wl[:, P : 3 * P]))
         wgs_natural = held([P, S], F32, "wgs_natural")
-        nc.sync.dma_start(out=wgs_natural[:], in_=wgs)
-        nc.sync.dma_start(lists["offs2"][:], offs2)
+        nc.sync.dma_start(out=wgs_natural[:, halves[0]], in_=wgs[:, halves[0]])
         load_page(0)
-        wh_b = load_words("wh_b", wh_i32[:, 2 * P : PASS])
+        nc.sync.dma_start(lists["offs2"][:], offs2)
+        nc.sync.dma_start(out=wgs_natural[:, halves[1]], in_=wgs[:, halves[1]])
         wg_b = load_words("wg_b", wg_i32[:, P : 2 * P])
+        wh_b = load_words("wh_b", wh_i32[:, 2 * P : PASS])
+        wl_raw3 = load_rows_of_four("wl_raw3", wl[:, 3 * P : PASS])
+        wl_raw_dealt = load_rows_of_four("wl_raw_dealt", wl[:, PASS:H])
         nc.sync.dma_start(lists["offs4"][:], offs4)
         nc.sync.dma_start(lists["offs3"][:], offs3)
-        wl_raw_dealt = load_rows_of_four("wl_raw_dealt", wl[:, PASS:H])
         load_page(1)
         wh_c = load_words("wh_c", wh_i32[:, PASS:H])
         wg_c = load_words("wg_c", wg_i32[:, 2 * P : PASS])
         load_page(2)
-        wd_raw = {1: held([P, PACK, N], F32, "wd_raw1")}
-        for t in range(PACK):
-            nc.sync.dma_start(out=wd_raw[1][:, t, :], in_=dealt_rows(wd[PASS:H, :], t))
         load_page(3)
-        wgs_rows = [wgs_natural] * PACK + [load_wgs_dealt(0)]
+        whole = slice(0, S)
+        wgs_rows = {i: [wgs_natural[:, halves[a]] for a in range(2)] if i < 2 else [wgs_natural[:]] for i in range(PACK)}
+        wd_raw = {}
 
         def load_rest():
+            wd_raw[1] = held([P, PACK, N], F32, "wd_raw1")
+            for t in range(PACK):
+                nc.sync.dma_start(out=wd_raw[1][:, t, :], in_=dealt_rows(wd[PASS:H, :], t))
             wd_raw[0] = load_rows_of_four("tab_w", wd[0:PASS, :])
-            for t in range(1, PACK):
-                load_page(PACK + t - 1)
-                wgs_rows.append(load_wgs_dealt(t))
-            load_page(LAST)
+            for i in range(PACK, TILES):
+                load_page(i)
+                if i < LAST:
+                    wgs_rows[i] = [load_wgs_dealt("wgs_dealt%d" % i, i - PACK, whole)[:]]
+                else:
+                    wgs_rows[i] = [load_wgs_dealt("wgs_last%d" % a, i - PACK, halves[a])[:] for a in range(2)]
 
         ident = held([P, P], F32, "ident")
         make_identity(nc, ident[:])
 
         v_s = held([P, S], U8, "v_s")
-        wl_w = held([P, H], U32, "wl_w")
         wl_s = held([P, H], U8, "wl_s")
         wd_s = held([P, 2 * N], U8, "wd_s")
-        z_w = {1: held([P, M_OUT], U32, "z_w1")}
         z_s = held([P, 2 * M_OUT], U8, "z_s")
-        wl_grouped = held([P, 2 * P * PACK], BF16, "wl_grouped")
+        z_w = {1: held([P, M_OUT], U32, "z_w1")[:]}
+        wl_w = {}
 
         def by_four(grouped):
             return grouped.rearrange("p (c i j) -> p c j i", i=PACK, j=PACK)
@@ -148,9 +153,8 @@ def tile_list_limb_cut_advice_kernel(
         def rows_by_four(raw):
             return raw.rearrange("p j (c i) -> p c j i", i=PACK)
 
-        def quantise(words, scales, c0, grouped):
-            cols = slice(c0, c0 + grouped.shape[1] // PACK)
-            nc.vector.quantize_mx(out=words[:, cols].bitcast(FP8X4), scales=scales[:, cols], in_=grouped)
+        def quantise(words, scales, grouped):
+            nc.vector.quantize_mx(out=words.bitcast(FP8X4), scales=scales, in_=grouped)
 
         def z_operand(b, m0, width):
             return z_w[b][:, m0 : m0 + width], z_s[:, b * M_OUT + m0 : b * M_OUT + m0 + width]
@@ -163,31 +167,35 @@ def tile_list_limb_cut_advice_kernel(
 
         def round_wl_dealt(grouped):
             for t in range(PACK):
-                negated(
+                nc.gpsimd.tensor_scalar(
                     grouped[:, t * PASS : (t + 1) * PASS].rearrange("p (q s j) -> p q s j", s=RUN, j=PACK),
                     wl_raw_dealt[:].rearrange("p j (q t s) -> p t q s j", t=PACK, s=RUN)[:, t],
+                    -1.0, 0.0, ALU.mult, ALU.add,
                 )
 
-        def deal_columns(engine, into, source):
+        def deal_columns(copy, into, source):
             run = source.shape[1] * RUN // PASS
-            engine.tensor_copy(
-                into.rearrange("p (t q s) -> p t q s", t=PACK, s=run), source.rearrange("p (q t s) -> p t q s", t=PACK, s=run)
-            )
+            copy(into.rearrange("p (t q s) -> p t q s", t=PACK, s=run), source.rearrange("p (q t s) -> p t q s", t=PACK, s=run))
 
-        nc.vector.tensor_copy(v_s[:], tab_s[:].indirect(lists["offs"][:]))
         v_w = [held([P, BANK], U32, "v_w%d" % a) for a in range(2)]
-        nc.vector.tensor_copy(v_w[0][:], tab_w[:].indirect(offsets("offs", 0, BANK)))
-        round_on_scalar(wl_grouped[:, 0:PASS], wl_raw01[:, :, 0:P])
-        quantise(wl_w, wl_s, 0, wl_grouped[:, 0:PASS])
-        nc.vector.tensor_copy(v_w[1][:], tab_w[:].indirect(offsets("offs", BANK, BANK)))
+        wl_grouped = held([P, PACK * PASS], BF16, "wl_grouped")
+        wl_first = held([P, 3 * P], U32, "wl_first")
+        for i in range(3):
+            wl_w[i] = wl_first[:, blocks[i]]
+        for a in range(2):
+            nc.vector.tensor_copy(v_s[:, halves[a]], tab_s[:].indirect(offsets("offs", a * BANK, BANK)))
+            nc.vector.tensor_copy(v_w[a][:], tab_w[:].indirect(offsets("offs", a * BANK, BANK)))
+            cols = slice(a * P, (1 + 2 * a) * P)
+            grouped = wl_grouped[:, cols.start * PACK : cols.stop * PACK]
+            round_on_scalar(grouped, wl_raw[a][:])
+            quantise(wl_first[:, cols], wl_s[:, cols], grouped)
         wh_sd = held([P, PASS], U8, "wh_sd")
         wg_sd = held([P, PASS], U8, "wg_sd")
-        wh_d = held([P, PASS], I32, "wh_d")
-        wg_d = held([P, PASS // 2], I32, "wg_d")
+        dealt = {}
 
         load_rest()
-        deal_columns(nc.gpsimd, wh_sd[:].bitcast(I32), wh_s[:, PASS:H].bitcast(I32))
-        deal_columns(nc.gpsimd, wg_sd[:].bitcast(I32), wg_s[:, PASS:H].bitcast(I32))
+        deal_columns(nc.gpsimd.tensor_copy, wh_sd[:].bitcast(I32), wh_s[:, PASS:H].bitcast(I32))
+        deal_columns(nc.gpsimd.tensor_copy, wg_sd[:].bitcast(I32), wg_s[:, PASS:H].bitcast(I32))
 
         def weights(i):
             cols = slice(P * i, P * (i + 1))
@@ -195,58 +203,57 @@ def tile_list_limb_cut_advice_kernel(
                 wh_t, wg_t, x = (wh_a, wg_a, i) if i < 2 else (wh_b, wg_b, i - 2)
                 high_scales, gate_scales = wh_s[:, cols], wg_s[:, cols]
             else:
-                wh_t, wg_t, x = wh_d, wg_d, i - PACK
+                wh_t, wg_t, x = dealt["high"], dealt["gate"], i - PACK
                 high_scales, gate_scales = wh_sd[:, P * x : P * (x + 1)], wg_sd[:, P * x : P * (x + 1)]
             return {
-                "gate": (wg_t[:, x * P // 2 : (x + 1) * P // 2].bitcast(U8).bitcast(FP4X4), gate_scales),
-                "low": (wl_w[:, cols].bitcast(FP8X4), wl_s[:, cols]),
-                "high": (wh_t[:, x * P : (x + 1) * P].bitcast(FP8X4), high_scales),
+                "gate": lambda: (wg_t[:, x * P // 2 : (x + 1) * P // 2].bitcast(U8).bitcast(FP4X4), gate_scales),
+                "low": lambda: (wl_w[i].bitcast(FP8X4), wl_s[:, cols]),
+                "high": lambda: (wh_t[:, x * P : (x + 1) * P].bitcast(FP8X4), high_scales),
             }
 
-        high = held([P, S], F32, "high")
-        sig = held([P, S], F32, "sig")
-        span = held([P, S], F32, "span")
-        minus_low = held([P, BANK], F32, "minus_low")
-        low_pair = held([P, 2 * S], F32, "low_pair")
-        tail = held([P, 2, S], F32, "tail")
-        weighted = [held([P, S], F32, "weighted0")[:], tail[:, 0, :]]
-        bearers = [held([P, S], F32, "bearers%d" % s)[:] for s in range(2)]
-        diff = held([P, PACK * M_OUT], F32, "diff")
+        span = {i: held([P, S], F32, "span%d" % i) for i in (1, 2)}
+        low = {i: held([P, S], F32, "low%d" % i) for i in (1, 2)}
+        for i in range(3, TILES):
+            span[i], low[i] = span[i - 2], low[i - 2]
+        step = held([P, S], F32, "step")
+        limbs = held([P, S], F32, "limbs")
+        relay = [held([P, S], F32, "relay%d" % s) for s in range(3)]
+        diff = held([P, 2 * S], F32, "diff")[:].rearrange("p (s m) -> p s m", s=2)
+        sig = {i: diff[:, 1 if i in (2, LAST - 1) else 0, :] for i in range(1, TILES)}
         turned = held([P, TILES * PASS], BF16, "turned")
         z0_grouped = held([P, M_OUT * PACK], BF16, "z0_grouped")
-        low_odd, low_even = held([P, S], F32, "low_odd")[:], held([P, S], F32, "low_even")[:]
-        low = {i: low_odd if i % 2 else low_even for i in range(TILES)}
-        low[2] = z0_grouped[:].bitcast(F32)[:, 0:S]
-        low[3], low[4] = low_pair[:, 0:S], low_pair[:, S : 2 * S]
+        h1 = held([P, BANK], F32, "wl_w3")
+        weighted1 = held([P, S], F32, "wl_w_dealt")
+        h = {i: [relay[i % 3][:, halves[a]] for a in range(2)] for i in range(TILES)}
+        h[1] = [h1[:], relay[1][:, BANK // 2 : BANK // 2 + BANK]]
+        sig0 = diff[:, 1, :]
 
-        def first_products():
+        def weighted(i):
+            return weighted1 if i == 1 else relay[(i + 2) % 3]
+
+        def bearers(i):
+            return relay[(i + 2) % 3 if i else 1]
+
+        def first_tile():
             w = weights(0)
             for a in range(2):
-                for bank, names in ((gate_bank, ("gate",)), (high_bank, ("high", "low")), (gate_bank, ("low",))):
+                for bank, names in ((gate_bank, ("gate",)), (low_bank, ("high", "low")), (sum_bank, ("low",))):
                     for name in names:
+                        words, scales = w[name]()
                         nc.tensor.matmul_mx(
-                            bank[a][:], lhsT=w[name][0], lhsT_scale=w[name][1],
+                            bank[a][:], lhsT=words, lhsT_scale=scales,
                             rhs=v_w[a][:].bitcast(FP8X4), rhs_scale=v_s[:, halves[a]],
                             start=(name == names[0]), stop=(name == names[-1]),
                         )
-                    if names == ("gate",):
-                        nc.scalar.activation(sig0[:, halves[a]], gate_bank[a][:], ACT.Sigmoid)
-
-        def first_interpolation():
+                nc.scalar.activation(sig0[:, halves[a]], gate_bank[a][:], ACT.Sigmoid)
             for a in range(2):
-                nc.vector.tensor_tensor(h0[:, halves[a]], high_bank[a][:], sig0[:, halves[a]], ALU.mult)
-                nc.vector.tensor_tensor(h0[:, halves[a]], h0[:, halves[a]], gate_bank[a][:], ALU.subtract)
-
-        def first_weighing():
-            for a in range(2):
-                nc.vector.tensor_tensor(weighted[0][:, halves[a]], h0[:, halves[a]], wgs_natural[:, halves[a]], ALU.mult)
-
-        sig0, h0 = tail[:, 1, :], low[0]
+                nc.vector.tensor_tensor(h[0][a], low_bank[a][:], sig0[:, halves[a]], ALU.mult)
+                nc.vector.tensor_tensor(h[0][a], h[0][a], sum_bank[a][:], ALU.subtract)
 
         def product(i, names, a, bank, empty, into):
             for blk in blocks:
                 for name in names:
-                    words, scales = weights(i)[name]
+                    words, scales = weights(i)[name]()
                     nc.tensor.matmul_mx(
                         bank[:, blk], lhsT=v_w[a][:, blk].bitcast(FP8X4),
                         lhsT_scale=v_s[:, a * BANK + blk.start : a * BANK + blk.stop],
@@ -257,34 +264,9 @@ def tile_list_limb_cut_advice_kernel(
         def sigmoid(into, source):
             nc.scalar.activation(into, source, ACT.Sigmoid)
 
-        def high_reading(i):
-            product(i, ("high",), 1, {1: low_bank, 2: high_bank}.get(i, sum_bank)[1], nc.scalar.copy, high)
-            if i > FOLDED:
-                words, scales = weights(i)["high"]
-                nc.tensor.matmul_mx(
-                    sum_bank[0][:], lhsT=words, lhsT_scale=scales,
-                    rhs=v_w[0][:].bitcast(FP8X4), rhs_scale=v_s[:, halves[0]], start=True, stop=True,
-                )
-                nc.scalar.copy(high[:, halves[0]], sum_bank[0][:])
-
-        def low_reading(i):
-            for a in (1, 0):
-                product(i, ("low",), a, {1: high_bank, 2: low_bank}.get(i, gate_bank)[a], negated, low[i])
-
-        def folded_difference(i):
-            if i <= FOLDED:
-                product(i, ("high", "low"), 0, (high_bank if i < 2 else sum_bank)[0], nc.scalar.copy, span)
-            else:
-                for blk in blocks:
-                    nc.tensor.transpose(low_bank[0][:, blk], low[i][:, blk], ident[:])
-                negated(minus_low[:], low_bank[0][:])
-                add_transposed(high_bank[0], high[:, halves[0]], True)
-                add_transposed(high_bank[0], minus_low[:], False)
-                nc.scalar.copy(span[:, halves[0]], high_bank[0][:])
-
         def gate(i):
-            for a in (1, 0):
-                product(i, ("gate",), a, gate_bank[a], sigmoid, sig)
+            for a in range(2):
+                product(i, ("gate",), a, gate_bank[a], sigmoid, sig[i])
 
         def add_transposed(bank, source, opens):
             for blk in blocks:
@@ -293,52 +275,74 @@ def tile_list_limb_cut_advice_kernel(
                     start=(opens and blk.start == 0), stop=(not opens and blk.stop == BANK),
                 )
 
-        def difference(i):
-            cols = halves[1]
-            nc.gpsimd.tensor_tensor(span[:, cols], high[:, cols], low[i][:, cols], ALU.subtract)
+        def high_reading(i):
+            names = ("high", "low") if i < FOLDED else ("high",)
+            for a in range(2):
+                product(i, names, a, high_bank[a], nc.scalar.copy, span[i])
 
-        def open_sums(i):
-            for a in (1, 0):
-                add_transposed(sum_bank[a], low[i][:, halves[a]], True)
+        def readings(i):
+            high_reading(i)
+            low_reading(i)
+
+        def low_reading(i):
+            for a in range(2):
+                product(i, ("low",), a, (low_bank if i < PACK else gate_bank if i == PACK else high_bank)[a], negated, low[i])
 
         def interpolate(i):
-            steps = [bearers[i % 2][:, halves[a]] for a in range(2)]
-            for a in (1, 0):
-                nc.gpsimd.tensor_tensor(steps[a], span[:, halves[a]], sig[:, halves[a]], ALU.mult)
-                add_transposed(sum_bank[a], steps[a], False)
-            for a in (1, 0):
-                nc.scalar.copy(sig[:, halves[a]], sum_bank[a][:])
+            for a in range(2):
+                add_transposed(sum_bank[a], low[i][:, halves[a]], True)
+            for a in range(2 if i >= FOLDED else 0):
+                nc.gpsimd.tensor_tensor(span[i][:, halves[a]], span[i][:, halves[a]], low[i][:, halves[a]], ALU.subtract)
+            for a in range(2):
+                nc.gpsimd.tensor_tensor(step[:, halves[a]], span[i][:, halves[a]], sig[i][:, halves[a]], ALU.mult)
+                add_transposed(sum_bank[a], step[:, halves[a]], False)
+                nc.scalar.copy(h[i][a], sum_bank[a][:])
 
         def weigh(i):
-            for a in (1, 0):
-                nc.gpsimd.tensor_tensor(weighted[i % 2][:, halves[a]], sig[:, halves[a]], wgs_rows[i][:, halves[a]], ALU.mult)
+            if len(wgs_rows[i]) == 1:
+                nc.gpsimd.tensor_tensor(weighted(i)[:], relay[i % 3][:], wgs_rows[i][0], ALU.mult)
+            else:
+                for a in range(2):
+                    nc.gpsimd.tensor_tensor(weighted(i)[:, halves[a]], h[i][a], wgs_rows[i][a], ALU.mult)
 
-        def scatter(i):
-            nc.vector.tensor_copy(pages[i][:].indirect(lists["offs2"][:]), weighted[i % 2])
+        def scatter(i, m0, width):
+            nc.vector.tensor_copy(pages[i][:].indirect(offsets("offs2", m0, width)), weighted(i)[:, m0 : m0 + width])
 
-        def fetch_bearers(i, m0, into):
-            nc.vector.tensor_copy(into, pages[i][:].indirect(offsets("offs4", m0, into.shape[1])))
+        def fetch(i, name, m0, into):
+            nc.vector.tensor_copy(into, pages[i][:].indirect(offsets(name, m0, into.shape[1])))
 
         def fetch_limbs(i, m0, minus, into):
             nc.vector.tensor_tensor(into, pages[i][:].indirect(offsets("offs3", m0, into.shape[1])), minus, ALU.subtract)
 
+        def fetch_bearers(i):
+            if i < PACK:
+                for a in range(2):
+                    nc.vector.tensor_scalar(
+                        bearers(i)[:, halves[a]], pages[i][:].indirect(offsets("offs4", a * BANK, BANK)),
+                        -1.0, 0.0, ALU.mult, ALU.add,
+                    )
+            else:
+                fetch(i, "offs4", 0, bearers(i)[:])
+
+        def subtract(i):
+            nc.gpsimd.tensor_tensor(diff[:, i - PACK, :], limbs[:], bearers(i)[:], ALU.subtract)
+
         def round_z(source, grouped, slots):
             nc.scalar.activation(by_four(grouped)[:, :, slots, :], rows_by_four(source), ACT.Abs)
-
-        diff_rows = diff[:].rearrange("p (t m) -> p t m", t=PACK)
 
         def turn_z(i):
             rows = turned[:].rearrange("p (g r) -> p g r", r=PASS)[:, :, P * i : P * (i + 1)]
             for a in range(2):
-                for blk in blocks:
-                    nc.tensor.transpose(gate_bank[a][:, blk], diff_rows[:, i, halves[a]][:, blk], ident[:])
+                add_transposed(sum_bank[a], bearers(i)[:, halves[a]], True)
+            for a in range(2):
+                add_transposed(sum_bank[a], limbs[:, halves[a]], False)
                 nc.scalar.activation(
-                    rows[:, PACK * a : PACK * (a + 1), :], gate_bank[a][:].rearrange("p (g r) -> p g r", r=P), ACT.Abs
+                    rows[:, PACK * a : PACK * (a + 1), :], sum_bank[a][:].rearrange("p (g r) -> p g r", r=P), ACT.Abs
                 )
 
         def turn_back_z():
             pairs = turned[:].bitcast(F32).rearrange("p (g q u) -> p g u q", u=2, q=P)
-            for x, bank in enumerate(high_bank + low_bank):
+            for x, bank in enumerate(low_bank + high_bank):
                 for y, blk in enumerate(blocks):
                     nc.tensor.transpose(bank[:, blk], pairs[:, 2 * x + y // 2, y % 2, :], ident[:])
                 nc.scalar.copy(
@@ -346,144 +350,132 @@ def tile_list_limb_cut_advice_kernel(
                     bank[:].rearrange("p (g u m) -> p g m u", g=2, u=2),
                 )
 
-        def stage(n):
-            spent = low[n + 1].bitcast(BF16)
-            if n == 1:
-                round_wl_dealt(spent)
-            if n in (2, 3):
-                for x in range(0, N, CHUNK):
-                    nc.scalar.copy(
-                        by_four(spent[:, x * PACK : (x + CHUNK) * PACK]), rows_by_four(wd_raw[3 - n][:, :, x : x + CHUNK])
-                    )
+        def score_bank(x, part):
+            return banks[(2 * x + part) % len(banks)]
 
-        def quantise_staged(n):
-            spent = low[n + 1].bitcast(BF16)
-            if n == 1:
-                quantise(wl_w, wl_s, PASS, spent)
-
-        def score_bank(m0, part):
-            return banks[(2 * [start for start, width in PIECES].index(m0) + part) % len(banks)]
-
-        def score_pass(b, m0, width):
+        def score_pass(b, x):
+            m0, width = PIECES[x]
             words, scales = z_operand(b, m0, width)
             for nb in range(N // P):
                 part, side = divmod(nb, 2)
-                cols = slice((1 - b) * N + nb * P, (1 - b) * N + (nb + 1) * P)
+                cols = slice(b * N + nb * P, b * N + (nb + 1) * P)
                 nc.tensor.matmul_mx(
-                    score_bank(m0, part)[:, side * width : (side + 1) * width],
-                    lhsT=wd_w[0][:, cols].bitcast(FP8X4), lhsT_scale=wd_s[:, cols],
+                    score_bank(x, part)[:, side * width : (side + 1) * width],
+                    lhsT=late_codes[:, cols].bitcast(FP8X4), lhsT_scale=wd_s[:, cols],
                     rhs=words.bitcast(FP8X4), rhs_scale=scales,
                     start=(b == 0 and side == 0), stop=(b == 1 and side == 1),
                 )
 
-        round_on_scalar(wl_grouped[:, PASS : 2 * PASS], wl_raw01[:, :, P : 2 * P])
-        quantise(wl_w, wl_s, P, wl_grouped[:, PASS : 2 * PASS])
-        first_products()
-        first_interpolation()
-        first_weighing()
-        spent_sigmoid = sig0[:, halves[0]].bitcast(BF16)
-        round_on_scalar(spent_sigmoid, wl_raw23[:])
-        quantise(wl_w, wl_s, 2 * P, spent_sigmoid)
-        high_reading(1)
-        low_reading(1)
-        difference(1)
+        first_tile()
         gate(1)
-        folded_difference(1)
-        open_sums(1)
-        high_reading(2)
-        low_reading(2)
+        readings(1)
+        weigh(0)
+        for a in range(2):
+            scatter(0, a * BANK, BANK)
+        interpolate(1)
+        round_on_scalar(wl_grouped[:, 3 * PASS : PACK * PASS], wl_raw3[:])
+        gate(2)
+        readings(2)
+        gate(3)
+        high_reading(3)
+        fetch(0, "offs3", 0, limbs[:])
+        weigh(1)
+        wl_w[3] = held([P, P], U32, "wl_w3")[:]
+        quantise(wl_w[3], wl_s[:, 3 * P : PASS], wl_grouped[:, 3 * PASS : PACK * PASS])
+        fetch_bearers(0)
+        scatter(1, 0, S)
+        interpolate(2)
+        low_reading(3)
+        round_wl_dealt(sig[2].bitcast(BF16))
+        wl_w_dealt = held([P, PASS], U32, "wl_w_dealt")
+        for t in range(PACK):
+            wl_w[PACK + t] = wl_w_dealt[:, blocks[t]]
+        quantise(wl_w_dealt[:], wl_s[:, PASS:H], sig[2].bitcast(BF16))
+        turn_z(0)
+        weigh(2)
+        dealt_words = held([P, PASS + PASS // 2], U32, "wl_w3_spent")
+        dealt["high"], dealt["gate"] = dealt_words[:, 0:PASS], dealt_words[:, PASS : PASS + PASS // 2]
+        deal_columns(nc.scalar.copy, dealt["high"], wh_c[:].bitcast(U32))
+        deal_columns(nc.scalar.copy, dealt["gate"], wg_c[:].bitcast(U32))
+        fetch(1, "offs3", 0, limbs[:])
+        interpolate(3)
+        gate(4)
+        readings(4)
 
-        for i in range(LAST):
-            n = i + 1
-            interpolate(n)
-            if n < LAST:
-                difference(n + 1)
-            weigh(n)
-            if 0 < i <= PACK:
-                turn_z(i - 1)
-            if i > 1:
-                stage(i)
-            scatter(i)
-            if i < LAST - 1:
-                for a in range(2):
-                    fetch_bearers(i, a * BANK, bearers[i % 2][:, halves[a]])
-                for a in range(2):
-                    fetch_limbs(i, a * BANK, bearers[i % 2][:, halves[a]], diff_rows[:, i % PACK, halves[a]])
-            else:
-                fetch_bearers(i, 0, bearers[i % 2][:, halves[0]])
-            quantise_staged(i)
-            if i == 0:
-                deal_columns(nc.vector, wh_d[:], wh_c[:])
-                deal_columns(nc.gpsimd, wg_d[:], wg_c[:])
-            if FOLDED <= n < LAST:
-                folded_difference(n + 1)
-            if n + 1 < LAST:
-                high_reading(n + 2)
-            if n < FOLDED:
-                folded_difference(n + 1)
-            if n < LAST:
-                open_sums(n + 1)
-                gate(n + 1)
-            if n + 1 < LAST:
-                low_reading(n + 2)
-            if n == 1:
-                stage(n)
-        turn_back_z()
-        last_wgs, last_h = wgs_rows[LAST][:].bitcast(BF16), sig[:].bitcast(BF16)
-        late = {
-            0: last_wgs[:, 0:S], 256: last_wgs[:, S : 2 * S], 512: last_h[:, 0:S],
-            768: last_h[:, S : S + BANK], 896: last_h[:, S + BANK : 2 * S],
-        }
-        for m0, width in PIECES:
-            round_z(diff_rows[:, 0:2, m0 : m0 + width], late[m0], slice(0, 2))
-        z_w[0] = held([P, M_OUT], U32, "span")
-        quantise(*z_operand(0, 0, M_OUT), 0, z0_grouped[:])
-        wd_w = [held([P, 2 * N], U32, "bearers%d" % (LAST % 2))]
-        quantise(wd_w[0], wd_s, 0, low_pair[:].bitcast(BF16))
+        for i in range(2, LAST):
+            scatter(i, 0, S)
+            if 0 < i - 2 < PACK:
+                turn_z(i - 2)
+            if i - 2 >= PACK:
+                subtract(i - 2)
+            weigh(i + 1)
+            if i + 2 <= LAST:
+                interpolate(i + 2)
+            if i + 3 <= LAST:
+                gate(i + 3)
+                readings(i + 3)
+            if i - 2 == PACK - 1:
+                turn_back_z()
+                wd_grouped = [diff[:, 1, :].bitcast(BF16), held([P, N * PACK], BF16, "wl_w3_spent")[:]]
+                for b in range(2):
+                    nc.scalar.copy(by_four(wd_grouped[b]), rows_by_four(wd_raw[b][:]))
+            if i > 2:
+                fetch(i - 1, "offs3", 0, limbs[:])
+            fetch_bearers(i - 1)
 
-        scatter(LAST)
-        for m0, width in PIECES[:-1]:
-            score_pass(0, m0, width)
+        late_codes = held([P, 2 * N + M_OUT], U32, "wgs_last0")
+        z_w[0] = late_codes[:, 2 * N : 2 * N + M_OUT]
+        quantise(*z_operand(0, 0, M_OUT), z0_grouped[:])
+        for b in (1, 0):
+            quantise(late_codes[:, b * N : (b + 1) * N], wd_s[:, b * N : (b + 1) * N], wd_grouped[b])
+        scatter(LAST, 0, S)
+        subtract(LAST - 2)
+        z1_grouped = held([P, M_OUT * PACK], BF16, "wl_raw_dealt")
 
-        spare = (wl_raw_dealt[:].rearrange("p j c -> p (j c)"), turned[:].bitcast(F32))
+        def late(x):
+            m0, width = PIECES[x]
+            return z1_grouped[:, m0 * PACK : (m0 + width) * PACK]
+
+        for half in halves:
+            round_z(diff[:, :, half], z1_grouped[:, half.start * PACK : half.stop * PACK], slice(0, 2))
+        for x in range(len(PIECES) - 1):
+            score_pass(0, x)
+
+        spare = (wd_raw[1][:].rearrange("p j c -> p (j c)"), turned[:].bitcast(F32))
         out_rows = out.rearrange("(a s p) m -> a p s m", s=2, p=P)
 
-        def store(m0, width, part, copy):
-            staged = spare[part][:, 2 * m0 : 2 * (m0 + width)]
-            copy(staged, score_bank(m0, part)[:, 0 : 2 * width])
+        def store(x, part, copy):
+            m0, width = PIECES[x]
+            staged = trio[2 * part] if x == 2 else spare[part][:, 2 * m0 : 2 * (m0 + width)]
+            copy(staged, score_bank(x, part)[:, 0 : 2 * width])
             nc.sync.dma_start(out=out_rows[part][:, :, m0 : m0 + width], in_=staged.rearrange("p (s m) -> p s m", s=2))
 
-        def finish(m0, width):
-            quantise(*z_operand(1, m0, width), 0, late[m0])
-            score_pass(1, m0, width)
+        def finish(x):
+            quantise(*z_operand(1, *PIECES[x]), late(x))
+            score_pass(1, x)
 
+        widest = PIECES[0][1]
+        free_pair = held([P, 2, 2 * widest], F32, "wl_w3_spent")
+        trio = [free_pair[:, 0, :], diff[:, 1, S - 2 * widest : S], free_pair[:, 1, :]]
         for x, (m0, width) in enumerate(PIECES):
-            c0 = m0 - m0 % CHUNK
-            if c0 < BANK:
-                borne = (bearers[(LAST - 1) % 2][:, c0 : c0 + CHUNK], diff_rows[:, 2, c0 : c0 + CHUNK])
-                pair = tail[:, :, c0 : c0 + CHUNK]
-            else:
-                borne = [tail[:, s, c0 - BANK : c0 - BANK + CHUNK] for s in range(2)]
-                spent = late[0 if c0 == BANK else BANK].bitcast(F32)[:, 2 * (m0 - c0) : 2 * (m0 - c0 + width)]
-                pair = spent.rearrange("p (s m) -> p s m", s=2)
+            borne, pair = [
+                trio[(2 * x + y) % 3][:, 0 : 2 * width].rearrange("p (s m) -> p s m", s=2) for y in range(2)
+            ]
             for s in range(2):
-                if m0 == c0 and (s == 1 or c0 >= BANK):
-                    fetch_bearers(LAST - 1 + s, c0, borne[s])
-            if x == 3:
-                finish(*PIECES[2])
-                store(*PIECES[2], 0, nc.scalar.copy)
+                fetch(LAST - 1 + s, "offs4", m0, borne[:, s, :])
             for s in range(2):
-                fetch_limbs(LAST - 1 + s, m0, borne[s][:, m0 - c0 : m0 - c0 + width], pair[:, s, :])
-            round_z(pair, late[m0], slice(2, PACK))
-            if x in (1, 2, 4):
-                finish(*PIECES[x - 1])
+                fetch_limbs(LAST - 1 + s, m0, borne[:, s, :], pair[:, s, :])
+            round_z(pair, late(x), slice(2, PACK))
+            if x > 0:
+                finish(x - 1)
             if 0 < x < 3:
                 for part in range(2):
-                    store(*PIECES[x - 1], part, nc.scalar.copy)
-            if x == 2:
-                score_pass(0, *PIECES[-1])
-        finish(*PIECES[4])
-        store(*PIECES[2], 1, nc.scalar.copy)
-        for piece in PIECES[3:]:
-            store(*piece, 0, nc.vector.tensor_copy)
-            store(*piece, 1, nc.scalar.copy)
+                    store(x - 1, part, nc.scalar.copy)
+            if x == 1:
+                score_pass(0, len(PIECES) - 1)
+        store(2, 1, nc.vector.tensor_copy)
+        store(2, 0, nc.scalar.copy)
+        finish(len(PIECES) - 1)
+        for x in (3, 4):
+            store(x, 0, nc.vector.tensor_copy)
+            store(x, 1, nc.scalar.copy)

@@ -61,9 +61,9 @@ def tile_list_limb_cut_advice_kernel(
                     in_=rows[0, 4 * q : 4 * q + 4, :].bitcast(I32).partition_broadcast(QUAD // 4),
                 )
 
-        def load_rows_of_four(name, src):
+        def load_rows_of_four(name, src, queue=nc.sync):
             raw = held([P, PACK, src.shape[1]], F32, name)
-            nc.sync.dma_start(out=raw[:], in_=src.rearrange("(p j) c -> p j c", j=PACK))
+            queue.dma_start(out=raw[:], in_=src.rearrange("(p j) c -> p j c", j=PACK))
             return raw
 
         wh_i32 = wh_words[0].rearrange("p c i -> p (c i)").bitcast(I32)
@@ -95,16 +95,15 @@ def tile_list_limb_cut_advice_kernel(
         load_scale_rows(tab_s, tab_scales, (nc.scalar, nc.sync))
         wg_s = held([P, H], U8, "wg_s")
         wh_s = held([P, H], U8, "wh_s")
-        load_scale_rows(wh_s, wh_scales, (nc.gpsimd,), (0, 1, 2))
         load_scale_rows(wg_s, wg_scales, (nc.sync,), (0,))
         tab_w = held([P, T], U32, "tab_w")
         nc.scalar.dma_start(out=tab_w[:].bitcast(I32), in_=tab_words[0].rearrange("p t i -> p (t i)").bitcast(I32))
-        wl_raw = [load_rows_of_four("wl_raw0", wl[:, 0:P])]
+        wl_raw01 = load_rows_of_four("wl_raw01", wl[:, 0 : 2 * P], nc.scalar)
         load_scale_rows(wg_s, wg_scales, (nc.sync,), (1, 2, 3))
         wg_a = load_words("wg_a", wg_i32[:, 0:P])
+        load_scale_rows(wh_s, wh_scales, (nc.sync,))
         wh_a = load_words("wh_a", wh_i32[:, 0 : 2 * P])
-        load_scale_rows(wh_s, wh_scales, (nc.sync,), (3,))
-        wl_raw.append(load_rows_of_four("wl_raw12", wl[:, P : 3 * P]))
+        wl_raw23 = load_rows_of_four("wl_raw23", wl[:, 2 * P : PASS])
         wgs_natural = held([P, S], F32, "wgs_natural")
         nc.sync.dma_start(out=wgs_natural[:, halves[0]], in_=wgs[:, halves[0]])
         load_page(0)
@@ -112,7 +111,6 @@ def tile_list_limb_cut_advice_kernel(
         nc.sync.dma_start(out=wgs_natural[:, halves[1]], in_=wgs[:, halves[1]])
         wg_b = load_words("wg_b", wg_i32[:, P : 2 * P])
         wh_b = load_words("wh_b", wh_i32[:, 2 * P : PASS])
-        wl_raw3 = load_rows_of_four("wl_raw3", wl[:, 3 * P : PASS])
         wl_raw_dealt = load_rows_of_four("wl_raw_dealt", wl[:, PASS:H])
         nc.sync.dma_start(lists["offs4"][:], offs4)
         nc.sync.dma_start(lists["offs3"][:], offs3)
@@ -177,18 +175,17 @@ def tile_list_limb_cut_advice_kernel(
             run = source.shape[1] * RUN // PASS
             copy(into.rearrange("p (t q s) -> p t q s", t=PACK, s=run), source.rearrange("p (q t s) -> p t q s", t=PACK, s=run))
 
-        v_w = [held([P, BANK], U32, "v_w%d" % a) for a in range(2)]
-        wl_grouped = held([P, PACK * PASS], BF16, "wl_grouped")
-        wl_first = held([P, 3 * P], U32, "wl_first")
-        for i in range(3):
+        wl_first = held([P, PASS], U32, "wl_first")
+        for i in range(PACK):
             wl_w[i] = wl_first[:, blocks[i]]
+        v_w = []
+        nc.vector.tensor_copy(v_s[:], tab_s[:].indirect(lists["offs"][:]))
         for a in range(2):
-            nc.vector.tensor_copy(v_s[:, halves[a]], tab_s[:].indirect(offsets("offs", a * BANK, BANK)))
+            v_w.append(held([P, BANK], U32, "v_w%d" % a))
             nc.vector.tensor_copy(v_w[a][:], tab_w[:].indirect(offsets("offs", a * BANK, BANK)))
-            cols = slice(a * P, (1 + 2 * a) * P)
-            grouped = wl_grouped[:, cols.start * PACK : cols.stop * PACK]
-            round_on_scalar(grouped, wl_raw[a][:])
-            quantise(wl_first[:, cols], wl_s[:, cols], grouped)
+            grouped = held([P, PASS], BF16, "wl_grouped1" if a else "v_w1")[:]
+            round_on_scalar(grouped, wl_raw01[:, :, blocks[a]])
+            quantise(wl_w[a], wl_s[:, blocks[a]], grouped)
         wh_sd = held([P, PASS], U8, "wh_sd")
         wg_sd = held([P, PASS], U8, "wg_sd")
         dealt = {}
@@ -222,10 +219,8 @@ def tile_list_limb_cut_advice_kernel(
         sig = {i: diff[:, 1 if i in (2, LAST - 1) else 0, :] for i in range(1, TILES)}
         turned = held([P, TILES * PASS], BF16, "turned")
         z0_grouped = held([P, M_OUT * PACK], BF16, "z0_grouped")
-        h1 = held([P, BANK], F32, "wl_w3")
         weighted1 = held([P, S], F32, "wl_w_dealt")
         h = {i: [relay[i % 3][:, halves[a]] for a in range(2)] for i in range(TILES)}
-        h[1] = [h1[:], relay[1][:, BANK // 2 : BANK // 2 + BANK]]
         sig0 = diff[:, 1, :]
 
         def weighted(i):
@@ -237,7 +232,7 @@ def tile_list_limb_cut_advice_kernel(
         def first_tile():
             w = weights(0)
             for a in range(2):
-                for bank, names in ((gate_bank, ("gate",)), (low_bank, ("high", "low")), (sum_bank, ("low",))):
+                for bank, names in ((gate_bank, ("gate",)), (low_bank, ("low", "high")), (sum_bank, ("low",))):
                     for name in names:
                         words, scales = w[name]()
                         nc.tensor.matmul_mx(
@@ -366,22 +361,23 @@ def tile_list_limb_cut_advice_kernel(
                     start=(b == 0 and side == 0), stop=(b == 1 and side == 1),
                 )
 
+        grouped23 = weighted(0)[:, halves[1]].bitcast(BF16)
+        round_on_scalar(grouped23, wl_raw23[:])
         first_tile()
+        nc.vector.tensor_tensor(weighted(0)[:, halves[0]], h[0][0], wgs_rows[0][0], ALU.mult)
+        quantise(wl_first[:, 2 * P : PASS], wl_s[:, 2 * P : PASS], grouped23)
         gate(1)
         readings(1)
-        weigh(0)
+        nc.gpsimd.tensor_tensor(weighted(0)[:, halves[1]], h[0][1], wgs_rows[0][1], ALU.mult)
         for a in range(2):
             scatter(0, a * BANK, BANK)
         interpolate(1)
-        round_on_scalar(wl_grouped[:, 3 * PASS : PACK * PASS], wl_raw3[:])
         gate(2)
         readings(2)
         gate(3)
         high_reading(3)
         fetch(0, "offs3", 0, limbs[:])
         weigh(1)
-        wl_w[3] = held([P, P], U32, "wl_w3")[:]
-        quantise(wl_w[3], wl_s[:, 3 * P : PASS], wl_grouped[:, 3 * PASS : PACK * PASS])
         fetch_bearers(0)
         scatter(1, 0, S)
         interpolate(2)

@@ -95,13 +95,14 @@ def tile_list_limb_cut_advice_kernel(
         load_scale_rows(tab_s, tab_scales, (nc.scalar, nc.sync))
         wg_s = held([P, H], U8, "wg_s")
         wh_s = held([P, H], U8, "wh_s")
+        load_scale_rows(wh_s, wh_scales, (nc.gpsimd,), (0, 1))
         load_scale_rows(wg_s, wg_scales, (nc.sync,), (0,))
         tab_w = held([P, T], U32, "tab_w")
         nc.scalar.dma_start(out=tab_w[:].bitcast(I32), in_=tab_words[0].rearrange("p t i -> p (t i)").bitcast(I32))
         wl_raw01 = load_rows_of_four("wl_raw01", wl[:, 0 : 2 * P], nc.scalar)
         load_scale_rows(wg_s, wg_scales, (nc.sync,), (1, 2, 3))
         wg_a = load_words("wg_a", wg_i32[:, 0:P])
-        load_scale_rows(wh_s, wh_scales, (nc.sync,))
+        load_scale_rows(wh_s, wh_scales, (nc.sync,), (2, 3))
         wh_a = load_words("wh_a", wh_i32[:, 0 : 2 * P])
         wl_raw23 = load_rows_of_four("wl_raw23", wl[:, 2 * P : PASS])
         wgs_natural = held([P, S], F32, "wgs_natural")
@@ -178,14 +179,13 @@ def tile_list_limb_cut_advice_kernel(
         wl_first = held([P, PASS], U32, "wl_first")
         for i in range(PACK):
             wl_w[i] = wl_first[:, blocks[i]]
-        v_w = []
         nc.vector.tensor_copy(v_s[:], tab_s[:].indirect(lists["offs"][:]))
+        v_w = [held([P, BANK], U32, "v_w%d" % a) for a in range(2)]
         for a in range(2):
-            v_w.append(held([P, BANK], U32, "v_w%d" % a))
             nc.vector.tensor_copy(v_w[a][:], tab_w[:].indirect(offsets("offs", a * BANK, BANK)))
-            grouped = held([P, PASS], BF16, "wl_grouped1" if a else "v_w1")[:]
-            round_on_scalar(grouped, wl_raw01[:, :, blocks[a]])
-            quantise(wl_w[a], wl_s[:, blocks[a]], grouped)
+        grouped01 = held([P, 2 * PASS], BF16, "grouped01")
+        nc.vector.tensor_scalar(by_four(grouped01[:]), rows_by_four(wl_raw01[:]), -1.0, None, ALU.mult)
+        quantise(wl_first[:, 0 : 2 * P], wl_s[:, 0 : 2 * P], grouped01[:])
         wh_sd = held([P, PASS], U8, "wh_sd")
         wg_sd = held([P, PASS], U8, "wg_sd")
         dealt = {}
@@ -220,19 +220,20 @@ def tile_list_limb_cut_advice_kernel(
         turned = held([P, TILES * PASS], BF16, "turned")
         z0_grouped = held([P, M_OUT * PACK], BF16, "z0_grouped")
         weighted1 = held([P, S], F32, "wl_w_dealt")
-        h = {i: [relay[i % 3][:, halves[a]] for a in range(2)] for i in range(TILES)}
+        home = {i: relay[i % 3 if i < PACK else (1 - i) % 3] for i in range(TILES)}
+        h = {i: [home[i][:, halves[a]] for a in range(2)] for i in range(TILES)}
         sig0 = diff[:, 1, :]
 
         def weighted(i):
-            return weighted1 if i == 1 else relay[(i + 2) % 3]
+            return {0: relay[2], 1: weighted1, PACK: relay[1]}.get(i, home.get(i - 1))
 
         def bearers(i):
-            return relay[(i + 2) % 3 if i else 1]
+            return {0: z0_grouped[:].bitcast(F32)[:, 0:S], 1: relay[1]}.get(i, home[i + 2])
 
         def first_tile():
             w = weights(0)
             for a in range(2):
-                for bank, names in ((gate_bank, ("gate",)), (low_bank, ("low", "high")), (sum_bank, ("low",))):
+                for bank, names in ((gate_bank, ("gate",)), (low_bank, ("high", "low")), (sum_bank, ("high",))):
                     for name in names:
                         words, scales = w[name]()
                         nc.tensor.matmul_mx(
@@ -240,10 +241,10 @@ def tile_list_limb_cut_advice_kernel(
                             rhs=v_w[a][:].bitcast(FP8X4), rhs_scale=v_s[:, halves[a]],
                             start=(name == names[0]), stop=(name == names[-1]),
                         )
-                nc.scalar.activation(sig0[:, halves[a]], gate_bank[a][:], ACT.Sigmoid)
+                nc.scalar.activation(sig0[:, halves[a]], gate_bank[a][:], ACT.Sigmoid, scale=-1.0)
             for a in range(2):
                 nc.vector.tensor_tensor(h[0][a], low_bank[a][:], sig0[:, halves[a]], ALU.mult)
-                nc.vector.tensor_tensor(h[0][a], h[0][a], sum_bank[a][:], ALU.subtract)
+                nc.vector.tensor_tensor(h[0][a], sum_bank[a][:], h[0][a], ALU.subtract)
 
         def product(i, names, a, bank, empty, into):
             for blk in blocks:
@@ -295,7 +296,7 @@ def tile_list_limb_cut_advice_kernel(
 
         def weigh(i):
             if len(wgs_rows[i]) == 1:
-                nc.gpsimd.tensor_tensor(weighted(i)[:], relay[i % 3][:], wgs_rows[i][0], ALU.mult)
+                nc.gpsimd.tensor_tensor(weighted(i)[:], home[i][:], wgs_rows[i][0], ALU.mult)
             else:
                 for a in range(2):
                     nc.gpsimd.tensor_tensor(weighted(i)[:, halves[a]], h[i][a], wgs_rows[i][a], ALU.mult)
@@ -362,8 +363,8 @@ def tile_list_limb_cut_advice_kernel(
                 )
 
         grouped23 = weighted(0)[:, halves[1]].bitcast(BF16)
-        round_on_scalar(grouped23, wl_raw23[:])
         first_tile()
+        round_on_scalar(grouped23, wl_raw23[:])
         nc.vector.tensor_tensor(weighted(0)[:, halves[0]], h[0][0], wgs_rows[0][0], ALU.mult)
         quantise(wl_first[:, 2 * P : PASS], wl_s[:, 2 * P : PASS], grouped23)
         gate(1)

@@ -311,14 +311,7 @@ def tile_list_limb_cut_advice_kernel(
             nc.vector.tensor_tensor(into, pages[i][:].indirect(offsets("offs3", m0, into.shape[1])), minus, ALU.subtract)
 
         def fetch_bearers(i):
-            if i < PACK:
-                for a in range(2):
-                    nc.vector.tensor_scalar(
-                        bearers(i)[:, halves[a]], pages[i][:].indirect(offsets("offs4", a * BANK, BANK)),
-                        -1.0, 0.0, ALU.mult, ALU.add,
-                    )
-            else:
-                fetch(i, "offs4", 0, bearers(i)[:])
+            fetch(i, "offs4", 0, bearers(i)[:])
 
         def subtract(i):
             nc.gpsimd.tensor_tensor(diff[:, i - PACK, :], limbs[:], bearers(i)[:], ALU.subtract)
@@ -329,7 +322,8 @@ def tile_list_limb_cut_advice_kernel(
         def turn_z(i):
             rows = turned[:].rearrange("p (g r) -> p g r", r=PASS)[:, :, P * i : P * (i + 1)]
             for a in range(2):
-                add_transposed(sum_bank[a], bearers(i)[:, halves[a]], True)
+                add_transposed(sum_bank[a], limbs[:, halves[a]], True)
+                negated(limbs[:, halves[a]], bearers(i)[:, halves[a]])
             for a in range(2):
                 add_transposed(sum_bank[a], limbs[:, halves[a]], False)
                 nc.scalar.activation(

@@ -27,6 +27,7 @@ RUN = 4
 TILES = H // P
 LAST = TILES - 1
 PIECES = ((0, 256), (256, 256), (512, 256), (768, 128), (896, 128))
+SHIFT = 16
 PAGE_BUFS = TILES
 FOLDED = 3
 
@@ -208,14 +209,16 @@ def tile_list_limb_cut_advice_kernel(
                 "high": lambda: (wh_t[:, x * P : (x + 1) * P].bitcast(FP8X4), high_scales),
             }
 
+        spent = held([P, 3 * S], F32, "diff")[:]
         span = {i: held([P, S], F32, "span%d" % i) for i in (1, 2)}
         low = {i: held([P, S], F32, "low%d" % i) for i in (1, 2)}
         for i in range(3, TILES):
             span[i], low[i] = span[i - 2], low[i - 2]
+        span[LAST - 1] = spent[:, 2 * S : 3 * S]
         step = held([P, S], F32, "step")
         limbs = held([P, S], F32, "limbs")
         relay = [held([P, S], F32, "relay%d" % s) for s in range(3)]
-        diff = held([P, 2 * S], F32, "diff")[:].rearrange("p (s m) -> p s m", s=2)
+        diff = spent[:, 0 : 2 * S].rearrange("p (s m) -> p s m", s=2)
         sig = {i: diff[:, 1 if i in (2, LAST - 1) else 0, :] for i in range(1, TILES)}
         turned = held([P, TILES * PASS], BF16, "turned")
         z0_grouped = held([P, M_OUT * PACK], BF16, "z0_grouped")
@@ -407,9 +410,10 @@ def tile_list_limb_cut_advice_kernel(
                 readings(i + 3)
             if i - 2 == PACK - 1:
                 turn_back_z()
-                wd_grouped = [diff[:, 1, :].bitcast(BF16), held([P, N * PACK], BF16, "wl_w3_spent")[:]]
-                for b in range(2):
-                    nc.scalar.copy(by_four(wd_grouped[b]), rows_by_four(wd_raw[b][:]))
+                wd_grouped = spent[:, S : 3 * S].bitcast(BF16)
+                for c0 in range(0, 2 * N, P):
+                    b, cols = c0 // N, blocks[c0 % N // P]
+                    nc.scalar.copy(by_four(wd_grouped[:, c0 * PACK : (c0 + P) * PACK]), rows_by_four(wd_raw[b][:, :, cols]))
             if i > 2:
                 fetch(i - 1, "offs3", 0, limbs[:])
             fetch_bearers(i - 1)
@@ -417,8 +421,7 @@ def tile_list_limb_cut_advice_kernel(
         late_codes = held([P, 2 * N + M_OUT], U32, "wgs_last0")
         z_w[0] = late_codes[:, 2 * N : 2 * N + M_OUT]
         quantise(*z_operand(0, 0, M_OUT), z0_grouped[:])
-        for b in (1, 0):
-            quantise(late_codes[:, b * N : (b + 1) * N], wd_s[:, b * N : (b + 1) * N], wd_grouped[b])
+        quantise(late_codes[:, 0 : 2 * N], wd_s[:], wd_grouped)
         scatter(LAST, 0, S)
         subtract(LAST - 2)
         z1_grouped = held([P, M_OUT * PACK], BF16, "wl_raw_dealt")
@@ -437,7 +440,7 @@ def tile_list_limb_cut_advice_kernel(
 
         def store(x, part, copy):
             m0, width = PIECES[x]
-            staged = trio[2 * part] if x == 2 else spare[part][:, 2 * m0 : 2 * (m0 + width)]
+            staged = held_back.get((x, part), spare[part][:, 2 * m0 : 2 * (m0 + width)])
             copy(staged, score_bank(x, part)[:, 0 : 2 * width])
             nc.sync.dma_start(out=out_rows[part][:, :, m0 : m0 + width], in_=staged.rearrange("p (s m) -> p s m", s=2))
 
@@ -445,17 +448,20 @@ def tile_list_limb_cut_advice_kernel(
             quantise(*z_operand(1, *PIECES[x]), late(x))
             score_pass(1, x)
 
-        widest = PIECES[0][1]
-        free_pair = held([P, 2, 2 * widest], F32, "wl_w3_spent")
-        trio = [free_pair[:, 0, :], diff[:, 1, S - 2 * widest : S], free_pair[:, 1, :]]
+        first = spent[:, 2 * S : 3 * S]
+        wide = PIECES[0][1]
+        pairs = [spent[:, S + BANK : 2 * S], spent[:, BANK:S], first[:, wide : 3 * wide]]
+        pairs += [first[:, 0:wide], first[:, wide : 2 * wide]]
+        gathers = {0: (BANK, first), 2: (wide, pairs[0]), 3: (wide, pairs[1])}
+        held_back = {(2, 0): pairs[2], (2, 1): pairs[1]}
         for x, (m0, width) in enumerate(PIECES):
-            borne, pair = [
-                trio[(2 * x + y) % 3][:, 0 : 2 * width].rearrange("p (s m) -> p s m", s=2) for y in range(2)
-            ]
+            pair = pairs[x].rearrange("p (s m) -> p s m", s=2)
+            if x in gathers:
+                start, borne = m0, gathers[x][1].rearrange("p (s m) -> p s m", s=2)
+                for s in range(2):
+                    fetch(LAST - 1 + s, "offs4", m0, borne[:, s, :])
             for s in range(2):
-                fetch(LAST - 1 + s, "offs4", m0, borne[:, s, :])
-            for s in range(2):
-                fetch_limbs(LAST - 1 + s, m0, borne[:, s, :], pair[:, s, :])
+                fetch_limbs(LAST - 1 + s, m0, borne[:, s, m0 - start : m0 - start + width], pair[:, s, :])
             round_z(pair, late(x), slice(2, PACK))
             if x > 0:
                 finish(x - 1)

@@ -187,8 +187,8 @@ def tile_list_limb_cut_advice_kernel(
         grouped01 = held([P, 2 * PASS], BF16, "grouped01")
         nc.vector.tensor_scalar(by_four(grouped01[:]), rows_by_four(wl_raw01[:]), -1.0, None, ALU.mult)
         quantise(wl_first[:, 0 : 2 * P], wl_s[:, 0 : 2 * P], grouped01[:])
-        wh_sd = held([P, PASS], U8, "wh_sd")
-        wg_sd = held([P, PASS], U8, "wg_sd")
+        dealt_scales = held([P, H], U8, "grouped01")
+        wh_sd, wg_sd = dealt_scales[:, 0:PASS], dealt_scales[:, PASS:H]
         dealt = {}
 
         load_rest()

@@ -26,9 +26,8 @@ QUADS = P // QUAD
 RUN = 4
 TILES = H // P
 LAST = TILES - 1
+QUARTER = S // 4
 PIECES = ((0, 256), (256, 256), (512, 256), (768, 128), (896, 128))
-SHIFT = 16
-PAGE_BUFS = TILES
 FOLDED = 3
 
 
@@ -39,28 +38,28 @@ def tile_list_limb_cut_advice_kernel(
     nc = tc.nc
     with ExitStack() as ctx:
         keep = ctx.enter_context(tc.tile_pool(name="keep", bufs=1))
-        ring = ctx.enter_context(tc.tile_pool(name="ring", bufs=PAGE_BUFS))
         psum = ctx.enter_context(tc.psum_pool(name="psum", bufs=1))
 
         def held(shape, dtype, name):
             return keep.tile(shape, dtype, name=name, align_bytes=64)
 
         banks = [psum.tile([P, BANK], F32, name="bank%d" % i) for i in range(8)]
-        gate_bank, low_bank, sum_bank, high_bank = banks[0:2], banks[2:4], banks[4:6], banks[6:8]
+        gate_bank, low_bank = (banks[0], banks[2]), (banks[1], banks[3])
+        sum_bank, high_bank = (banks[4], banks[6]), (banks[5], banks[7])
         halves = [slice(0, BANK), slice(BANK, 2 * BANK)]
         blocks = [slice(x, x + P) for x in range(0, BANK, P)]
+        quarters = [slice(x, x + QUARTER) for x in range(0, S, QUARTER)]
 
         lists = {name: held([P, S // 16], U16, name) for name in ("offs", "offs2", "offs3", "offs4")}
 
         def offsets(name, start, count):
             return lists[name][:, start // 16 : (start + count) // 16]
 
-        def load_scale_rows(plane, rows, queues, quads=range(QUADS)):
-            for q in quads:
-                queues[q % len(queues)].dma_start(
-                    out=plane[QUAD * q : QUAD * (q + 1), :].bitcast(I32),
-                    in_=rows[0, 4 * q : 4 * q + 4, :].bitcast(I32).partition_broadcast(QUAD // 4),
-                )
+        def load_scale_rows(plane, rows, queue, q):
+            queue.dma_start(
+                out=plane[QUAD * q : QUAD * (q + 1), :].bitcast(I32),
+                in_=rows[0, 4 * q : 4 * q + 4, :].bitcast(I32).partition_broadcast(QUAD // 4),
+            )
 
         def load_rows_of_four(name, src, queue=nc.sync):
             raw = held([P, PACK, src.shape[1]], F32, name)
@@ -70,59 +69,60 @@ def tile_list_limb_cut_advice_kernel(
         wh_i32 = wh_words[0].rearrange("p c i -> p (c i)").bitcast(I32)
         wg_i32 = wg_words[0].bitcast(I32)
 
-        def load_words(name, src):
-            words = held([P, src.shape[1]], I32, name)
-            nc.sync.dma_start(out=words[:], in_=src)
-            return words
+        def load_plain(name, src, dtype, queue=nc.sync):
+            into = held([P, src.shape[1]], dtype, name)
+            queue.dma_start(out=into[:], in_=src)
+            return into
 
         def dealt_rows(src, t):
             return src.rearrange("(q t s) c -> t q s c", t=PACK, s=RUN)[t]
 
         pages = {}
 
-        def load_page(i):
-            pages[i] = ring.tile([P, T2], F32, name="page")
+        def load_page(i, queue=nc.sync):
+            pages[i] = held([P, T2], F32, "page%d" % i)
             rows = page0[P * i : P * (i + 1), :] if i < PACK else dealt_rows(page0[PASS:H, :], i - PACK)
-            nc.sync.dma_start(out=pages[i][:], in_=rows)
+            queue.dma_start(out=pages[i][:], in_=rows)
 
-        def load_wgs_dealt(name, t, cols):
-            rows = held([P, cols.stop - cols.start], F32, name)
+        def load_wgs_dealt(rows, t):
             for q in range(QUADS):
-                nc.sync.dma_start(out=rows[QUAD * q : QUAD * (q + 1), :], in_=dealt_rows(wgs[:, cols], t))
+                nc.sync.dma_start(out=rows[QUAD * q : QUAD * (q + 1), :], in_=dealt_rows(wgs, t))
             return rows
 
-        nc.sync.dma_start(lists["offs"][:], offs)
         tab_s = held([P, T], U8, "tab_s")
-        load_scale_rows(tab_s, tab_scales, (nc.scalar, nc.sync))
         wg_s = held([P, H], U8, "wg_s")
         wh_s = held([P, H], U8, "wh_s")
-        load_scale_rows(wh_s, wh_scales, (nc.gpsimd,), (0, 1))
-        load_scale_rows(wg_s, wg_scales, (nc.sync,), (0,))
+        nc.sync.dma_start(lists["offs"][:], offs)
+        for q in range(QUADS):
+            load_scale_rows(tab_s, tab_scales, (nc.scalar, nc.sync)[q % 2], q)
+        for q in (1, 2, 3):
+            load_scale_rows(wh_s, wh_scales, nc.gpsimd, q)
+        wl_raw = {0: load_rows_of_four("wl_raw0", wl[:, 0:P], nc.scalar)}
+        wg_first = load_plain("wg_first", wg_i32[:, 0 : P // 2], I32)
         tab_w = held([P, T], U32, "tab_w")
-        nc.scalar.dma_start(out=tab_w[:].bitcast(I32), in_=tab_words[0].rearrange("p t i -> p (t i)").bitcast(I32))
-        wl_raw01 = load_rows_of_four("wl_raw01", wl[:, 0 : 2 * P], nc.scalar)
-        load_scale_rows(wg_s, wg_scales, (nc.sync,), (1, 2, 3))
-        wg_a = load_words("wg_a", wg_i32[:, 0:P])
-        load_scale_rows(wh_s, wh_scales, (nc.sync,), (2, 3))
-        wh_a = load_words("wh_a", wh_i32[:, 0 : 2 * P])
-        wl_raw23 = load_rows_of_four("wl_raw23", wl[:, 2 * P : PASS])
-        wgs_natural = held([P, S], F32, "wgs_natural")
-        nc.sync.dma_start(out=wgs_natural[:, halves[0]], in_=wgs[:, halves[0]])
-        load_page(0)
+        nc.sync.dma_start(out=tab_w[:].bitcast(I32), in_=tab_words[0].rearrange("p t i -> p (t i)").bitcast(I32))
+        for q in range(QUADS):
+            load_scale_rows(wg_s, wg_scales, nc.sync, q)
+        wh_first = load_plain("wh_first", wh_i32[:, 0:P], I32)
+        load_scale_rows(wh_s, wh_scales, nc.sync, 0)
+        wgs_natural = load_plain("wgs_natural", wgs, F32)
         nc.sync.dma_start(lists["offs2"][:], offs2)
-        nc.sync.dma_start(out=wgs_natural[:, halves[1]], in_=wgs[:, halves[1]])
-        wg_b = load_words("wg_b", wg_i32[:, P : 2 * P])
-        wh_b = load_words("wh_b", wh_i32[:, 2 * P : PASS])
-        wl_raw_dealt = load_rows_of_four("wl_raw_dealt", wl[:, PASS:H])
-        nc.sync.dma_start(lists["offs4"][:], offs4)
+        wl_raw[1] = load_rows_of_four("wl_raw1", wl[:, P : 2 * P])
+        load_page(0)
+        wh_rest = load_plain("wh_rest", wh_i32[:, P:PASS], I32)
+        wg_rest = load_plain("wg_rest", wg_i32[:, P // 2 : PASS // 2], I32)
+        for i in (2, 3):
+            wl_raw[i] = load_rows_of_four("wl_raw%d" % i, wl[:, i * P : (i + 1) * P])
         nc.sync.dma_start(lists["offs3"][:], offs3)
+        nc.sync.dma_start(lists["offs4"][:], offs4)
         load_page(1)
-        wh_c = load_words("wh_c", wh_i32[:, PASS:H])
-        wg_c = load_words("wg_c", wg_i32[:, 2 * P : PASS])
+        wl_raw_dealt = load_rows_of_four("wl_raw_dealt", wl[:, PASS:H])
+        wh_c = load_plain("wh_c", wh_i32[:, PASS:H], I32)
+        wg_c = load_plain("wg_c", wg_i32[:, PASS // 2 : H // 2], I32)
         load_page(2)
         load_page(3)
-        whole = slice(0, S)
-        wgs_rows = {i: [wgs_natural[:, halves[a]] for a in range(2)] if i < 2 else [wgs_natural[:]] for i in range(PACK)}
+        wide_tile = held([P, 3 * S], F32, "wide_tile")
+        wgs_rows = {i: wgs_natural[:] for i in range(PACK)}
         wd_raw = {}
 
         def load_rest():
@@ -132,13 +132,8 @@ def tile_list_limb_cut_advice_kernel(
             wd_raw[0] = load_rows_of_four("tab_w", wd[0:PASS, :])
             for i in range(PACK, TILES):
                 load_page(i)
-                if i < LAST:
-                    wgs_rows[i] = [load_wgs_dealt("wgs_dealt%d" % i, i - PACK, whole)[:]]
-                else:
-                    wgs_rows[i] = [load_wgs_dealt("wgs_last%d" % a, i - PACK, halves[a])[:] for a in range(2)]
-
-        ident = held([P, P], F32, "ident")
-        make_identity(nc, ident[:])
+                rows = held([P, S], F32, "wgs_dealt%d" % i)[:] if i < LAST else wide_tile[:, 2 * S : 3 * S]
+                wgs_rows[i] = load_wgs_dealt(rows, i - PACK)
 
         v_s = held([P, S], U8, "v_s")
         wl_s = held([P, H], U8, "wl_s")
@@ -162,6 +157,9 @@ def tile_list_limb_cut_advice_kernel(
         def negated(into, source):
             nc.scalar.activation(into, source, ACT.Copy, scale=-1.0)
 
+        def sigmoid(into, source):
+            nc.scalar.activation(into, source, ACT.Sigmoid)
+
         def round_on_scalar(grouped, raw):
             negated(by_four(grouped), rows_by_four(raw))
 
@@ -177,132 +175,136 @@ def tile_list_limb_cut_advice_kernel(
             run = source.shape[1] * RUN // PASS
             copy(into.rearrange("p (t q s) -> p t q s", t=PACK, s=run), source.rearrange("p (q t s) -> p t q s", t=PACK, s=run))
 
+        def round_on_gpsimd(grouped, raw):
+            nc.gpsimd.tensor_scalar(
+                grouped.rearrange("p (c j) -> p c j", j=PACK), raw.rearrange("p j c -> p c j"), -1.0, 0.0, ALU.mult, ALU.add
+            )
+
+        grouped0 = held([P, PASS], BF16, "grouped0")
+        round_on_gpsimd(grouped0[:], wl_raw[0][:])
+        ident = held([P, P], F32, "ident")
+        make_identity(nc, ident[:])
+
+        nc.vector.tensor_copy(v_s[:], tab_s[:].indirect(lists["offs"][:]))
+        v_cut = (0, QUARTER, BANK, S)
+
+        def gather_words(a):
+            nc.vector.tensor_copy(v_w[:, v_cut[a] : v_cut[a + 1]], tab_w[:].indirect(offsets("offs", v_cut[a], v_cut[a + 1] - v_cut[a])))
+
+        def v_operand(c0, width):
+            return v_w[:, c0 : c0 + width].bitcast(FP8X4), v_s[:, c0 : c0 + width]
+
         wl_first = held([P, PASS], U32, "wl_first")
         for i in range(PACK):
             wl_w[i] = wl_first[:, blocks[i]]
-        nc.vector.tensor_copy(v_s[:], tab_s[:].indirect(lists["offs"][:]))
-        v_w = [held([P, BANK], U32, "v_w%d" % a) for a in range(2)]
-        for a in range(2):
-            nc.vector.tensor_copy(v_w[a][:], tab_w[:].indirect(offsets("offs", a * BANK, BANK)))
-        grouped01 = held([P, 2 * PASS], BF16, "grouped01")
-        nc.vector.tensor_scalar(by_four(grouped01[:]), rows_by_four(wl_raw01[:]), -1.0, None, ALU.mult)
-        quantise(wl_first[:, 0 : 2 * P], wl_s[:, 0 : 2 * P], grouped01[:])
-        dealt_scales = held([P, H], U8, "grouped01")
+        quantise(wl_w[0], wl_s[:, 0:P], grouped0[:])
+        v_w = held([P, S], U32, "grouped0")
+        for a in range(3):
+            gather_words(a)
+        dealt_scales = held([P, H], U8, "wl_raw0")
         wh_sd, wg_sd = dealt_scales[:, 0:PASS], dealt_scales[:, PASS:H]
         dealt = {}
-
         load_rest()
         deal_columns(nc.gpsimd.tensor_copy, wh_sd[:].bitcast(I32), wh_s[:, PASS:H].bitcast(I32))
         deal_columns(nc.gpsimd.tensor_copy, wg_sd[:].bitcast(I32), wg_s[:, PASS:H].bitcast(I32))
 
-        def weights(i):
+        def weights(i, name):
             cols = slice(P * i, P * (i + 1))
             if i < PACK:
-                wh_t, wg_t, x = (wh_a, wg_a, i) if i < 2 else (wh_b, wg_b, i - 2)
+                wh_t, wg_t, x = (wh_first, wg_first, 0) if i == 0 else (wh_rest, wg_rest, i - 1)
                 high_scales, gate_scales = wh_s[:, cols], wg_s[:, cols]
             else:
                 wh_t, wg_t, x = dealt["high"], dealt["gate"], i - PACK
                 high_scales, gate_scales = wh_sd[:, P * x : P * (x + 1)], wg_sd[:, P * x : P * (x + 1)]
-            return {
-                "gate": lambda: (wg_t[:, x * P // 2 : (x + 1) * P // 2].bitcast(U8).bitcast(FP4X4), gate_scales),
-                "low": lambda: (wl_w[i].bitcast(FP8X4), wl_s[:, cols]),
-                "high": lambda: (wh_t[:, x * P : (x + 1) * P].bitcast(FP8X4), high_scales),
-            }
+            if name == "gate":
+                return wg_t[:, x * P // 2 : (x + 1) * P // 2].bitcast(U8).bitcast(FP4X4), gate_scales
+            if name == "low":
+                return wl_w[i].bitcast(FP8X4), wl_s[:, cols]
+            return wh_t[:, x * P : (x + 1) * P].bitcast(FP8X4), high_scales
 
-        spent = held([P, 3 * S], F32, "diff")[:]
-        span = {i: held([P, S], F32, "span%d" % i) for i in (1, 2)}
-        low = {i: held([P, S], F32, "low%d" % i) for i in (1, 2)}
-        for i in range(3, TILES):
-            span[i], low[i] = span[i - 2], low[i - 2]
-        span[LAST - 1] = spent[:, 2 * S : 3 * S]
+        pair_a, pair_b, pair_c, pair_d = (held([P, S], F32, "pair_" + x) for x in "abcd")
+        side = {i: (i + (i >= FOLDED)) % 2 for i in range(TILES)}
+        sig = {i: (pair_a, pair_b)[side[i]][:] for i in range(TILES)}
+        span = {i: (pair_c, pair_d)[side[i]][:] for i in range(TILES)}
+        double = held([P, 2 * S], F32, "double")
+        sig[2] = double[:, S - QUARTER : 2 * S - QUARTER]
+        low_rows = [held([P, S], F32, "low%d" % s) for s in range(2)]
         step = held([P, S], F32, "step")
-        limbs = held([P, S], F32, "limbs")
-        relay = [held([P, S], F32, "relay%d" % s) for s in range(3)]
-        diff = spent[:, 0 : 2 * S].rearrange("p (s m) -> p s m", s=2)
-        sig = {i: diff[:, 1 if i in (2, LAST - 1) else 0, :] for i in range(1, TILES)}
+        limb_rows = [held([P, S], F32, "limbs%d" % s) for s in range(2)]
+        h_rows = [held([P, S + (1 - s) * QUARTER], F32, "h_rows%d" % s) for s in range(2)]
+        weighted_rows = [held([P, S], F32, "weighted%d" % s) for s in range(2)]
         turned = held([P, TILES * PASS], BF16, "turned")
-        z0_grouped = held([P, M_OUT * PACK], BF16, "z0_grouped")
-        weighted1 = held([P, S], F32, "wl_w_dealt")
-        home = {i: relay[i % 3 if i < PACK else (1 - i) % 3] for i in range(TILES)}
-        h = {i: [home[i][:, halves[a]] for a in range(2)] for i in range(TILES)}
-        sig0 = diff[:, 1, :]
+        fetched = {}
+
+        def low(i):
+            return double[:, S : 2 * S] if i == 3 else low_rows[i % 2][:]
+
+        def h(i):
+            return h_rows[i % 2][:, 0:S]
 
         def weighted(i):
-            return {0: relay[2], 1: weighted1, PACK: relay[1]}.get(i, home.get(i - 1))
+            return double[:, 0:S] if i == 2 else weighted_rows[i % 2][:, 0:S]
 
         def bearers(i):
-            return {0: z0_grouped[:].bitcast(F32)[:, 0:S], 1: relay[1]}.get(i, home[i + 2])
+            return fetched[i][:, S : 2 * S] if i < 2 else h(i + 1)
 
-        def first_tile():
-            w = weights(0)
-            for a in range(2):
-                for bank, names in ((gate_bank, ("gate",)), (low_bank, ("high", "low")), (sum_bank, ("high",))):
-                    for name in names:
-                        words, scales = w[name]()
-                        nc.tensor.matmul_mx(
-                            bank[a][:], lhsT=words, lhsT_scale=scales,
-                            rhs=v_w[a][:].bitcast(FP8X4), rhs_scale=v_s[:, halves[a]],
-                            start=(name == names[0]), stop=(name == names[-1]),
-                        )
-                nc.scalar.activation(sig0[:, halves[a]], gate_bank[a][:], ACT.Sigmoid, scale=-1.0)
-            for a in range(2):
-                nc.vector.tensor_tensor(h[0][a], low_bank[a][:], sig0[:, halves[a]], ALU.mult)
-                nc.vector.tensor_tensor(h[0][a], sum_bank[a][:], h[0][a], ALU.subtract)
+        def limbs(i):
+            return fetched[i][:, 0:S] if i < 2 else limb_rows[i % 2][:]
 
-        def product(i, names, a, bank, empty, into):
-            for blk in blocks:
-                for name in names:
-                    words, scales = weights(i)[name]()
-                    nc.tensor.matmul_mx(
-                        bank[:, blk], lhsT=v_w[a][:, blk].bitcast(FP8X4),
-                        lhsT_scale=v_s[:, a * BANK + blk.start : a * BANK + blk.stop],
-                        rhs=words, rhs_scale=scales, start=(name == names[0]), stop=(name == names[-1]),
-                    )
-            empty(into[:, halves[a]], bank[:])
-
-        def sigmoid(into, source):
-            nc.scalar.activation(into, source, ACT.Sigmoid)
-
-        def gate(i):
-            for a in range(2):
-                product(i, ("gate",), a, gate_bank[a], sigmoid, sig[i])
-
-        def add_transposed(bank, source, opens):
-            for blk in blocks:
-                nc.tensor.matmul(
-                    bank[:, blk], source[:, blk], ident[:], is_transpose=True,
-                    start=(opens and blk.start == 0), stop=(not opens and blk.stop == BANK),
+        def group(into, lhs, rhs):
+            for x in range(len(lhs)):
+                nc.tensor.matmul_mx(
+                    into, lhsT=lhs[x][0], lhsT_scale=lhs[x][1], rhs=rhs[x][0], rhs_scale=rhs[x][1],
+                    start=(x == 0), stop=(x == len(lhs) - 1),
                 )
 
-        def high_reading(i):
-            names = ("high", "low") if i < FOLDED else ("high",)
-            for a in range(2):
-                product(i, names, a, high_bank[a], nc.scalar.copy, span[i])
+        def rows_on_partitions(into, names, c0):
+            group(into, [weights(0, n) for n in names], [v_operand(c0, QUARTER)] * len(names))
 
-        def readings(i):
-            high_reading(i)
-            low_reading(i)
+        def columns_on_partitions(into, i, names, c0):
+            for x in range(0, into.shape[1], P):
+                group(into[:, x : x + P], [v_operand(c0 + x, P)] * len(names), [weights(i, n) for n in names])
 
-        def low_reading(i):
-            for a in range(2):
-                product(i, ("low",), a, (low_bank if i < PACK else gate_bank if i == PACK else high_bank)[a], negated, low[i])
+        def add_transposed(bank, source, opens):
+            width = source.shape[1]
+            for x in range(0, width, P):
+                nc.tensor.matmul(
+                    bank[:, x : x + P], source[:, x : x + P], ident[:], is_transpose=True,
+                    start=(opens and x == 0), stop=(not opens and x + P == width),
+                )
 
-        def interpolate(i):
+        left, right = slice(0, QUARTER), slice(QUARTER, BANK)
+
+        def product(i, names, a, bank, empty, into):
+            columns_on_partitions(bank[:], i, names, a * BANK)
+            empty(into[:, halves[a]], bank[:])
+
+        def gate_and_span(i, a):
+            product(i, ("gate",), a, (sum_bank if i == 1 else gate_bank)[a], sigmoid, sig[i])
+            names = ("low", "high") if i < FOLDED else ("high",)
+            product(i, names, a, {1: gate_bank, 2: low_bank}.get(i, high_bank)[a], nc.scalar.copy, span[i])
+
+        def low_reading(i, a):
+            product(i, ("low",), a, (gate_bank if i == 1 else low_bank)[a], negated, low(i))
+
+        def products(i):
             for a in range(2):
-                add_transposed(sum_bank[a], low[i][:, halves[a]], True)
+                gate_and_span(i, a)
+                low_reading(i, a)
+
+        def interpolate(i, sums=sum_bank):
+            for a in range(2):
+                add_transposed(sums[a], low(i)[:, halves[a]], True)
             for a in range(2 if i >= FOLDED else 0):
-                nc.gpsimd.tensor_tensor(span[i][:, halves[a]], span[i][:, halves[a]], low[i][:, halves[a]], ALU.subtract)
+                nc.gpsimd.tensor_tensor(span[i][:, halves[a]], span[i][:, halves[a]], low(i)[:, halves[a]], ALU.subtract)
             for a in range(2):
                 nc.gpsimd.tensor_tensor(step[:, halves[a]], span[i][:, halves[a]], sig[i][:, halves[a]], ALU.mult)
-                add_transposed(sum_bank[a], step[:, halves[a]], False)
-                nc.scalar.copy(h[i][a], sum_bank[a][:])
+                add_transposed(sums[a], step[:, halves[a]], False)
+                nc.scalar.copy(h(i)[:, halves[a]], sums[a][:])
 
-        def weigh(i):
-            if len(wgs_rows[i]) == 1:
-                nc.gpsimd.tensor_tensor(weighted(i)[:], home[i][:], wgs_rows[i][0], ALU.mult)
-            else:
-                for a in range(2):
-                    nc.gpsimd.tensor_tensor(weighted(i)[:, halves[a]], h[i][a], wgs_rows[i][a], ALU.mult)
+        def weigh(i, parts=(slice(0, S),)):
+            for cols in parts:
+                nc.gpsimd.tensor_tensor(weighted(i)[:, cols], h(i)[:, cols], wgs_rows[i][:, cols], ALU.mult)
 
         def scatter(i, m0, width):
             nc.vector.tensor_copy(pages[i][:].indirect(offsets("offs2", m0, width)), weighted(i)[:, m0 : m0 + width])
@@ -310,36 +312,36 @@ def tile_list_limb_cut_advice_kernel(
         def fetch(i, name, m0, into):
             nc.vector.tensor_copy(into, pages[i][:].indirect(offsets(name, m0, into.shape[1])))
 
-        def fetch_limbs(i, m0, minus, into):
-            nc.vector.tensor_tensor(into, pages[i][:].indirect(offsets("offs3", m0, into.shape[1])), minus, ALU.subtract)
+        def fetch_limbs(i):
+            fetch(i, "offs3", 0, limbs(i))
 
         def fetch_bearers(i):
-            fetch(i, "offs4", 0, bearers(i)[:])
+            fetch(i, "offs4", 0, bearers(i))
 
-        def subtract(i):
-            nc.gpsimd.tensor_tensor(diff[:, i - PACK, :], limbs[:], bearers(i)[:], ALU.subtract)
+        def subtract(i, into):
+            nc.gpsimd.tensor_tensor(into, limbs(i), bearers(i), ALU.subtract)
 
         def round_z(source, grouped, slots):
             nc.scalar.activation(by_four(grouped)[:, :, slots, :], rows_by_four(source), ACT.Abs)
 
-        def turn_z(i):
+        def turn_z(i, sums=sum_bank):
             rows = turned[:].rearrange("p (g r) -> p g r", r=PASS)[:, :, P * i : P * (i + 1)]
             for a in range(2):
-                add_transposed(sum_bank[a], limbs[:, halves[a]], True)
-                negated(limbs[:, halves[a]], bearers(i)[:, halves[a]])
+                add_transposed(sums[a], limbs(i)[:, halves[a]], True)
+                negated(limbs(i)[:, halves[a]], bearers(i)[:, halves[a]])
             for a in range(2):
-                add_transposed(sum_bank[a], limbs[:, halves[a]], False)
+                add_transposed(sums[a], limbs(i)[:, halves[a]], False)
                 nc.scalar.activation(
-                    rows[:, PACK * a : PACK * (a + 1), :], sum_bank[a][:].rearrange("p (g r) -> p g r", r=P), ACT.Abs
+                    rows[:, PACK * a : PACK * (a + 1), :], sums[a][:].rearrange("p (g r) -> p g r", r=P), ACT.Abs
                 )
 
-        def turn_back_z():
+        def turn_back_z(z0_grouped):
             pairs = turned[:].bitcast(F32).rearrange("p (g q u) -> p g u q", u=2, q=P)
-            for x, bank in enumerate(low_bank + high_bank):
+            for x, bank in enumerate(sum_bank + sum_bank):
                 for y, blk in enumerate(blocks):
                     nc.tensor.transpose(bank[:, blk], pairs[:, 2 * x + y // 2, y % 2, :], ident[:])
                 nc.scalar.copy(
-                    z0_grouped[:].bitcast(F32)[:, x * BANK : (x + 1) * BANK].rearrange("p (g m u) -> p g m u", g=2, u=2),
+                    z0_grouped[:, x * BANK : (x + 1) * BANK].rearrange("p (g m u) -> p g m u", g=2, u=2),
                     bank[:].rearrange("p (g u m) -> p g m u", g=2, u=2),
                 )
 
@@ -354,84 +356,119 @@ def tile_list_limb_cut_advice_kernel(
                 cols = slice(b * N + nb * P, b * N + (nb + 1) * P)
                 nc.tensor.matmul_mx(
                     score_bank(x, part)[:, side * width : (side + 1) * width],
-                    lhsT=late_codes[:, cols].bitcast(FP8X4), lhsT_scale=wd_s[:, cols],
+                    lhsT=wd_w[:, cols].bitcast(FP8X4), lhsT_scale=wd_s[:, cols],
                     rhs=words.bitcast(FP8X4), rhs_scale=scales,
                     start=(b == 0 and side == 0), stop=(b == 1 and side == 1),
                 )
 
-        grouped23 = weighted(0)[:, halves[1]].bitcast(BF16)
-        first_tile()
-        round_on_scalar(grouped23, wl_raw23[:])
-        nc.vector.tensor_tensor(weighted(0)[:, halves[0]], h[0][0], wgs_rows[0][0], ALU.mult)
-        quantise(wl_first[:, 2 * P : PASS], wl_s[:, 2 * P : PASS], grouped23)
-        gate(1)
-        readings(1)
-        nc.gpsimd.tensor_tensor(weighted(0)[:, halves[1]], h[0][1], wgs_rows[0][1], ALU.mult)
+        for x in (0, 1):
+            rows_on_partitions(banks[2 * x][:, left], ("gate",), quarters[x].start)
+            sigmoid(sig[0][:, quarters[x]], banks[2 * x][:, left])
+            rows_on_partitions(banks[2 * x + 1][:, left], ("low", "high"), quarters[x].start)
+        for x in (0, 1):
+            rows_on_partitions(banks[2 * x][:, right], ("low",), quarters[x].start)
+        for x in (2, 3):
+            columns_on_partitions(banks[2 * x][:, left], 0, ("gate",), quarters[x].start)
+            sigmoid(sig[0][:, quarters[x]], banks[2 * x][:, left])
+            columns_on_partitions(banks[2 * x + 1][:, left], 0, ("low", "high"), quarters[x].start)
+            columns_on_partitions(banks[2 * x + 1][:, right], 0, ("low",), quarters[x].start)
+            nc.scalar.copy(span[0][:, quarters[x]], banks[2 * x + 1][:, left])
+            negated(low(0)[:, quarters[x]], banks[2 * x + 1][:, right])
+        for x in (0, 1):
+            nc.vector.tensor_tensor(h(0)[:, quarters[x]], banks[2 * x + 1][:, left], sig[0][:, quarters[x]], ALU.mult)
+        grouped1 = limb_rows[0][:, left].bitcast(BF16)
+        round_on_gpsimd(grouped1, wl_raw[1][:])
+        for x in (0, 1):
+            nc.vector.tensor_tensor(h(0)[:, quarters[x]], h(0)[:, quarters[x]], banks[2 * x][:, right], ALU.subtract)
+        for x in (0, 1):
+            nc.vector.tensor_tensor(weighted(0)[:, quarters[x]], h(0)[:, quarters[x]], wgs_natural[:, quarters[x]], ALU.mult)
+        quantise(wl_w[1], wl_s[:, blocks[1]], grouped1)
+        scatter(0, 0, BANK)
+        first_step = {x: sig[1][:, P + (x - 2) * QUARTER : P + (x - 1) * QUARTER] for x in (2, 3)}
+        for x in (2, 3):
+            nc.gpsimd.tensor_tensor(first_step[x], span[0][:, quarters[x]], sig[0][:, quarters[x]], ALU.mult)
+        for x in (2, 3):
+            bank = gate_bank[x - 2][:, left]
+            add_transposed(bank, low(0)[:, quarters[x]], True)
+            add_transposed(bank, first_step[x], False)
+            nc.scalar.copy(h(0)[:, quarters[x]], bank)
+            nc.gpsimd.tensor_tensor(weighted(0)[:, quarters[x]], h(0)[:, quarters[x]], wgs_natural[:, quarters[x]], ALU.mult)
+        scatter(0, BANK, BANK)
+        grouped23 = h_rows[0][:, S - QUARTER - P // 2 : S + QUARTER - P // 2]
+        round_on_gpsimd(grouped23[:, left].bitcast(BF16), wl_raw[2][:])
         for a in range(2):
-            scatter(0, a * BANK, BANK)
-        interpolate(1)
-        gate(2)
-        readings(2)
-        gate(3)
-        high_reading(3)
-        fetch(0, "offs3", 0, limbs[:])
-        weigh(1)
+            gate_and_span(1, a)
+        low_reading(1, 0)
+        round_on_scalar(grouped23[:, right].bitcast(BF16), wl_raw[3][:])
+        quantise(wl_first[:, 2 * P : PASS], wl_s[:, 2 * P : PASS], grouped23.bitcast(BF16))
+        fetched[0] = held([P, 2 * S], F32, "wl_raw3")
+        fetch_limbs(0)
         fetch_bearers(0)
-        scatter(1, 0, S)
+
+        low_reading(1, 1)
+        interpolate(1, low_bank)
+        weigh(1, halves)
+        products(2)
         interpolate(2)
-        low_reading(3)
-        round_wl_dealt(sig[2].bitcast(BF16))
+        grouped_dealt = sig[2].bitcast(BF16)
+        round_wl_dealt(grouped_dealt)
+        scatter(1, 0, S)
         wl_w_dealt = held([P, PASS], U32, "wl_w_dealt")
         for t in range(PACK):
             wl_w[PACK + t] = wl_w_dealt[:, blocks[t]]
-        quantise(wl_w_dealt[:], wl_s[:, PASS:H], sig[2].bitcast(BF16))
-        turn_z(0)
+        quantise(wl_w_dealt[:], wl_s[:, PASS:H], grouped_dealt)
+        fetched[1] = held([P, 2 * S], F32, "wl_raw_dealt")
+        fetch_limbs(1)
+        fetch_bearers(1)
         weigh(2)
-        dealt_words = held([P, PASS + PASS // 2], U32, "wl_w3_spent")
+        products(3)
+        turn_z(0)
+        interpolate(3)
+        dealt_words = held([P, PASS + PASS // 2], U32, "wl_raw2")
         dealt["high"], dealt["gate"] = dealt_words[:, 0:PASS], dealt_words[:, PASS : PASS + PASS // 2]
         deal_columns(nc.scalar.copy, dealt["high"], wh_c[:].bitcast(U32))
         deal_columns(nc.scalar.copy, dealt["gate"], wg_c[:].bitcast(U32))
-        fetch(1, "offs3", 0, limbs[:])
-        interpolate(3)
-        gate(4)
-        readings(4)
+        products(4)
 
+        z0_grouped = wide_tile[:, 0 : 2 * S]
+        base = 2 * S - BANK
+        differences = {PACK: wgs_rows[PACK + 2], PACK + 1: wide_tile[:, base : base + S]}
         for i in range(2, LAST):
             scatter(i, 0, S)
-            if 0 < i - 2 < PACK:
-                turn_z(i - 2)
-            if i - 2 >= PACK:
-                subtract(i - 2)
+            if i > 2:
+                fetch_bearers(i - 1)
+            if i == LAST - 1:
+                z_w[0] = held([P, M_OUT], U32, "weighted0")[:]
+                quantise(*z_operand(0, 0, M_OUT), z0_grouped.bitcast(BF16))
+            fetch_limbs(i)
             weigh(i + 1)
+            if i - 1 < PACK:
+                turn_z(i - 1)
+            else:
+                subtract(i - 1, differences[i - 1])
             if i + 2 <= LAST:
                 interpolate(i + 2)
             if i + 3 <= LAST:
-                gate(i + 3)
-                readings(i + 3)
-            if i - 2 == PACK - 1:
-                turn_back_z()
-                wd_grouped = spent[:, S : 3 * S].bitcast(BF16)
+                products(i + 3)
+            if i == 2:
+                wd_grouped = held([P, 2 * N * PACK], BF16, "wgs_natural")
                 for c0 in range(0, 2 * N, P):
                     b, cols = c0 // N, blocks[c0 % N // P]
                     nc.scalar.copy(by_four(wd_grouped[:, c0 * PACK : (c0 + P) * PACK]), rows_by_four(wd_raw[b][:, :, cols]))
-            if i > 2:
-                fetch(i - 1, "offs3", 0, limbs[:])
-            fetch_bearers(i - 1)
+            if i == PACK:
+                turn_back_z(z0_grouped)
 
-        late_codes = held([P, 2 * N + M_OUT], U32, "wgs_last0")
-        z_w[0] = late_codes[:, 2 * N : 2 * N + M_OUT]
-        quantise(*z_operand(0, 0, M_OUT), z0_grouped[:])
-        quantise(late_codes[:, 0 : 2 * N], wd_s[:], wd_grouped)
         scatter(LAST, 0, S)
-        subtract(LAST - 2)
+        wd_w = held([P, 2 * N], U32, "limbs1")
+        quantise(wd_w[:], wd_s[:], wd_grouped[:])
         z1_grouped = held([P, M_OUT * PACK], BF16, "wl_raw_dealt")
 
-        def late(x):
+        def z1_piece(x):
             m0, width = PIECES[x]
             return z1_grouped[:, m0 * PACK : (m0 + width) * PACK]
 
-        for half in halves:
-            round_z(diff[:, :, half], z1_grouped[:, half.start * PACK : half.stop * PACK], slice(0, 2))
+        for t in range(2):
+            round_z(differences[PACK + t].unsqueeze(1), z1_grouped[:], slice(t, t + 1))
         for x in range(len(PIECES) - 1):
             score_pass(0, x)
 
@@ -445,34 +482,47 @@ def tile_list_limb_cut_advice_kernel(
             nc.sync.dma_start(out=out_rows[part][:, :, m0 : m0 + width], in_=staged.rearrange("p (s m) -> p s m", s=2))
 
         def finish(x):
-            quantise(*z_operand(1, *PIECES[x]), late(x))
+            quantise(*z_operand(1, *PIECES[x]), z1_piece(x))
             score_pass(1, x)
 
-        first = spent[:, 2 * S : 3 * S]
-        wide = PIECES[0][1]
-        pairs = [spent[:, S + BANK : 2 * S], spent[:, BANK:S], first[:, wide : 3 * wide]]
-        pairs += [first[:, 0:wide], first[:, wide : 2 * wide]]
-        gathers = {0: (BANK, first), 2: (wide, pairs[0]), 3: (wide, pairs[1])}
-        held_back = {(2, 0): pairs[2], (2, 1): pairs[1]}
-        for x, (m0, width) in enumerate(PIECES):
-            pair = pairs[x].rearrange("p (s m) -> p s m", s=2)
-            if x in gathers:
-                start, borne = m0, gathers[x][1].rearrange("p (s m) -> p s m", s=2)
-                for s in range(2):
-                    fetch(LAST - 1 + s, "offs4", m0, borne[:, s, :])
+        def spent(start, width):
+            return wide_tile[:, base + start : base + start + width]
+
+        borne = (spent(-3 * P, BANK), spent(-5 * P, BANK))
+        pairs = [spent(start, 2 * PIECES[x][1]).rearrange("p (s m) -> p s m", s=2) for x, start in enumerate((P, 5 * P, P, 5 * P, P))]
+        held_back = {(1, 1): spent(P, BANK), (2, 0): borne[1], (2, 1): z1_grouped[:, PIECES[3][0] * PACK :].bitcast(F32)}
+
+        def differ(x, s):
+            m0, width = PIECES[x]
+            if s == 0:
+                window, minus = pages[LAST - 1][:].indirect(offsets("offs4", m0, width)), limbs(LAST - 1)[:, m0 : m0 + width]
+            else:
+                window, minus = pages[LAST][:].indirect(offsets("offs3", m0, width)), borne[m0 // BANK][:, m0 % BANK : m0 % BANK + width]
+            nc.vector.tensor_tensor(pairs[x][:, s, :], window, minus, ALU.subtract)
+
+        differ(0, 0)
+        fetch(LAST, "offs4", 0, borne[0])
+        differ(1, 0)
+        for x in range(2):
+            differ(x, 1)
+            round_z(pairs[x], z1_piece(x), slice(2, PACK))
+        fetch(LAST, "offs4", BANK, borne[1])
+        for x in range(2, len(PIECES)):
+            finish(x - 2)
             for s in range(2):
-                fetch_limbs(LAST - 1 + s, m0, borne[:, s, m0 - start : m0 - start + width], pair[:, s, :])
-            round_z(pair, late(x), slice(2, PACK))
-            if x > 0:
-                finish(x - 1)
-            if 0 < x < 3:
+                differ(x, s)
+            round_z(pairs[x], z1_piece(x), slice(2, PACK))
+            if x == 2:
                 for part in range(2):
-                    store(x - 1, part, nc.scalar.copy)
-            if x == 1:
+                    store(0, part, nc.scalar.copy)
                 score_pass(0, len(PIECES) - 1)
+            if x == 3:
+                store(1, 0, nc.scalar.copy)
+        store(1, 1, nc.scalar.copy)
+        finish(3)
+        store(2, 0, nc.vector.tensor_copy)
+        finish(4)
         store(2, 1, nc.vector.tensor_copy)
-        store(2, 0, nc.scalar.copy)
-        finish(len(PIECES) - 1)
         for x in (3, 4):
             store(x, 0, nc.vector.tensor_copy)
             store(x, 1, nc.scalar.copy)

@@ -105,14 +105,20 @@ def tile_list_limb_cut_advice_kernel(
             load_scale_rows(wg_s, wg_scales, nc.sync, q)
         wh_first = load_plain("wh_first", wh_i32[:, 0:P], I32)
         load_scale_rows(wh_s, wh_scales, nc.sync, 0)
-        wgs_natural = load_plain("wgs_natural", wgs, F32)
+        pages[0] = held([P, T2], F32, "page0")
+        nc.sync.dma_start(out=pages[0][:, 0 : T2 // 2], in_=page0[0:P, 0 : T2 // 2])
         nc.sync.dma_start(lists["offs2"][:], offs2)
+        wgs_natural = held([P, S], F32, "wgs_natural")
+        nc.sync.dma_start(out=wgs_natural[:, halves[0]], in_=wgs[:, halves[0]])
         wl_raw[1] = load_rows_of_four("wl_raw1", wl[:, P : 2 * P])
-        load_page(0)
+        nc.sync.dma_start(out=pages[0][:, T2 // 2 : T2], in_=page0[0:P, T2 // 2 : T2])
+        nc.sync.dma_start(out=wgs_natural[:, halves[1]], in_=wgs[:, halves[1]])
         wh_rest = load_plain("wh_rest", wh_i32[:, P:PASS], I32)
         wg_rest = load_plain("wg_rest", wg_i32[:, P // 2 : PASS // 2], I32)
+        wl_raw23 = held([P, 2, PACK, P], F32, "wl_raw23")
         for i in (2, 3):
-            wl_raw[i] = load_rows_of_four("wl_raw%d" % i, wl[:, i * P : (i + 1) * P])
+            wl_raw[i] = wl_raw23[:, i - 2]
+            nc.sync.dma_start(out=wl_raw[i], in_=wl[:, i * P : (i + 1) * P].rearrange("(p j) c -> p j c", j=PACK))
         nc.sync.dma_start(lists["offs3"][:], offs3)
         nc.sync.dma_start(lists["offs4"][:], offs4)
         load_page(1)
@@ -251,19 +257,16 @@ def tile_list_limb_cut_advice_kernel(
         def limbs(i):
             return fetched[i][:, 0:S] if i < 2 else limb_rows[i % 2][:]
 
-        def group(into, lhs, rhs):
-            for x in range(len(lhs)):
-                nc.tensor.matmul_mx(
-                    into, lhsT=lhs[x][0], lhsT_scale=lhs[x][1], rhs=rhs[x][0], rhs_scale=rhs[x][1],
-                    start=(x == 0), stop=(x == len(lhs) - 1),
-                )
+        def multiply(into, lhs, rhs, start, stop):
+            nc.tensor.matmul_mx(into, lhsT=lhs[0], lhsT_scale=lhs[1], rhs=rhs[0], rhs_scale=rhs[1], start=start, stop=stop)
 
-        def rows_on_partitions(into, names, c0):
-            group(into, [weights(0, n) for n in names], [v_operand(c0, QUARTER)] * len(names))
+        def rows_on_partitions(into, name, x, start, stop):
+            multiply(into, weights(0, name), v_operand(quarters[x].start, QUARTER), start, stop)
 
         def columns_on_partitions(into, i, names, c0):
             for x in range(0, into.shape[1], P):
-                group(into[:, x : x + P], [v_operand(c0 + x, P)] * len(names), [weights(i, n) for n in names])
+                for name in names:
+                    multiply(into[:, x : x + P], v_operand(c0 + x, P), weights(i, name), name == names[0], name == names[-1])
 
         def add_transposed(bank, source, opens):
             width = source.shape[1]
@@ -280,12 +283,12 @@ def tile_list_limb_cut_advice_kernel(
             empty(into[:, halves[a]], bank[:])
 
         def gate_and_span(i, a):
-            product(i, ("gate",), a, (sum_bank if i == 1 else gate_bank)[a], sigmoid, sig[i])
+            product(i, ("gate",), a, (high_bank if i == 1 else gate_bank)[a], sigmoid, sig[i])
             names = ("low", "high") if i < FOLDED else ("high",)
-            product(i, names, a, {1: gate_bank, 2: low_bank}.get(i, high_bank)[a], nc.scalar.copy, span[i])
+            product(i, names, a, {1: sum_bank, 2: low_bank}.get(i, high_bank)[a], nc.scalar.copy, span[i])
 
         def low_reading(i, a):
-            product(i, ("low",), a, (gate_bank if i == 1 else low_bank)[a], negated, low(i))
+            product(i, ("low",), a, (sum_bank if i == 1 else low_bank)[a], negated, low(i))
 
         def products(i):
             for a in range(2):
@@ -362,46 +365,49 @@ def tile_list_limb_cut_advice_kernel(
                 )
 
         for x in (0, 1):
-            rows_on_partitions(banks[2 * x][:, left], ("gate",), quarters[x].start)
+            rows_on_partitions(banks[2 * x][:, left], "gate", x, True, True)
             sigmoid(sig[0][:, quarters[x]], banks[2 * x][:, left])
-            rows_on_partitions(banks[2 * x + 1][:, left], ("low", "high"), quarters[x].start)
+            rows_on_partitions(banks[2 * x + 1][:, left], "low", x, True, False)
         for x in (0, 1):
-            rows_on_partitions(banks[2 * x][:, right], ("low",), quarters[x].start)
-        for x in (2, 3):
-            columns_on_partitions(banks[2 * x][:, left], 0, ("gate",), quarters[x].start)
-            sigmoid(sig[0][:, quarters[x]], banks[2 * x][:, left])
-            columns_on_partitions(banks[2 * x + 1][:, left], 0, ("low", "high"), quarters[x].start)
-            columns_on_partitions(banks[2 * x + 1][:, right], 0, ("low",), quarters[x].start)
-            nc.scalar.copy(span[0][:, quarters[x]], banks[2 * x + 1][:, left])
-            negated(low(0)[:, quarters[x]], banks[2 * x + 1][:, right])
+            rows_on_partitions(banks[2 * x + 1][:, left], "high", x, False, True)
+        for x in (0, 1):
+            rows_on_partitions(banks[2 * x][:, right], "low", x, True, True)
         for x in (0, 1):
             nc.vector.tensor_tensor(h(0)[:, quarters[x]], banks[2 * x + 1][:, left], sig[0][:, quarters[x]], ALU.mult)
-        grouped1 = limb_rows[0][:, left].bitcast(BF16)
+        grouped1 = sig[0][:, quarters[0]].bitcast(BF16)
         round_on_gpsimd(grouped1, wl_raw[1][:])
         for x in (0, 1):
             nc.vector.tensor_tensor(h(0)[:, quarters[x]], h(0)[:, quarters[x]], banks[2 * x][:, right], ALU.subtract)
+        for x in (2, 3):
+            columns_on_partitions(banks[1][:, quarters[x - 2]], 0, ("gate",), quarters[x].start)
+        sigmoid(sig[0][:, halves[1]], banks[1][:])
+        for x, bank in ((2, banks[3]), (3, banks[0])):
+            columns_on_partitions(bank[:, left], 0, ("low", "high"), quarters[x].start)
+            columns_on_partitions(bank[:, right], 0, ("low",), quarters[x].start)
+            nc.scalar.copy(span[0][:, quarters[x]], bank[:, left])
+            negated(low(0)[:, quarters[x]], bank[:, right])
         for x in (0, 1):
             nc.vector.tensor_tensor(weighted(0)[:, quarters[x]], h(0)[:, quarters[x]], wgs_natural[:, quarters[x]], ALU.mult)
         quantise(wl_w[1], wl_s[:, blocks[1]], grouped1)
         scatter(0, 0, BANK)
-        first_step = {x: sig[1][:, P + (x - 2) * QUARTER : P + (x - 1) * QUARTER] for x in (2, 3)}
+        first_step = {x: sig[1][:, P // 2 + (x - 2) * QUARTER : P // 2 + (x - 1) * QUARTER] for x in (2, 3)}
         for x in (2, 3):
             nc.gpsimd.tensor_tensor(first_step[x], span[0][:, quarters[x]], sig[0][:, quarters[x]], ALU.mult)
         for x in (2, 3):
-            bank = gate_bank[x - 2][:, left]
+            bank = sum_bank[x - 2][:, left]
             add_transposed(bank, low(0)[:, quarters[x]], True)
             add_transposed(bank, first_step[x], False)
             nc.scalar.copy(h(0)[:, quarters[x]], bank)
             nc.gpsimd.tensor_tensor(weighted(0)[:, quarters[x]], h(0)[:, quarters[x]], wgs_natural[:, quarters[x]], ALU.mult)
         scatter(0, BANK, BANK)
         grouped23 = h_rows[0][:, S - QUARTER - P // 2 : S + QUARTER - P // 2]
-        round_on_gpsimd(grouped23[:, left].bitcast(BF16), wl_raw[2][:])
+        round_on_gpsimd(grouped23[:, left].bitcast(BF16), wl_raw[2])
         for a in range(2):
             gate_and_span(1, a)
         low_reading(1, 0)
-        round_on_scalar(grouped23[:, right].bitcast(BF16), wl_raw[3][:])
+        round_on_scalar(grouped23[:, right].bitcast(BF16), wl_raw[3])
         quantise(wl_first[:, 2 * P : PASS], wl_s[:, 2 * P : PASS], grouped23.bitcast(BF16))
-        fetched[0] = held([P, 2 * S], F32, "wl_raw3")
+        fetched[0] = held([P, 2 * S], F32, "wl_raw23")
         fetch_limbs(0)
         fetch_bearers(0)
 
@@ -424,7 +430,7 @@ def tile_list_limb_cut_advice_kernel(
         products(3)
         turn_z(0)
         interpolate(3)
-        dealt_words = held([P, PASS + PASS // 2], U32, "wl_raw2")
+        dealt_words = held([P, PASS + PASS // 2], U32, "wl_raw1")
         dealt["high"], dealt["gate"] = dealt_words[:, 0:PASS], dealt_words[:, PASS : PASS + PASS // 2]
         deal_columns(nc.scalar.copy, dealt["high"], wh_c[:].bitcast(U32))
         deal_columns(nc.scalar.copy, dealt["gate"], wg_c[:].bitcast(U32))
@@ -469,8 +475,6 @@ def tile_list_limb_cut_advice_kernel(
 
         for t in range(2):
             round_z(differences[PACK + t].unsqueeze(1), z1_grouped[:], slice(t, t + 1))
-        for x in range(len(PIECES) - 1):
-            score_pass(0, x)
 
         spare = (wd_raw[1][:].rearrange("p j c -> p (j c)"), turned[:].bitcast(F32))
         out_rows = out.rearrange("(a s p) m -> a p s m", s=2, p=P)
@@ -488,41 +492,34 @@ def tile_list_limb_cut_advice_kernel(
         def spent(start, width):
             return wide_tile[:, base + start : base + start + width]
 
-        borne = (spent(-3 * P, BANK), spent(-5 * P, BANK))
-        pairs = [spent(start, 2 * PIECES[x][1]).rearrange("p (s m) -> p s m", s=2) for x, start in enumerate((P, 5 * P, P, 5 * P, P))]
-        held_back = {(1, 1): spent(P, BANK), (2, 0): borne[1], (2, 1): z1_grouped[:, PIECES[3][0] * PACK :].bitcast(F32)}
+        borne = [spent(start, QUARTER) for start in (-192, 576, -64, 832)]
+        pairs = [
+            spent(start, 2 * PIECES[x][1]).rearrange("p (s m) -> p s m", s=2)
+            for x, start in enumerate((64, 832, 192, 1088, 192))
+        ]
+        held_back = {(2, 0): spent(BANK + P // 2, BANK)}
 
-        def differ(x, s):
-            m0, width = PIECES[x]
-            if s == 0:
-                window, minus = pages[LAST - 1][:].indirect(offsets("offs4", m0, width)), limbs(LAST - 1)[:, m0 : m0 + width]
-            else:
-                window, minus = pages[LAST][:].indirect(offsets("offs3", m0, width)), borne[m0 // BANK][:, m0 % BANK : m0 % BANK + width]
-            nc.vector.tensor_tensor(pairs[x][:, s, :], window, minus, ALU.subtract)
-
-        differ(0, 0)
-        fetch(LAST, "offs4", 0, borne[0])
-        differ(1, 0)
-        for x in range(2):
-            differ(x, 1)
+        for x, (m0, width) in enumerate(PIECES):
+            if m0 % QUARTER == 0:
+                fetch(LAST, "offs4", m0, borne[m0 // QUARTER])
+            nc.vector.tensor_tensor(
+                pairs[x][:, 0, :], pages[LAST - 1][:].indirect(offsets("offs4", m0, width)),
+                limbs(LAST - 1)[:, m0 : m0 + width], ALU.subtract,
+            )
+            nc.vector.tensor_tensor(
+                pairs[x][:, 1, :], pages[LAST][:].indirect(offsets("offs3", m0, width)),
+                borne[m0 // QUARTER][:, m0 % QUARTER : m0 % QUARTER + width], ALU.subtract,
+            )
             round_z(pairs[x], z1_piece(x), slice(2, PACK))
-        fetch(LAST, "offs4", BANK, borne[1])
-        for x in range(2, len(PIECES)):
-            finish(x - 2)
-            for s in range(2):
-                differ(x, s)
-            round_z(pairs[x], z1_piece(x), slice(2, PACK))
-            if x == 2:
+            if x > 0:
+                finish(x - 1)
+            if x in (1, 2):
                 for part in range(2):
-                    store(0, part, nc.scalar.copy)
-                score_pass(0, len(PIECES) - 1)
-            if x == 3:
-                store(1, 0, nc.scalar.copy)
-        store(1, 1, nc.scalar.copy)
-        finish(3)
+                    store(x - 1, part, nc.scalar.copy)
+            score_pass(0, x)
         store(2, 0, nc.vector.tensor_copy)
-        finish(4)
-        store(2, 1, nc.vector.tensor_copy)
+        store(2, 1, nc.scalar.copy)
+        finish(len(PIECES) - 1)
         for x in (3, 4):
             store(x, 0, nc.vector.tensor_copy)
             store(x, 1, nc.scalar.copy)

@@ -171,11 +171,15 @@ def tile_list_limb_cut_advice_kernel(
 
         def round_wl_dealt(grouped):
             for t in range(PACK):
-                nc.gpsimd.tensor_scalar(
-                    grouped[:, t * PASS : (t + 1) * PASS].rearrange("p (q s j) -> p q s j", s=RUN, j=PACK),
-                    wl_raw_dealt[:].rearrange("p j (q t s) -> p t q s j", t=PACK, s=RUN)[:, t],
-                    -1.0, 0.0, ALU.mult, ALU.add,
-                )
+                into = grouped[:, t * PASS : (t + 1) * PASS]
+                if t < 2:
+                    negated(by_four(into), wl_raw_dealt[:].rearrange("p j (q t s) -> p t q j s", t=PACK, s=RUN)[:, t])
+                else:
+                    nc.gpsimd.tensor_scalar(
+                        into.rearrange("p (q s j) -> p q s j", s=RUN, j=PACK),
+                        wl_raw_dealt[:].rearrange("p j (q t s) -> p t q s j", t=PACK, s=RUN)[:, t],
+                        -1.0, 0.0, ALU.mult, ALU.add,
+                    )
 
         def deal_columns(copy, into, source):
             run = source.shape[1] * RUN // PASS
@@ -237,7 +241,7 @@ def tile_list_limb_cut_advice_kernel(
         low_rows = [held([P, S], F32, "low%d" % s) for s in range(2)]
         step = held([P, S], F32, "step")
         limb_rows = [held([P, S], F32, "limbs%d" % s) for s in range(2)]
-        h_rows = [held([P, S + (1 - s) * QUARTER], F32, "h_rows%d" % s) for s in range(2)]
+        h_rows = [held([P, S], F32, "h_rows%d" % s) for s in range(2)]
         weighted_rows = [held([P, S], F32, "weighted%d" % s) for s in range(2)]
         turned = held([P, TILES * PASS], BF16, "turned")
         fetched = {}
@@ -283,12 +287,12 @@ def tile_list_limb_cut_advice_kernel(
             empty(into[:, halves[a]], bank[:])
 
         def gate_and_span(i, a):
-            product(i, ("gate",), a, (high_bank if i == 1 else gate_bank)[a], sigmoid, sig[i])
+            product(i, ("gate",), a, gate_bank[1 - a if i == 1 else a], sigmoid, sig[i])
             names = ("low", "high") if i < FOLDED else ("high",)
-            product(i, names, a, {1: sum_bank, 2: low_bank}.get(i, high_bank)[a], nc.scalar.copy, span[i])
+            product(i, names, a, (low_bank if i == 2 else high_bank)[a], nc.scalar.copy, span[i])
 
         def low_reading(i, a):
-            product(i, ("low",), a, (sum_bank if i == 1 else low_bank)[a], negated, low(i))
+            product(i, ("low",), a, (high_bank if i == 1 else low_bank)[a], negated, low(i))
 
         def products(i):
             for a in range(2):
@@ -375,7 +379,7 @@ def tile_list_limb_cut_advice_kernel(
         for x in (0, 1):
             nc.vector.tensor_tensor(h(0)[:, quarters[x]], banks[2 * x + 1][:, left], sig[0][:, quarters[x]], ALU.mult)
         grouped1 = sig[0][:, quarters[0]].bitcast(BF16)
-        round_on_gpsimd(grouped1, wl_raw[1][:])
+        round_on_scalar(grouped1, wl_raw[1][:])
         for x in (0, 1):
             nc.vector.tensor_tensor(h(0)[:, quarters[x]], h(0)[:, quarters[x]], banks[2 * x][:, right], ALU.subtract)
         for x in (2, 3):
@@ -390,28 +394,29 @@ def tile_list_limb_cut_advice_kernel(
             nc.vector.tensor_tensor(weighted(0)[:, quarters[x]], h(0)[:, quarters[x]], wgs_natural[:, quarters[x]], ALU.mult)
         quantise(wl_w[1], wl_s[:, blocks[1]], grouped1)
         scatter(0, 0, BANK)
-        first_step = {x: sig[1][:, P // 2 + (x - 2) * QUARTER : P // 2 + (x - 1) * QUARTER] for x in (2, 3)}
+        first_step = {2: span[1][:, quarters[1]], 3: sig[1][:, quarters[2]]}
+        first_h = {2: span[1][:, quarters[2]], 3: limb_rows[0][:, P : 3 * P]}
         for x in (2, 3):
             nc.gpsimd.tensor_tensor(first_step[x], span[0][:, quarters[x]], sig[0][:, quarters[x]], ALU.mult)
         for x in (2, 3):
             bank = sum_bank[x - 2][:, left]
             add_transposed(bank, low(0)[:, quarters[x]], True)
             add_transposed(bank, first_step[x], False)
-            nc.scalar.copy(h(0)[:, quarters[x]], bank)
-            nc.gpsimd.tensor_tensor(weighted(0)[:, quarters[x]], h(0)[:, quarters[x]], wgs_natural[:, quarters[x]], ALU.mult)
-        scatter(0, BANK, BANK)
-        grouped23 = h_rows[0][:, S - QUARTER - P // 2 : S + QUARTER - P // 2]
-        round_on_gpsimd(grouped23[:, left].bitcast(BF16), wl_raw[2])
+            nc.scalar.copy(first_h[x], bank)
+            nc.gpsimd.tensor_tensor(weighted(0)[:, quarters[x]], first_h[x], wgs_natural[:, quarters[x]], ALU.mult)
+            scatter(0, quarters[x].start, QUARTER)
         for a in range(2):
             gate_and_span(1, a)
-        low_reading(1, 0)
-        round_on_scalar(grouped23[:, right].bitcast(BF16), wl_raw[3])
+        grouped23 = limb_rows[0][:, halves[0]]
+        for i in (2, 3):
+            round_on_scalar(grouped23[:, quarters[i - 2]].bitcast(BF16), wl_raw[i])
         quantise(wl_first[:, 2 * P : PASS], wl_s[:, 2 * P : PASS], grouped23.bitcast(BF16))
         fetched[0] = held([P, 2 * S], F32, "wl_raw23")
         fetch_limbs(0)
         fetch_bearers(0)
 
-        low_reading(1, 1)
+        for a in range(2):
+            low_reading(1, a)
         interpolate(1, low_bank)
         weigh(1, halves)
         products(2)
@@ -447,7 +452,7 @@ def tile_list_limb_cut_advice_kernel(
                 z_w[0] = held([P, M_OUT], U32, "weighted0")[:]
                 quantise(*z_operand(0, 0, M_OUT), z0_grouped.bitcast(BF16))
             fetch_limbs(i)
-            weigh(i + 1)
+            weigh(i + 1, halves if i == 2 else (slice(0, S),))
             if i - 1 < PACK:
                 turn_z(i - 1)
             else:
@@ -467,7 +472,7 @@ def tile_list_limb_cut_advice_kernel(
         scatter(LAST, 0, S)
         wd_w = held([P, 2 * N], U32, "limbs1")
         quantise(wd_w[:], wd_s[:], wd_grouped[:])
-        z1_grouped = held([P, M_OUT * PACK], BF16, "wl_raw_dealt")
+        z1_grouped = held([P, M_OUT * PACK], BF16, "h_rows1")
 
         def z1_piece(x):
             m0, width = PIECES[x]

@@ -171,31 +171,27 @@ def tile_list_limb_cut_advice_kernel(
 
         def round_wl_dealt(grouped):
             for t in range(PACK):
-                into = grouped[:, t * PASS : (t + 1) * PASS]
-                if t < 2:
-                    negated(by_four(into), wl_raw_dealt[:].rearrange("p j (q t s) -> p t q j s", t=PACK, s=RUN)[:, t])
-                else:
-                    nc.gpsimd.tensor_scalar(
-                        into.rearrange("p (q s j) -> p q s j", s=RUN, j=PACK),
-                        wl_raw_dealt[:].rearrange("p j (q t s) -> p t q s j", t=PACK, s=RUN)[:, t],
-                        -1.0, 0.0, ALU.mult, ALU.add,
-                    )
+                raw = wl_raw_dealt[:].rearrange("p j (q t s) -> p t q j s", t=PACK, s=RUN)[:, t]
+                negated(by_four(grouped[:, t * PASS : (t + 1) * PASS]), raw)
 
         def deal_columns(copy, into, source):
             run = source.shape[1] * RUN // PASS
             copy(into.rearrange("p (t q s) -> p t q s", t=PACK, s=run), source.rearrange("p (q t s) -> p t q s", t=PACK, s=run))
 
-        def round_on_gpsimd(grouped, raw):
-            nc.gpsimd.tensor_scalar(
-                grouped.rearrange("p (c j) -> p c j", j=PACK), raw.rearrange("p j c -> p c j"), -1.0, 0.0, ALU.mult, ALU.add
+        grouped0 = held([P, PASS], BF16, "grouped0")
+
+        def round_first(engine, cols):
+            engine.tensor_scalar(
+                grouped0[:].rearrange("p (c j) -> p c j", j=PACK)[:, cols], wl_raw[0][:].rearrange("p j c -> p c j")[:, cols],
+                -1.0, 0.0, ALU.mult, ALU.add,
             )
 
-        grouped0 = held([P, PASS], BF16, "grouped0")
-        round_on_gpsimd(grouped0[:], wl_raw[0][:])
+        round_first(nc.gpsimd, slice(0, P // 2))
         ident = held([P, P], F32, "ident")
         make_identity(nc, ident[:])
 
         nc.vector.tensor_copy(v_s[:], tab_s[:].indirect(lists["offs"][:]))
+        round_first(nc.vector, slice(P // 2, P))
         v_cut = (0, QUARTER, BANK, S)
 
         def gather_words(a):
@@ -299,15 +295,24 @@ def tile_list_limb_cut_advice_kernel(
                 gate_and_span(i, a)
                 low_reading(i, a)
 
-        def interpolate(i, sums=sum_bank):
+        def open_sums(i, sums=sum_bank):
             for a in range(2):
                 add_transposed(sums[a], low(i)[:, halves[a]], True)
+
+        def make_step(i, a):
+            nc.gpsimd.tensor_tensor(step[:, halves[a]], span[i][:, halves[a]], sig[i][:, halves[a]], ALU.mult)
+
+        def close_sum(i, a, sums=sum_bank):
+            add_transposed(sums[a], step[:, halves[a]], False)
+            nc.scalar.copy(h(i)[:, halves[a]], sums[a][:])
+
+        def interpolate(i, sums=sum_bank):
+            open_sums(i, sums)
             for a in range(2 if i >= FOLDED else 0):
                 nc.gpsimd.tensor_tensor(span[i][:, halves[a]], span[i][:, halves[a]], low(i)[:, halves[a]], ALU.subtract)
             for a in range(2):
-                nc.gpsimd.tensor_tensor(step[:, halves[a]], span[i][:, halves[a]], sig[i][:, halves[a]], ALU.mult)
-                add_transposed(sums[a], step[:, halves[a]], False)
-                nc.scalar.copy(h(i)[:, halves[a]], sums[a][:])
+                make_step(i, a)
+                close_sum(i, a, sums)
 
         def weigh(i, parts=(slice(0, S),)):
             for cols in parts:
@@ -420,9 +425,13 @@ def tile_list_limb_cut_advice_kernel(
         interpolate(1, low_bank)
         weigh(1, halves)
         products(2)
-        interpolate(2)
+        open_sums(2)
+        for a in range(2):
+            make_step(2, a)
         grouped_dealt = sig[2].bitcast(BF16)
         round_wl_dealt(grouped_dealt)
+        for a in range(2):
+            close_sum(2, a)
         scatter(1, 0, S)
         wl_w_dealt = held([P, PASS], U32, "wl_w_dealt")
         for t in range(PACK):

@@ -107,10 +107,10 @@ def tile_list_limb_cut_advice_kernel(
         load_scale_rows(wh_s, wh_scales, nc.sync, 0)
         pages[0] = held([P, T2], F32, "page0")
         nc.sync.dma_start(out=pages[0][:, 0 : T2 // 2], in_=page0[0:P, 0 : T2 // 2])
+        wl_raw[1] = load_rows_of_four("wl_raw1", wl[:, P : 2 * P])
         nc.sync.dma_start(lists["offs2"][:], offs2)
         wgs_natural = held([P, S], F32, "wgs_natural")
         nc.sync.dma_start(out=wgs_natural[:, halves[0]], in_=wgs[:, halves[0]])
-        wl_raw[1] = load_rows_of_four("wl_raw1", wl[:, P : 2 * P])
         nc.sync.dma_start(out=pages[0][:, T2 // 2 : T2], in_=page0[0:P, T2 // 2 : T2])
         nc.sync.dma_start(out=wgs_natural[:, halves[1]], in_=wgs[:, halves[1]])
         wh_rest = load_plain("wh_rest", wh_i32[:, P:PASS], I32)
@@ -497,7 +497,8 @@ def tile_list_limb_cut_advice_kernel(
             m0, width = PIECES[x]
             staged = held_back.get((x, part), spare[part][:, 2 * m0 : 2 * (m0 + width)])
             copy(staged, score_bank(x, part)[:, 0 : 2 * width])
-            nc.sync.dma_start(out=out_rows[part][:, :, m0 : m0 + width], in_=staged.rearrange("p (s m) -> p s m", s=2))
+            queue = nc.scalar if x == len(PIECES) - 1 and part == 1 else nc.sync
+            queue.dma_start(out=out_rows[part][:, :, m0 : m0 + width], in_=staged.rearrange("p (s m) -> p s m", s=2))
 
         def finish(x):
             quantise(*z_operand(1, *PIECES[x]), z1_piece(x))

@@ -169,8 +169,8 @@ def tile_list_limb_cut_advice_kernel(
         def round_on_scalar(grouped, raw):
             negated(by_four(grouped), rows_by_four(raw))
 
-        def round_wl_dealt(grouped):
-            for t in range(PACK):
+        def round_wl_dealt(grouped, tiles):
+            for t in tiles:
                 raw = wl_raw_dealt[:].rearrange("p j (q t s) -> p t q j s", t=PACK, s=RUN)[:, t]
                 negated(by_four(grouped[:, t * PASS : (t + 1) * PASS]), raw)
 
@@ -232,30 +232,29 @@ def tile_list_limb_cut_advice_kernel(
         side = {i: (i + (i >= FOLDED)) % 2 for i in range(TILES)}
         sig = {i: (pair_a, pair_b)[side[i]][:] for i in range(TILES)}
         span = {i: (pair_c, pair_d)[side[i]][:] for i in range(TILES)}
-        double = held([P, 2 * S], F32, "double")
-        sig[2] = double[:, S - QUARTER : 2 * S - QUARTER]
+        double = held([P, S + QUARTER], F32, "double")
+        sig[2] = double[:, 0:S]
         low_rows = [held([P, S], F32, "low%d" % s) for s in range(2)]
         step = held([P, S], F32, "step")
         limb_rows = [held([P, S], F32, "limbs%d" % s) for s in range(2)]
         h_rows = [held([P, S], F32, "h_rows%d" % s) for s in range(2)]
         weighted_rows = [held([P, S], F32, "weighted%d" % s) for s in range(2)]
         turned = held([P, TILES * PASS], BF16, "turned")
-        fetched = {}
 
         def low(i):
-            return double[:, S : 2 * S] if i == 3 else low_rows[i % 2][:]
+            return double[:, QUARTER : S + QUARTER] if i == 3 else low_rows[i % 2][:]
 
         def h(i):
             return h_rows[i % 2][:, 0:S]
 
         def weighted(i):
-            return double[:, 0:S] if i == 2 else weighted_rows[i % 2][:, 0:S]
+            return weighted_rows[i % 2][:]
 
         def bearers(i):
-            return fetched[i][:, S : 2 * S] if i < 2 else h(i + 1)
+            return first_fetched[:, S : 2 * S] if i == 0 else h(i + 1)
 
         def limbs(i):
-            return fetched[i][:, 0:S] if i < 2 else limb_rows[i % 2][:]
+            return first_fetched[:, 0:S] if i == 0 else second_limbs[:] if i == 1 else limb_rows[i % 2][:]
 
         def multiply(into, lhs, rhs, start, stop):
             nc.tensor.matmul_mx(into, lhsT=lhs[0], lhsT_scale=lhs[1], rhs=rhs[0], rhs_scale=rhs[1], start=start, stop=stop)
@@ -409,14 +408,14 @@ def tile_list_limb_cut_advice_kernel(
             add_transposed(bank, first_step[x], False)
             nc.scalar.copy(first_h[x], bank)
             nc.gpsimd.tensor_tensor(weighted(0)[:, quarters[x]], first_h[x], wgs_natural[:, quarters[x]], ALU.mult)
-            scatter(0, quarters[x].start, QUARTER)
+        scatter(0, BANK, BANK)
         for a in range(2):
             gate_and_span(1, a)
         grouped23 = limb_rows[0][:, halves[0]]
         for i in (2, 3):
             round_on_scalar(grouped23[:, quarters[i - 2]].bitcast(BF16), wl_raw[i])
         quantise(wl_first[:, 2 * P : PASS], wl_s[:, 2 * P : PASS], grouped23.bitcast(BF16))
-        fetched[0] = held([P, 2 * S], F32, "wl_raw23")
+        first_fetched = held([P, 2 * S], F32, "wl_raw23")
         fetch_limbs(0)
         fetch_bearers(0)
 
@@ -429,18 +428,18 @@ def tile_list_limb_cut_advice_kernel(
         for a in range(2):
             make_step(2, a)
         grouped_dealt = sig[2].bitcast(BF16)
-        round_wl_dealt(grouped_dealt)
+        round_wl_dealt(grouped_dealt, (0, 1))
         for a in range(2):
             close_sum(2, a)
+        round_wl_dealt(grouped_dealt, (2, 3))
+        weigh(2)
         scatter(1, 0, S)
         wl_w_dealt = held([P, PASS], U32, "wl_w_dealt")
         for t in range(PACK):
             wl_w[PACK + t] = wl_w_dealt[:, blocks[t]]
         quantise(wl_w_dealt[:], wl_s[:, PASS:H], grouped_dealt)
-        fetched[1] = held([P, 2 * S], F32, "wl_raw_dealt")
+        second_limbs = held([P, S], F32, "wl_raw_dealt")
         fetch_limbs(1)
-        fetch_bearers(1)
-        weigh(2)
         products(3)
         turn_z(0)
         interpolate(3)
@@ -455,8 +454,7 @@ def tile_list_limb_cut_advice_kernel(
         differences = {PACK: wgs_rows[PACK + 2], PACK + 1: wide_tile[:, base : base + S]}
         for i in range(2, LAST):
             scatter(i, 0, S)
-            if i > 2:
-                fetch_bearers(i - 1)
+            fetch_bearers(i - 1)
             if i == LAST - 1:
                 z_w[0] = held([P, M_OUT], U32, "weighted0")[:]
                 quantise(*z_operand(0, 0, M_OUT), z0_grouped.bitcast(BF16))

@@ -55,10 +55,11 @@ def tile_list_limb_cut_advice_kernel(
         def offsets(name, start, count):
             return lists[name][:, start // 16 : (start + count) // 16]
 
-        def load_scale_rows(plane, rows, queue, q):
+        def load_scale_rows(plane, rows, queue, q, copies=QUAD // 4):
+            source = rows[0, 4 * q : 4 * q + 4, :].bitcast(I32)
             queue.dma_start(
-                out=plane[QUAD * q : QUAD * (q + 1), :].bitcast(I32),
-                in_=rows[0, 4 * q : 4 * q + 4, :].bitcast(I32).partition_broadcast(QUAD // 4),
+                out=plane[QUAD * q : QUAD * q + 4 * copies, :].bitcast(I32),
+                in_=source.partition_broadcast(copies) if copies > 1 else source,
             )
 
         def load_rows_of_four(name, src, queue=nc.sync):
@@ -92,6 +93,8 @@ def tile_list_limb_cut_advice_kernel(
         tab_s = held([P, T], U8, "tab_s")
         wg_s = held([P, H], U8, "wg_s")
         wh_s = held([P, H], U8, "wh_s")
+        for zeroed in (wg_s[:], wh_s[0:QUAD, :]):
+            nc.vector.memset(zeroed.bitcast(I32), 0)
         nc.sync.dma_start(lists["offs"][:], offs)
         for q in range(QUADS):
             load_scale_rows(tab_s, tab_scales, (nc.scalar, nc.sync)[q % 2], q)
@@ -102,9 +105,9 @@ def tile_list_limb_cut_advice_kernel(
         tab_w = held([P, T], U32, "tab_w")
         nc.sync.dma_start(out=tab_w[:].bitcast(I32), in_=tab_words[0].rearrange("p t i -> p (t i)").bitcast(I32))
         for q in range(QUADS):
-            load_scale_rows(wg_s, wg_scales, nc.sync, q)
+            load_scale_rows(wg_s, wg_scales, nc.sync, q, 1)
         wh_first = load_plain("wh_first", wh_i32[:, 0:P], I32)
-        load_scale_rows(wh_s, wh_scales, nc.sync, 0)
+        load_scale_rows(wh_s, wh_scales, nc.sync, 0, 1)
         pages[0] = held([P, T2], F32, "page0")
         nc.sync.dma_start(out=pages[0][:, 0 : T2 // 2], in_=page0[0:P, 0 : T2 // 2])
         wl_raw[1] = load_rows_of_four("wl_raw1", wl[:, P : 2 * P])

from contextlib import ExitStack

import concourse.mybir as mybir
from concourse.masks import make_identity

K, T, S, H, T2, M_OUT, N = 512, 2048, 1024, 1024, 2048, 1024, 512
FLOPS = 2 * (3 * K * H * S + H * N * M_OUT)

F32 = mybir.dt.float32
BF16 = mybir.dt.bfloat16
I32 = mybir.dt.int32
U32 = mybir.dt.uint32
U16 = mybir.dt.uint16
U8 = mybir.dt.uint8
FP8X4 = mybir.dt.float8_e4m3fn_x4
FP4X4 = mybir.dt.float4_e2m1fn_x4
ACT = mybir.ActivationFunctionType
ALU = mybir.AluOpType

P = 128
PACK = 4
PASS = P * PACK
BANK = 512
QUAD = 32
QUADS = P // QUAD
RUN = 4
TILES = H // P
LAST = TILES - 1
QUARTER = S // 4
PIECES = ((0, 256), (256, 256), (512, 256), (768, 128), (896, 128))
FOLDED = 3


def tile_list_limb_cut_advice_kernel(
    tc, tab_words, tab_scales, offs, offs2, offs3, offs4, wg_words, wg_scales,
    wl, wh_words, wh_scales, wgs, page0, wd, out,
):
    nc = tc.nc
    with ExitStack() as ctx:
        keep = ctx.enter_context(tc.tile_pool(name="keep", bufs=1))
        psum = ctx.enter_context(tc.psum_pool(name="psum", bufs=1))

        def held(shape, dtype, name):
            return keep.tile(shape, dtype, name=name, align_bytes=64)

        banks = [psum.tile([P, BANK], F32, name="bank%d" % i) for i in range(8)]
        gate_bank, low_bank = (banks[0], banks[2]), (banks[1], banks[3])
        sum_bank, high_bank = (banks[4], banks[6]), (banks[5], banks[7])
        halves = [slice(0, BANK), slice(BANK, 2 * BANK)]
        blocks = [slice(x, x + P) for x in range(0, BANK, P)]
        quarters = [slice(x, x + QUARTER) for x in range(0, S, QUARTER)]

        lists = {name: held([P, S // 16], U16, name) for name in ("offs", "offs2", "offs3", "offs4")}

        def offsets(name, start, count):
            return lists[name][:, start // 16 : (start + count) // 16]

        def load_scale_rows(plane, rows, queue, q, copies=QUAD // 4):
            source = rows[0, 4 * q : 4 * q + 4, :].bitcast(I32)
            queue.dma_start(
                out=plane[QUAD * q : QUAD * q + 4 * copies, :].bitcast(I32),
                in_=source.partition_broadcast(copies) if copies > 1 else source,
            )

        def load_rows_of_four(name, src, queue=nc.sync):
            raw = held([P, PACK, src.shape[1]], F32, name)
            queue.dma_start(out=raw[:], in_=src.rearrange("(p j) c -> p j c", j=PACK))
            return raw

        wh_i32 = wh_words[0].rearrange("p c i -> p (c i)").bitcast(I32)
        wg_i32 = wg_words[0].bitcast(I32)

        def load_plain(name, src, dtype, queue=nc.sync):
            into = held([P, src.shape[1]], dtype, name)
            queue.dma_start(out=into[:], in_=src)
            return into

        def dealt_rows(src, t):
            return src.rearrange("(q t s) c -> t q s c", t=PACK, s=RUN)[t]

        pages = {}

        def load_page(i, queue=nc.sync):
            pages[i] = held([P, T2], F32, "page%d" % i)
            rows = page0[P * i : P * (i + 1), :] if i < PACK else dealt_rows(page0[PASS:H, :], i - PACK)
            queue.dma_start(out=pages[i][:], in_=rows)

        def load_wgs_dealt(rows, t):
            for q in range(QUADS):
                nc.sync.dma_start(out=rows[QUAD * q : QUAD * (q + 1), :], in_=dealt_rows(wgs, t))
            return rows

        tab_s = held([P, T], U8, "tab_s")
        wg_s = held([P, H], U8, "wg_s")
        wh_s = held([P, H], U8, "wh_s")
        for zeroed in (wg_s[:], wh_s[0:QUAD, :]):
            nc.vector.memset(zeroed.bitcast(I32), 0)
        nc.sync.dma_start(lists["offs"][:], offs)
        for q in range(QUADS):
            load_scale_rows(tab_s, tab_scales, (nc.scalar, nc.sync)[q % 2], q)
        for q in (1, 2, 3):
            load_scale_rows(wh_s, wh_scales, nc.gpsimd, q)
        wl_raw = {0: load_rows_of_four("wl_raw0", wl[:, 0:P], nc.scalar)}
        wg_first = load_plain("wg_first", wg_i32[:, 0 : P // 2], I32)
        tab_w = held([P, T], U32, "tab_w")
        nc.sync.dma_start(out=tab_w[:].bitcast(I32), in_=tab_words[0].rearrange("p t i -> p (t i)").bitcast(I32))
        for q in range(QUADS):
            load_scale_rows(wg_s, wg_scales, nc.sync, q, 1)
        wh_first = load_plain("wh_first", wh_i32[:, 0:P], I32)
        load_scale_rows(wh_s, wh_scales, nc.sync, 0, 1)
        pages[0] = held([P, T2], F32, "page0")
        nc.sync.dma_start(out=pages[0][:, 0 : T2 // 2], in_=page0[0:P, 0 : T2 // 2])
        wl_raw[1] = load_rows_of_four("wl_raw1", wl[:, P : 2 * P])
        nc.sync.dma_start(lists["offs2"][:], offs2)
        wgs_natural = held([P, S], F32, "wgs_natural")
        nc.sync.dma_start(out=wgs_natural[:, halves[0]], in_=wgs[:, halves[0]])
        nc.sync.dma_start(out=pages[0][:, T2 // 2 : T2], in_=page0[0:P, T2 // 2 : T2])
        nc.sync.dma_start(out=wgs_natural[:, halves[1]], in_=wgs[:, halves[1]])
        wh_rest = load_plain("wh_rest", wh_i32[:, P:PASS], I32)
        wg_rest = load_plain("wg_rest", wg_i32[:, P // 2 : PASS // 2], I32)
        wl_raw23 = held([P, 2, PACK, P], F32, "wl_raw23")
        for i in (2, 3):
            wl_raw[i] = wl_raw23[:, i - 2]
            nc.sync.dma_start(out=wl_raw[i], in_=wl[:, i * P : (i + 1) * P].rearrange("(p j) c -> p j c", j=PACK))
        nc.sync.dma_start(lists["offs3"][:], offs3)
        nc.sync.dma_start(lists["offs4"][:], offs4)
        load_page(1)
        wl_raw_dealt = load_rows_of_four("wl_raw_dealt", wl[:, PASS:H])
        wh_c = load_plain("wh_c", wh_i32[:, PASS:H], I32)
        wg_c = load_plain("wg_c", wg_i32[:, PASS // 2 : H // 2], I32)
        load_page(2)
        load_page(3)
        wide_tile = held([P, 3 * S], F32, "wide_tile")
        wgs_rows = {i: wgs_natural[:] for i in range(PACK)}
        wd_raw = {}

        def load_rest():
            wd_raw[1] = held([P, PACK, N], F32, "wd_raw1")
            for t in range(PACK):
                nc.sync.dma_start(out=wd_raw[1][:, t, :], in_=dealt_rows(wd[PASS:H, :], t))
            wd_raw[0] = load_rows_of_four("tab_w", wd[0:PASS, :])
            for i in range(PACK, TILES):
                load_page(i)
                rows = held([P, S], F32, "wgs_dealt%d" % i)[:] if i < LAST else wide_tile[:, 2 * S : 3 * S]
                wgs_rows[i] = load_wgs_dealt(rows, i - PACK)

        v_s = held([P, S], U8, "v_s")
        wl_s = held([P, H], U8, "wl_s")
        wd_s = held([P, 2 * N], U8, "wd_s")
        z_s = held([P, 2 * M_OUT], U8, "z_s")
        z_w = {1: held([P, M_OUT], U32, "z_w1")[:]}
        wl_w = {}

        def by_four(grouped):
            return grouped.rearrange("p (c i j) -> p c j i", i=PACK, j=PACK)

        def rows_by_four(raw):
            return raw.rearrange("p j (c i) -> p c j i", i=PACK)

        def quantise(words, scales, grouped):
            nc.vector.quantize_mx(out=words.bitcast(FP8X4), scales=scales, in_=grouped)

        def z_operand(b, m0, width):
            return z_w[b][:, m0 : m0 + width], z_s[:, b * M_OUT + m0 : b * M_OUT + m0 + width]

        def negated(into, source):
            nc.scalar.activation(into, source, ACT.Copy, scale=-1.0)

        def sigmoid(into, source):
            nc.scalar.activation(into, source, ACT.Sigmoid)

        def round_on_scalar(grouped, raw):
            negated(by_four(grouped), rows_by_four(raw))

        def round_wl_dealt(grouped, tiles):
            for t in tiles:
                raw = wl_raw_dealt[:].rearrange("p j (q t s) -> p t q j s", t=PACK, s=RUN)[:, t]
                negated(by_four(grouped[:, t * PASS : (t + 1) * PASS]), raw)

        def deal_columns(copy, into, source):
            run = source.shape[1] * RUN // PASS
            copy(into.rearrange("p (t q s) -> p t q s", t=PACK, s=run), source.rearrange("p (q t s) -> p t q s", t=PACK, s=run))

        grouped0 = held([P, PASS], BF16, "grouped0")

        def round_first(engine, cols):
            engine.tensor_scalar(
                grouped0[:].rearrange("p (c j) -> p c j", j=PACK)[:, cols], wl_raw[0][:].rearrange("p j c -> p c j")[:, cols],
                -1.0, 0.0, ALU.mult, ALU.add,
            )

        round_first(nc.gpsimd, slice(0, P // 2))
        ident = held([P, P], F32, "ident")
        make_identity(nc, ident[:])

        nc.vector.tensor_copy(v_s[:], tab_s[:].indirect(lists["offs"][:]))
        round_first(nc.vector, slice(P // 2, P))
        v_cut = (0, QUARTER, BANK, S)

        def gather_words(a):
            nc.vector.tensor_copy(v_w[:, v_cut[a] : v_cut[a + 1]], tab_w[:].indirect(offsets("offs", v_cut[a], v_cut[a + 1] - v_cut[a])))

        def v_operand(c0, width):
            return v_w[:, c0 : c0 + width].bitcast(FP8X4), v_s[:, c0 : c0 + width]

        wl_first = held([P, PASS], U32, "wl_first")
        for i in range(PACK):
            wl_w[i] = wl_first[:, blocks[i]]
        quantise(wl_w[0], wl_s[:, 0:P], grouped0[:])
        v_w = held([P, S], U32, "grouped0")
        for a in range(3):
            gather_words(a)
        dealt_scales = held([P, H], U8, "wl_raw0")
        wh_sd, wg_sd = dealt_scales[:, 0:PASS], dealt_scales[:, PASS:H]
        dealt = {}
        load_rest()
        deal_columns(nc.gpsimd.tensor_copy, wh_sd[:].bitcast(I32), wh_s[:, PASS:H].bitcast(I32))
        deal_columns(nc.gpsimd.tensor_copy, wg_sd[:].bitcast(I32), wg_s[:, PASS:H].bitcast(I32))

        def weights(i, name):
            cols = slice(P * i, P * (i + 1))
            if i < PACK:
                wh_t, wg_t, x = (wh_first, wg_first, 0) if i == 0 else (wh_rest, wg_rest, i - 1)
                high_scales, gate_scales = wh_s[:, cols], wg_s[:, cols]
            else:
                wh_t, wg_t, x = dealt["high"], dealt["gate"], i - PACK
                high_scales, gate_scales = wh_sd[:, P * x : P * (x + 1)], wg_sd[:, P * x : P * (x + 1)]
            if name == "gate":
                return wg_t[:, x * P // 2 : (x + 1) * P // 2].bitcast(U8).bitcast(FP4X4), gate_scales
            if name == "low":
                return wl_w[i].bitcast(FP8X4), wl_s[:, cols]
            return wh_t[:, x * P : (x + 1) * P].bitcast(FP8X4), high_scales

        pair_a, pair_b, pair_c, pair_d = (held([P, S], F32, "pair_" + x) for x in "abcd")
        side = {i: (i + (i >= FOLDED)) % 2 for i in range(TILES)}
        sig = {i: (pair_a, pair_b)[side[i]][:] for i in range(TILES)}
        span = {i: (pair_c, pair_d)[side[i]][:] for i in range(TILES)}
        double = held([P, S + QUARTER], F32, "double")
        sig[2] = double[:, 0:S]
        low_rows = [held([P, S], F32, "low%d" % s) for s in range(2)]
        step = held([P, S], F32, "step")
        limb_rows = [held([P, S], F32, "limbs%d" % s) for s in range(2)]
        h_rows = [held([P, S], F32, "h_rows%d" % s) for s in range(2)]
        weighted_rows = [held([P, S], F32, "weighted%d" % s) for s in range(2)]
        turned = held([P, TILES * PASS], BF16, "turned")

        def low(i):
            return double[:, QUARTER : S + QUARTER] if i == 3 else low_rows[i % 2][:]

        def h(i):
            return h_rows[i % 2][:, 0:S]

        def weighted(i):
            return weighted_rows[i % 2][:]

        def bearers(i):
            return first_fetched[:, S : 2 * S] if i == 0 else h(i + 1)

        def limbs(i):
            return first_fetched[:, 0:S] if i == 0 else second_limbs[:] if i == 1 else limb_rows[i % 2][:]

        def multiply(into, lhs, rhs, start, stop):
            nc.tensor.matmul_mx(into, lhsT=lhs[0], lhsT_scale=lhs[1], rhs=rhs[0], rhs_scale=rhs[1], start=start, stop=stop)

        def rows_on_partitions(into, name, x, start, stop):
            multiply(into, weights(0, name), v_operand(quarters[x].start, QUARTER), start, stop)

        def columns_on_partitions(into, i, names, c0):
            for x in range(0, into.shape[1], P):
                for name in names:
                    multiply(into[:, x : x + P], v_operand(c0 + x, P), weights(i, name), name == names[0], name == names[-1])

        def add_transposed(bank, source, opens):
            width = source.shape[1]
            for x in range(0, width, P):
                nc.tensor.matmul(
                    bank[:, x : x + P], source[:, x : x + P], ident[:], is_transpose=True,
                    start=(opens and x == 0), stop=(not opens and x + P == width),
                )

        left, right = slice(0, QUARTER), slice(QUARTER, BANK)

        def product(i, names, a, bank, empty, into):
            columns_on_partitions(bank[:], i, names, a * BANK)
            empty(into[:, halves[a]], bank[:])

        def gate_and_span(i, a):
            product(i, ("gate",), a, gate_bank[1 - a if i == 1 else a], sigmoid, sig[i])
            names = ("low", "high") if i < FOLDED else ("high",)
            product(i, names, a, (low_bank if i == 2 else high_bank)[a], nc.scalar.copy, span[i])

        def low_reading(i, a):
            product(i, ("low",), a, (high_bank if i == 1 else low_bank)[a], negated, low(i))

        def products(i):
            for a in range(2):
                gate_and_span(i, a)
                low_reading(i, a)

        def open_sums(i, sums=sum_bank):
            for a in range(2):
                add_transposed(sums[a], low(i)[:, halves[a]], True)

        def make_step(i, a):
            nc.gpsimd.tensor_tensor(step[:, halves[a]], span[i][:, halves[a]], sig[i][:, halves[a]], ALU.mult)

        def close_sum(i, a, sums=sum_bank):
            add_transposed(sums[a], step[:, halves[a]], False)
            nc.scalar.copy(h(i)[:, halves[a]], sums[a][:])

        def interpolate(i, sums=sum_bank):
            open_sums(i, sums)
            for a in range(2 if i >= FOLDED else 0):
                nc.gpsimd.tensor_tensor(span[i][:, halves[a]], span[i][:, halves[a]], low(i)[:, halves[a]], ALU.subtract)
            for a in range(2):
                make_step(i, a)
                close_sum(i, a, sums)

        def weigh(i, parts=(slice(0, S),)):
            for cols in parts:
                nc.gpsimd.tensor_tensor(weighted(i)[:, cols], h(i)[:, cols], wgs_rows[i][:, cols], ALU.mult)

        def scatter(i, m0, width):
            nc.vector.tensor_copy(pages[i][:].indirect(offsets("offs2", m0, width)), weighted(i)[:, m0 : m0 + width])

        def fetch(i, name, m0, into):
            nc.vector.tensor_copy(into, pages[i][:].indirect(offsets(name, m0, into.shape[1])))

        def fetch_limbs(i):
            fetch(i, "offs3", 0, limbs(i))

        def fetch_bearers(i):
            fetch(i, "offs4", 0, bearers(i))

        def subtract(i, into):
            nc.gpsimd.tensor_tensor(into, limbs(i), bearers(i), ALU.subtract)

        def round_z(source, grouped, slots):
            nc.scalar.activation(by_four(grouped)[:, :, slots, :], rows_by_four(source), ACT.Abs)

        def turn_z(i, sums=sum_bank):
            rows = turned[:].rearrange("p (g r) -> p g r", r=PASS)[:, :, P * i : P * (i + 1)]
            for a in range(2):
                add_transposed(sums[a], limbs(i)[:, halves[a]], True)
                negated(limbs(i)[:, halves[a]], bearers(i)[:, halves[a]])
            for a in range(2):
                add_transposed(sums[a], limbs(i)[:, halves[a]], False)
                nc.scalar.activation(
                    rows[:, PACK * a : PACK * (a + 1), :], sums[a][:].rearrange("p (g r) -> p g r", r=P), ACT.Abs
                )

        def turn_back_z(z0_grouped):
            pairs = turned[:].bitcast(F32).rearrange("p (g q u) -> p g u q", u=2, q=P)
            for x, bank in enumerate(sum_bank + sum_bank):
                for y, blk in enumerate(blocks):
                    nc.tensor.transpose(bank[:, blk], pairs[:, 2 * x + y // 2, y % 2, :], ident[:])
                nc.scalar.copy(
                    z0_grouped[:, x * BANK : (x + 1) * BANK].rearrange("p (g m u) -> p g m u", g=2, u=2),
                    bank[:].rearrange("p (g u m) -> p g m u", g=2, u=2),
                )

        def score_bank(x, part):
            return banks[(2 * x + part) % len(banks)]

        def score_pass(b, x):
            m0, width = PIECES[x]
            words, scales = z_operand(b, m0, width)
            for nb in range(N // P):
                part, side = divmod(nb, 2)
                cols = slice(b * N + nb * P, b * N + (nb + 1) * P)
                nc.tensor.matmul_mx(
                    score_bank(x, part)[:, side * width : (side + 1) * width],
                    lhsT=wd_w[:, cols].bitcast(FP8X4), lhsT_scale=wd_s[:, cols],
                    rhs=words.bitcast(FP8X4), rhs_scale=scales,
                    start=(b == 0 and side == 0), stop=(b == 1 and side == 1),
                )

        for x in (0, 1):
            rows_on_partitions(banks[2 * x][:, left], "gate", x, True, True)
            sigmoid(sig[0][:, quarters[x]], banks[2 * x][:, left])
            rows_on_partitions(banks[2 * x + 1][:, left], "low", x, True, False)
        for x in (0, 1):
            rows_on_partitions(banks[2 * x + 1][:, left], "high", x, False, True)
        for x in (0, 1):
            rows_on_partitions(banks[2 * x][:, right], "low", x, True, True)
        for x in (0, 1):
            nc.vector.tensor_tensor(h(0)[:, quarters[x]], banks[2 * x + 1][:, left], sig[0][:, quarters[x]], ALU.mult)
        grouped1 = sig[0][:, quarters[0]].bitcast(BF16)
        round_on_scalar(grouped1, wl_raw[1][:])
        for x in (0, 1):
            nc.vector.tensor_tensor(h(0)[:, quarters[x]], h(0)[:, quarters[x]], banks[2 * x][:, right], ALU.subtract)
        for x in (2, 3):
            columns_on_partitions(banks[1][:, quarters[x - 2]], 0, ("gate",), quarters[x].start)
        sigmoid(sig[0][:, halves[1]], banks[1][:])
        for x, bank in ((2, banks[3]), (3, banks[0])):
            columns_on_partitions(bank[:, left], 0, ("low", "high"), quarters[x].start)
            columns_on_partitions(bank[:, right], 0, ("low",), quarters[x].start)
            nc.scalar.copy(span[0][:, quarters[x]], bank[:, left])
            negated(low(0)[:, quarters[x]], bank[:, right])
        for x in (0, 1):
            nc.vector.tensor_tensor(weighted(0)[:, quarters[x]], h(0)[:, quarters[x]], wgs_natural[:, quarters[x]], ALU.mult)
        quantise(wl_w[1], wl_s[:, blocks[1]], grouped1)
        scatter(0, 0, BANK)
        first_step = {2: span[1][:, quarters[1]], 3: sig[1][:, quarters[2]]}
        first_h = {2: span[1][:, quarters[2]], 3: limb_rows[0][:, P : 3 * P]}
        for x in (2, 3):
            nc.gpsimd.tensor_tensor(first_step[x], span[0][:, quarters[x]], sig[0][:, quarters[x]], ALU.mult)
        for x in (2, 3):
            bank = sum_bank[x - 2][:, left]
            add_transposed(bank, low(0)[:, quarters[x]], True)
            add_transposed(bank, first_step[x], False)
            nc.scalar.copy(first_h[x], bank)
            nc.gpsimd.tensor_tensor(weighted(0)[:, quarters[x]], first_h[x], wgs_natural[:, quarters[x]], ALU.mult)
        scatter(0, BANK, BANK)
        for a in range(2):
            gate_and_span(1, a)
        grouped23 = limb_rows[0][:, halves[0]]
        for i in (2, 3):
            round_on_scalar(grouped23[:, quarters[i - 2]].bitcast(BF16), wl_raw[i])
        quantise(wl_first[:, 2 * P : PASS], wl_s[:, 2 * P : PASS], grouped23.bitcast(BF16))
        first_fetched = held([P, 2 * S], F32, "wl_raw23")
        fetch_limbs(0)
        fetch_bearers(0)

        for a in range(2):
            low_reading(1, a)
        interpolate(1, low_bank)
        weigh(1, halves)
        products(2)
        open_sums(2)
        for a in range(2):
            make_step(2, a)
        grouped_dealt = sig[2].bitcast(BF16)
        round_wl_dealt(grouped_dealt, (0, 1))
        for a in range(2):
            close_sum(2, a)
        round_wl_dealt(grouped_dealt, (2, 3))
        weigh(2)
        scatter(1, 0, S)
        wl_w_dealt = held([P, PASS], U32, "wl_w_dealt")
        for t in range(PACK):
            wl_w[PACK + t] = wl_w_dealt[:, blocks[t]]
        quantise(wl_w_dealt[:], wl_s[:, PASS:H], grouped_dealt)
        second_limbs = held([P, S], F32, "wl_raw_dealt")
        fetch_limbs(1)
        products(3)
        turn_z(0)
        interpolate(3)
        dealt_words = held([P, PASS + PASS // 2], U32, "wl_raw1")
        dealt["high"], dealt["gate"] = dealt_words[:, 0:PASS], dealt_words[:, PASS : PASS + PASS // 2]
        deal_columns(nc.scalar.copy, dealt["high"], wh_c[:].bitcast(U32))
        deal_columns(nc.scalar.copy, dealt["gate"], wg_c[:].bitcast(U32))
        products(4)

        z0_grouped = wide_tile[:, 0 : 2 * S]
        base = 2 * S - BANK
        differences = {PACK: wgs_rows[PACK + 2], PACK + 1: wide_tile[:, base : base + S]}
        for i in range(2, LAST):
            scatter(i, 0, S)
            fetch_bearers(i - 1)
            if i == LAST - 1:
                z_w[0] = held([P, M_OUT], U32, "weighted0")[:]
                quantise(*z_operand(0, 0, M_OUT), z0_grouped.bitcast(BF16))
            fetch_limbs(i)
            weigh(i + 1, halves if i == 2 else (slice(0, S),))
            if i - 1 < PACK:
                turn_z(i - 1)
            else:
                subtract(i - 1, differences[i - 1])
            if i + 2 <= LAST:
                interpolate(i + 2)
            if i + 3 <= LAST:
                products(i + 3)
            if i == 2:
                wd_grouped = held([P, 2 * N * PACK], BF16, "wgs_natural")
                for c0 in range(0, 2 * N, P):
                    b, cols = c0 // N, blocks[c0 % N // P]
                    nc.scalar.copy(by_four(wd_grouped[:, c0 * PACK : (c0 + P) * PACK]), rows_by_four(wd_raw[b][:, :, cols]))
            if i == PACK:
                turn_back_z(z0_grouped)

        scatter(LAST, 0, S)
        wd_w = held([P, 2 * N], U32, "limbs1")
        quantise(wd_w[:], wd_s[:], wd_grouped[:])
        z1_grouped = held([P, M_OUT * PACK], BF16, "h_rows1")

        def z1_piece(x):
            m0, width = PIECES[x]
            return z1_grouped[:, m0 * PACK : (m0 + width) * PACK]

        for t in range(2):
            round_z(differences[PACK + t].unsqueeze(1), z1_grouped[:], slice(t, t + 1))

        spare = (wd_raw[1][:].rearrange("p j c -> p (j c)"), turned[:].bitcast(F32))
        out_rows = out.rearrange("(a s p) m -> a p s m", s=2, p=P)

        def store(x, part, copy):
            m0, width = PIECES[x]
            staged = held_back.get((x, part), spare[part][:, 2 * m0 : 2 * (m0 + width)])
            copy(staged, score_bank(x, part)[:, 0 : 2 * width])
            queue = nc.scalar if x == len(PIECES) - 1 and part == 1 else nc.sync
            queue.dma_start(out=out_rows[part][:, :, m0 : m0 + width], in_=staged.rearrange("p (s m) -> p s m", s=2))

        def finish(x):
            quantise(*z_operand(1, *PIECES[x]), z1_piece(x))
            score_pass(1, x)

        def spent(start, width):
            return wide_tile[:, base + start : base + start + width]

        borne = [spent(start, QUARTER) for start in (-192, 576, -64, 832)]
        pairs = [
            spent(start, 2 * PIECES[x][1]).rearrange("p (s m) -> p s m", s=2)
            for x, start in enumerate((64, 832, 192, 1088, 192))
        ]
        held_back = {(2, 0): spent(BANK + P // 2, BANK)}

        for x, (m0, width) in enumerate(PIECES):
            if m0 % QUARTER == 0:
                fetch(LAST, "offs4", m0, borne[m0 // QUARTER])
            nc.vector.tensor_tensor(
                pairs[x][:, 0, :], pages[LAST - 1][:].indirect(offsets("offs4", m0, width)),
                limbs(LAST - 1)[:, m0 : m0 + width], ALU.subtract,
            )
            nc.vector.tensor_tensor(
                pairs[x][:, 1, :], pages[LAST][:].indirect(offsets("offs3", m0, width)),
                borne[m0 // QUARTER][:, m0 % QUARTER : m0 % QUARTER + width], ALU.subtract,
            )
            round_z(pairs[x], z1_piece(x), slice(2, PACK))
            if x > 0:
                finish(x - 1)
            if x in (1, 2):
                for part in range(2):
                    store(x - 1, part, nc.scalar.copy)
            score_pass(0, x)
        store(2, 0, nc.vector.tensor_copy)
        store(2, 1, nc.scalar.copy)
        finish(len(PIECES) - 1)
        for x in (3, 4):
            store(x, 0, nc.vector.tensor_copy)
            store(x, 1, nc.scalar.copy)
